import numpy as np
import ml_dtypes


def mxq(x, axis, fmt="e4m3"):
    dtype, down = {"e4m3": (ml_dtypes.float8_e4m3fn, 7), "e5m2": (ml_dtypes.float8_e5m2, 14)}[fmt]
    v = np.moveaxis(np.asarray(x, np.float32).astype(ml_dtypes.bfloat16).astype(np.float64), axis, -1)
    blocks = v.reshape(v.shape[:-1] + (-1, 32))
    amax = np.abs(blocks).max(-1, keepdims=True)
    byte = np.maximum(np.where(amax > 0, np.frexp(amax)[1] - 1 + 127, 0) - down, 1)
    scale = np.exp2(byte - 127.0)
    codes = (blocks / scale).astype(np.float32).astype(dtype).astype(np.float64)
    return np.moveaxis((codes * scale).reshape(v.shape), -1, axis)


WIDE = False


def mx_kscale(k):
    if not WIDE:
        return np.ones(k)
    levels = np.array([10, -10, 5, -5, 0])
    if k % 512:
        return np.exp2(np.random.permutation(np.resize(levels, k // 32))).repeat(32)
    a = np.empty((k // 512, 16))
    for p in range(k // 512):
        a[p, :8] = np.random.permutation(np.resize(levels, 8))
        for g in range(8):
            far = levels[np.abs(levels - a[p, g]) >= 10]
            a[p, g + 8] = far[np.random.randint(len(far))]
    return np.exp2(a.ravel()).repeat(32)


def f64(x):
    return np.asarray(x).astype(np.float64)


def striped(idx):
    return np.tile(idx.reshape(-1, 16).T, (8, 1)).astype(np.uint16)


def unstriped(offs):
    return offs[:16].T.reshape(-1).astype(np.int64)


E2M1 = np.array([0.0, 0.5, 1.0, 1.5, 2.0, 3.0, 4.0, 6.0, -0.0, -0.5, -1.0, -1.5, -2.0, -3.0, -4.0, -6.0])


def pack_weight(w, fmt):
    k, n = w.shape
    w = f64(np.asarray(w, np.float32).astype(ml_dtypes.bfloat16)).reshape(k // 32, 32, n)
    amax = np.abs(w).max(1)
    if fmt == "e4m3":
        byte = np.frexp(amax)[1] - 1 + 127 - 7
    else:
        mant, ex = np.frexp(amax / 6.0)
        byte = np.where(mant > 0.5, ex, ex - 1) + 127
    byte = np.clip(np.where(amax > 0, byte, 1), 1, 254)
    scaled = (w * np.exp2(127.0 - byte)[:, None, :]).reshape(k, n).astype(np.float32)
    by_word = np.ascontiguousarray(scaled.reshape(k // 512, 128, 4, n).transpose(0, 1, 3, 2))
    if fmt == "e4m3":
        words = by_word.astype(ml_dtypes.float8_e4m3fn).view(np.uint8)
    else:
        c = by_word.astype(ml_dtypes.float4_e2m1fn).view(np.uint8) & 0xF
        words = (c[..., 0::2] | (c[..., 1::2] << 4)).reshape(k // 512, 128, 2 * n)
    return np.ascontiguousarray(words), np.ascontiguousarray(byte.astype(np.uint8).reshape(k // 512, 16, n))


def unpack_weight(words, scales, fmt):
    g, _, n = scales.shape
    words = np.ascontiguousarray(words).reshape(g, 128, n, -1)
    if fmt == "e4m3":
        vals = words.view(ml_dtypes.float8_e4m3fn).astype(np.float64)
    else:
        nib = np.empty((g, 128, n, 4), np.uint8)
        nib[..., 0::2] = words & 0xF
        nib[..., 1::2] = words >> 4
        vals = E2M1[nib]
    vals = vals * np.repeat(np.exp2(scales.astype(np.float64) - 127.0), 8, axis=1)[..., None]
    return vals.transpose(0, 1, 3, 2).reshape(g * 512, n)


def gelu(v):
    return 0.5 * v * (1.0 + np.tanh(np.sqrt(2.0 / np.pi) * (v + 0.044715 * v**3)))


K, T, S, P, H, N = 1536, 2048, 1024, 512, 1024, 512

def setup_inputs():
    n = np.random.standard_normal
    s = mx_kscale(K)[:, None]
    u = mx_kscale(H)[:, None]
    tab_words, tab_scales = pack_weight(n((K, T)) * s, "e4m3")
    w1 = n((K, H)) / np.sqrt(K) / s * u.T
    w2_words, w2_scales = pack_weight(n((H, N)) / np.sqrt(H) / (u * u), "e2m1")
    return {
        "tab_words": tab_words, "tab_scales": tab_scales,
        "offs": striped(np.random.permutation(T)[:S]),
        "pos1": striped(np.random.permutation(S)[:P]),
        "pos2": striped(np.random.permutation(S)[:P]),
        "w1": w1.astype(np.float32),
        "w2_words": w2_words, "w2_scales": w2_scales,
    }

def reference(tab_words, tab_scales, offs, pos1, pos2, w1, w2_words, w2_scales):
    v = unpack_weight(tab_words, tab_scales, "e4m3")[:, unstriped(offs)]
    w1q = mxq(f64(w1), 0, "e4m3")
    h = w1q.T @ v
    a = h[:, unstriped(pos1)]
    b = h[:, unstriped(pos2)]
    d = a - b
    z = np.square(d)
    zq = mxq(z, 0, "e4m3")
    w2 = unpack_weight(w2_words, w2_scales, "e2m1")
    y = w2.T @ zq
    return np.log(1.0 + np.abs(y))

@@ -1,0 +1,280 @@
+from contextlib import ExitStack
+
+import concourse.mybir as mybir
+
+K, T, S, E, H, N = 1536, 2048, 1024, 512, 1024, 512
+FLOPS = 2 * K * H * S + 2 * H * N * E
+
+F32 = mybir.dt.float32
+BF16 = mybir.dt.bfloat16
+I32 = mybir.dt.int32
+U32 = mybir.dt.uint32
+U16 = mybir.dt.uint16
+U8 = mybir.dt.uint8
+FP8X4 = mybir.dt.float8_e4m3fn_x4
+FP4X4 = mybir.dt.float4_e2m1fn_x4
+ACT = mybir.ActivationFunctionType
+ALU = mybir.AluOpType
+
+P = 128
+PACK = 4
+K_PASS = P * PACK
+K_PASSES = K // K_PASS
+R_PASSES = H // K_PASS
+BANK = 512
+HALVES = S // BANK
+LANES = 16
+E_TILE = 128
+EDGE_BLOCKS = ((0, 256), (256, 384), (384, 512))
+
+
+def tile_list_cloth_edge_strain_kernel(
+    tc, tab_words, tab_scales, offs, pos1, pos2, w1, w2_words, w2_scales, out
+):
+    nc = tc.nc
+    sub_engine = nc.vector
+    with ExitStack() as ctx:
+        keep = ctx.enter_context(tc.tile_pool(name="keep", bufs=1))
+        ring = ctx.enter_context(tc.tile_pool(name="ring", bufs=3))
+        psum = ctx.enter_context(tc.psum_pool(name="psum", bufs=1))
+
+        def held(shape, dtype, name):
+            return keep.tile(shape, dtype, name=name, align_bytes=64)
+
+        offs_sb = keep.tile([P, S // LANES], U16, name="offs_sb")
+        pos1_sb = keep.tile([P, E // LANES], U16, name="pos1_sb")
+        pos2_sb = keep.tile([P, E // LANES], U16, name="pos2_sb")
+        tab_plane = held([P, T // 4], I32, "tab_plane")
+        w2_plane = held([P, R_PASSES, N // 4], I32, "w2_plane")
+        w2_codes = held([P, R_PASSES, N // 2], I32, "w2_codes")
+        table = [held([P, T], I32, "table%d" % a) for a in range(K_PASSES)]
+        v_codes = [held([P, S], U32, "v_codes%d" % a) for a in range(K_PASSES)]
+        v_plane = held([P, S], U8, "v_plane")
+        raw = {}
+        w1_codes = {}
+        w1_plane = {}
+        for g in range(R_PASSES):
+            for a in range(K_PASSES):
+                raw[g, a] = held([P, PACK, K_PASS], F32, "raw%d_%d" % (g, a))
+                w1_codes[g, a] = held([P, K_PASS], U32, "w1_codes%d_%d" % (g, a))
+                w1_plane[g, a] = held([P, K_PASS], U8, "w1_plane%d_%d" % (g, a))
+        h = {}
+        for g in range(R_PASSES):
+            for t in range(PACK):
+                h[g, t] = held([P, S], F32, "h%d_%d" % (g, t))
+
+        nc.gpsimd.memset(tab_plane[:], 0)
+        warm = held([P, 8], F32, "warm")
+        nc.gpsimd.memset(warm[:], 1.0)
+        nc.scalar.activation(warm[:, 4:5], warm[:, 0:1], ACT.Ln)
+
+        def load_table(a):
+            words = tab_words[a].rearrange("p t i -> p (t i)").bitcast(I32)
+            nc.sync.dma_start(out=table[a][:], in_=words)
+
+        def load_w1(g, a):
+            rows = w1[a * K_PASS : (a + 1) * K_PASS, g * K_PASS : (g + 1) * K_PASS]
+            nc.sync.dma_start(out=raw[g, a][:], in_=rows.rearrange("(p j) c -> p j c", j=PACK))
+
+        nc.sync.dma_start(offs_sb[:], offs)
+        load_table(0)
+        for q in range(4):
+            nc.scalar.dma_start(
+                out=tab_plane[32 * q : 32 * q + 4 * K_PASSES, :],
+                in_=tab_scales[:, 4 * q : 4 * q + 4, :].bitcast(I32),
+            )
+        load_w1(0, 0)
+        for a in range(1, K_PASSES):
+            load_table(a)
+            load_w1(0, a)
+        nc.sync.dma_start(pos1_sb[:], pos1)
+        nc.sync.dma_start(pos2_sb[:], pos2)
+        nc.gpsimd.memset(w2_plane[:], 0)
+        for q in range(4):
+            nc.sync.dma_start(
+                out=w2_plane[32 * q : 32 * q + 4, :, :],
+                in_=w2_scales[:, 4 * q : 4 * q + 4, :].bitcast(I32).rearrange("a r c -> r a c"),
+            )
+        nc.sync.dma_start(out=w2_codes[:], in_=w2_words.bitcast(I32).rearrange("a p c -> p a c"))
+        for a in range(K_PASSES):
+            load_w1(1, a)
+        rounded = [held([P, PACK * K_PASS], BF16, "rounded%d" % a) for a in range(K_PASSES)]
+
+        def gather_words(a):
+            nc.vector.tensor_copy(v_codes[a][:], table[a][:].bitcast(U32).indirect(offs_sb[:]))
+
+        def gather_scales():
+            nc.vector.tensor_copy(v_plane[:], tab_plane[:].bitcast(U8).indirect(offs_sb[:]))
+
+        def round_w1(g, a, copy, t0, t1):
+            dst = rounded[(a + 2 * g) % K_PASSES][:].rearrange("p (t m j) -> p m t j", t=PACK, j=PACK)[:, :, t0:t1, :]
+            src = raw[g, a][:].rearrange("p j (m t) -> p m t j", t=PACK)[:, :, t0:t1, :]
+            copy(dst, src)
+
+        def gp_copy(dst, src):
+            nc.gpsimd.tensor_scalar(dst, src, 1.0, 0.0, ALU.mult, ALU.add)
+
+        def quantize_w1(g, a, t0, t1):
+            cols = slice(t0 * P, t1 * P)
+            nc.vector.quantize_mx(
+                out=w1_codes[g, a][:, cols].bitcast(FP8X4),
+                scales=w1_plane[g, a][:, cols],
+                in_=rounded[(a + 2 * g) % K_PASSES][:, t0 * K_PASS : t1 * K_PASS],
+            )
+
+        banks = {}
+        for t in range(PACK):
+            for half in range(HALVES):
+                banks[t, half] = psum.tile([P, BANK], F32, name="bank%d_%d" % (t, half))
+
+        def project(g, a, t):
+            for half in range(HALVES):
+                cols = slice(half * BANK, (half + 1) * BANK)
+                nc.tensor.matmul_mx(
+                    out=banks[t, half][:],
+                    lhsT=w1_codes[g, a][:, t * P : (t + 1) * P].bitcast(FP8X4),
+                    lhsT_scale=w1_plane[g, a][:, t * P : (t + 1) * P],
+                    rhs=v_codes[a][:, cols].bitcast(FP8X4),
+                    rhs_scale=v_plane[4 * a : P, cols],
+                    start=(a == 0),
+                    stop=(a == K_PASSES - 1),
+                )
+
+        def drain(g, t, second=nc.scalar.copy):
+            nc.scalar.copy(h[g, t][:, 0:BANK], banks[t, 0][:])
+            second(h[g, t][:, BANK:S], banks[t, 1][:])
+
+        def gather_end(dst, g, t, pos_sb, e0, e1):
+            nc.vector.tensor_copy(dst, h[g, t][:].indirect(pos_sb[:, e0 // LANES : e1 // LANES]))
+
+        def subtract(dst, first, second, engine=None):
+            (engine or sub_engine).tensor_tensor(dst, first, second, ALU.subtract)
+
+        def square(z, diff):
+            nc.scalar.activation(
+                z.rearrange("p (c i t) -> p c t i", i=4, t=PACK),
+                diff.rearrange("p t (c i) -> p c t i", i=4),
+                ACT.Square,
+            )
+
+        z_codes = [held([P, E], U32, "z_codes%d" % g) for g in range(R_PASSES)]
+        z_plane = [held([P, E], U8, "z_plane%d" % g) for g in range(R_PASSES)]
+
+        def quantize_z(g, z, e0, e1):
+            nc.vector.quantize_mx(
+                out=z_codes[g][:, e0:e1].bitcast(FP8X4),
+                scales=z_plane[g][:, e0:e1],
+                in_=z,
+            )
+
+        def mix(e0):
+            cols = slice(e0, e0 + E_TILE)
+            y = banks[e0 // E_TILE, 0][:].rearrange("p (b e) -> p b e", e=E_TILE)
+            for b in range(N // P):
+                for g in range(R_PASSES):
+                    nc.tensor.matmul_mx(
+                        out=y[:, b, :],
+                        lhsT=w2_codes[:, g, :].bitcast(U8)[:, 2 * b * P : 2 * (b + 1) * P].bitcast(FP4X4),
+                        lhsT_scale=w2_plane[:, g, :].bitcast(U8)[:, b * P : (b + 1) * P],
+                        rhs=z_codes[g][:, cols].bitcast(FP8X4),
+                        rhs_scale=z_plane[g][:, cols],
+                        start=(g == 0),
+                        stop=(g == R_PASSES - 1),
+                    )
+            return y
+
+        def finish(y, e0):
+            cols = slice(e0, e0 + E_TILE)
+            size = ring.tile([P, N // P, E_TILE], F32, name="size")
+            nc.scalar.activation(size[:], y, ACT.Abs)
+            res = ring.tile([P, N // P, E_TILE], F32, name="res")
+            nc.scalar.activation(res[:], size[:], ACT.Ln, bias=1.0)
+            nc.sync.dma_start(out=out[:, cols].rearrange("(b p) e -> p b e", p=P), in_=res[:])
+
+        gather_words(0)
+        gather_scales()
+        round_w1(0, 0, nc.scalar.copy, 0, PACK)
+        gather_words(1)
+        quantize_w1(0, 0, 0, PACK)
+        for t in range(PACK):
+            project(0, 0, t)
+        round_w1(0, 1, nc.scalar.copy, 0, PACK)
+        gather_words(2)
+        quantize_w1(0, 1, 0, PACK)
+        for t in range(PACK):
+            project(0, 1, t)
+        round_w1(0, 2, nc.vector.tensor_copy, 0, 2)
+        round_w1(0, 2, nc.scalar.copy, 2, PACK)
+        quantize_w1(0, 2, 0, 2)
+        project(0, 2, 0)
+        project(0, 2, 1)
+        quantize_w1(0, 2, 2, PACK)
+        project(0, 2, 2)
+        project(0, 2, 3)
+        drain(0, 0, nc.vector.tensor_copy)
+        drain(0, 1)
+
+        casts = [nc.scalar.copy] * 3
+        diff = raw[0, 2]
+        first = [raw[0, 0][:, 0, :], raw[0, 0][:, 1, :], raw[1, 0][:, 0, :], raw[1, 1][:, 0, :]]
+        second = [raw[0, 1][:, 0, :], raw[0, 1][:, 1, :], raw[0, 1][:, 2, :], raw[1, 2][:, 0, :]]
+        for t in range(PACK):
+            if t > 1:
+                a = t - 2
+                round_w1(1, a, casts[a], 0, PACK)
+                quantize_w1(1, a, 0, PACK)
+                drain(0, t)
+                if a == 1:
+                    project(1, 0, PACK - 1)
+                for u in range(t + 1):
+                    project(1, a, u)
+            gather_end(first[t], 0, t, pos1_sb, 0, E)
+            if t > 0:
+                subtract(diff[:, t - 1, :], first[t - 1], second[t - 1])
+            if t == PACK - 1:
+                for t0 in (0, 2):
+                    round_w1(1, 2, casts[2], t0, t0 + 2)
+                    quantize_w1(1, 2, t0, t0 + 2)
+                    project(1, 2, t0)
+                    project(1, 2, t0 + 1)
+            gather_end(second[t], 0, t, pos2_sb, 0, E)
+        subtract(diff[:, PACK - 1, :], first[PACK - 1], second[PACK - 1])
+        for t in range(PACK):
+            drain(1, t)
+        z_low = rounded[1][:]
+        half = E // 2
+        square(z_low[:, 0 : PACK * half], diff[:, :, 0:half])
+        square(z_low[:, PACK * half : PACK * E], diff[:, :, half:E])
+
+        before = None
+        for e0, e1 in EDGE_BLOCKS:
+            n = e1 - e0
+            first = held([P, PACK, n], F32, "first%d" % e0)
+            second = held([P, PACK, n], F32, "second%d" % e0)
+            diff = held([P, PACK, n], F32, "diff%d" % e0)
+            z = held([P, PACK * n], BF16, "z%d" % e0)
+            late = second[:, 2:PACK, :]
+            if before is not None:
+                late = before[3][:].rearrange("p t e -> p (t e)")[:, 0 : 2 * n].rearrange("p (t e) -> p t e", t=2)
+            for t in range(2):
+                gather_end(first[:, t, :], 1, t, pos1_sb, e0, e1)
+                gather_end(second[:, t, :], 1, t, pos2_sb, e0, e1)
+            gather_end(first[:, 2, :], 1, 2, pos1_sb, e0, e1)
+            subtract(diff[:, 0:2, :], first[:, 0:2, :], second[:, 0:2, :])
+            gather_end(first[:, 3, :], 1, 3, pos1_sb, e0, e1)
+            ready = []
+            if before is not None:
+                if before[1] == 0:
+                    quantize_z(0, z_low, 0, E)
+                quantize_z(1, before[0][:], before[1], before[2])
+                ready = [(mix(e), e) for e in range(before[1], before[2], E_TILE)]
+            gather_end(late[:, 0, :], 1, 2, pos2_sb, e0, e1)
+            gather_end(late[:, 1, :], 1, 3, pos2_sb, e0, e1)
+            subtract(diff[:, 2:PACK, :], first[:, 2:PACK, :], late, nc.vector if e1 == E else None)
+            square(z[:], diff[:])
+            for y, e in ready:
+                finish(y, e)
+            before = (z, e0, e1, diff)
+        quantize_z(1, before[0][:], before[1], before[2])
+        for e in range(before[1], before[2], E_TILE):
+            finish(mix(e), e)

@@ -1,6 +1,7 @@
 from contextlib import ExitStack
 
 import concourse.mybir as mybir
+from concourse.masks import make_identity
 
 K, T, S, E, H, N = 1536, 2048, 1024, 512, 1024, 512
 FLOPS = 2 * K * H * S + 2 * H * N * E
@@ -18,24 +19,28 @@ ALU = mybir.AluOpType
 
 P = 128
 PACK = 4
-K_PASS = P * PACK
-K_PASSES = K // K_PASS
-R_PASSES = H // K_PASS
+PASS = P * PACK
+K_PASSES = K // PASS
+R_PASSES = H // PASS
+QUADS = 4
 BANK = 512
-HALVES = S // BANK
 LANES = 16
-E_TILE = 128
-EDGE_BLOCKS = ((0, 256), (256, 384), (384, 512))
+RUN = 4
+PAIR = 2 * P
+PAIRS = H // PAIR
+TILES = H // P
+BLOCKS = E // P
+OUT_TILES = N // P
+DUOS = PASS // 2
+LATE_TILES = (TILES - 2, TILES - 1)
 
 
 def tile_list_cloth_edge_strain_kernel(
     tc, tab_words, tab_scales, offs, pos1, pos2, w1, w2_words, w2_scales, out
 ):
     nc = tc.nc
-    sub_engine = nc.vector
     with ExitStack() as ctx:
         keep = ctx.enter_context(tc.tile_pool(name="keep", bufs=1))
-        ring = ctx.enter_context(tc.tile_pool(name="ring", bufs=3))
         psum = ctx.enter_context(tc.psum_pool(name="psum", bufs=1))
 
         def held(shape, dtype, name):
@@ -50,231 +55,261 @@ def tile_list_cloth_edge_strain_kernel(
         table = [held([P, T], I32, "table%d" % a) for a in range(K_PASSES)]
         v_codes = [held([P, S], U32, "v_codes%d" % a) for a in range(K_PASSES)]
         v_plane = held([P, S], U8, "v_plane")
-        raw = {}
-        w1_codes = {}
-        w1_plane = {}
-        for g in range(R_PASSES):
+        raw, rounded, w1_codes, w1_plane = {}, {}, {}, {}
+        for j in range(PAIRS):
             for a in range(K_PASSES):
-                raw[g, a] = held([P, PACK, K_PASS], F32, "raw%d_%d" % (g, a))
-                w1_codes[g, a] = held([P, K_PASS], U32, "w1_codes%d_%d" % (g, a))
-                w1_plane[g, a] = held([P, K_PASS], U8, "w1_plane%d_%d" % (g, a))
-        h = {}
-        for g in range(R_PASSES):
-            for t in range(PACK):
-                h[g, t] = held([P, S], F32, "h%d_%d" % (g, t))
+                raw[j, a] = held([P, PACK, PAIR], F32, "raw%d_%d" % (j, a))
+                rounded[j, a] = held([P, PACK * PAIR], BF16, "rounded%d_%d" % (j, a))
+                w1_codes[j, a] = held([P, PAIR], U32, "w1_codes%d_%d" % (j, a))
+                w1_plane[j, a] = held([P, PAIR], U8, "w1_plane%d_%d" % (j, a))
+        h = [held([P, S], F32, "h%d" % c) for c in range(TILES)]
+        first = [held([P, E], F32, "first%d" % c) for c in range(TILES)]
+        second = [held([P, E], F32, "second%d" % c) for c in range(TILES)]
+        z_rows = [held([P, BLOCKS, DUOS], F32, "z_rows%d" % g) for g in range(R_PASSES)]
+        z_cols = [held([P, E, 2], F32, "z_cols%d" % g) for g in range(R_PASSES)]
+        z_codes = [held([P, E], U32, "z_codes%d" % g) for g in range(R_PASSES)]
+        z_plane = [held([P, E], U8, "z_plane%d" % g) for g in range(R_PASSES)]
+        size = [held([P, OUT_TILES, P], F32, "size%d" % b) for b in range(BLOCKS)]
+        result = [held([P, OUT_TILES, P], F32, "result%d" % b) for b in range(BLOCKS)]
+        minus_one = held([P, E], F32, "minus_one")
+        identity = held([P, P], F32, "identity")
+        low = [psum.tile([P, BANK], F32, name="low%d" % i) for i in range(2)]
+        high = [psum.tile([P, BANK], F32, name="high%d" % i) for i in range(4)]
+        back = [psum.tile([P, BANK], F32, name="back%d" % i) for i in range(2)]
 
         nc.gpsimd.memset(tab_plane[:], 0)
-        warm = held([P, 8], F32, "warm")
-        nc.gpsimd.memset(warm[:], 1.0)
-        nc.scalar.activation(warm[:, 4:5], warm[:, 0:1], ACT.Ln)
+        one = held([P, 1], F32, "one")
+        zero = held([P, 1], F32, "zero")
+        nc.vector.memset(one[:], 1.0)
+        nc.scalar.activation(zero[:], one[:], ACT.Ln)
+        nc.vector.memset(w2_plane[:], 0)
+        nc.vector.memset(minus_one[:], -1.0)
+        make_identity(nc, identity[:])
 
         def load_table(a):
             words = tab_words[a].rearrange("p t i -> p (t i)").bitcast(I32)
             nc.sync.dma_start(out=table[a][:], in_=words)
 
-        def load_w1(g, a):
-            rows = w1[a * K_PASS : (a + 1) * K_PASS, g * K_PASS : (g + 1) * K_PASS]
-            nc.sync.dma_start(out=raw[g, a][:], in_=rows.rearrange("(p j) c -> p j c", j=PACK))
+        def load_w1(j, a):
+            rows = w1[a * PASS : (a + 1) * PASS, j * PAIR : (j + 1) * PAIR]
+            nc.sync.dma_start(out=raw[j, a][:], in_=rows.rearrange("(p i) c -> p i c", i=PACK))
 
         nc.sync.dma_start(offs_sb[:], offs)
-        load_table(0)
-        for q in range(4):
-            nc.scalar.dma_start(
-                out=tab_plane[32 * q : 32 * q + 4 * K_PASSES, :],
-                in_=tab_scales[:, 4 * q : 4 * q + 4, :].bitcast(I32),
-            )
-        load_w1(0, 0)
-        for a in range(1, K_PASSES):
+        for a in range(K_PASSES):
             load_table(a)
             load_w1(0, a)
+            if a == 0:
+                for q in range(QUADS):
+                    nc.sync.dma_start(
+                        out=tab_plane[32 * q : 32 * q + 4 * K_PASSES, :],
+                        in_=tab_scales[:, 4 * q : 4 * q + 4, :].bitcast(I32),
+                    )
         nc.sync.dma_start(pos1_sb[:], pos1)
         nc.sync.dma_start(pos2_sb[:], pos2)
-        nc.gpsimd.memset(w2_plane[:], 0)
-        for q in range(4):
+        for j in range(1, PAIRS):
+            for a in range(K_PASSES):
+                load_w1(j, a)
+        nc.sync.dma_start(out=w2_codes[:], in_=w2_words.bitcast(I32).rearrange("a p c -> p a c"))
+        for q in range(QUADS):
             nc.sync.dma_start(
                 out=w2_plane[32 * q : 32 * q + 4, :, :],
                 in_=w2_scales[:, 4 * q : 4 * q + 4, :].bitcast(I32).rearrange("a r c -> r a c"),
             )
-        nc.sync.dma_start(out=w2_codes[:], in_=w2_words.bitcast(I32).rearrange("a p c -> p a c"))
-        for a in range(K_PASSES):
-            load_w1(1, a)
-        rounded = [held([P, PACK * K_PASS], BF16, "rounded%d" % a) for a in range(K_PASSES)]
 
-        def gather_words(a):
-            nc.vector.tensor_copy(v_codes[a][:], table[a][:].bitcast(U32).indirect(offs_sb[:]))
+        def gather_words(a, s0, s1):
+            window = table[a][:].bitcast(U32)
+            nc.vector.tensor_copy(v_codes[a][:, s0:s1], window.indirect(offs_sb[:, s0 // LANES : s1 // LANES]))
 
-        def gather_scales():
-            nc.vector.tensor_copy(v_plane[:], tab_plane[:].bitcast(U8).indirect(offs_sb[:]))
-
-        def round_w1(g, a, copy, t0, t1):
-            dst = rounded[(a + 2 * g) % K_PASSES][:].rearrange("p (t m j) -> p m t j", t=PACK, j=PACK)[:, :, t0:t1, :]
-            src = raw[g, a][:].rearrange("p j (m t) -> p m t j", t=PACK)[:, :, t0:t1, :]
-            copy(dst, src)
-
-        def gp_copy(dst, src):
-            nc.gpsimd.tensor_scalar(dst, src, 1.0, 0.0, ALU.mult, ALU.add)
-
-        def quantize_w1(g, a, t0, t1):
-            cols = slice(t0 * P, t1 * P)
-            nc.vector.quantize_mx(
-                out=w1_codes[g, a][:, cols].bitcast(FP8X4),
-                scales=w1_plane[g, a][:, cols],
-                in_=rounded[(a + 2 * g) % K_PASSES][:, t0 * K_PASS : t1 * K_PASS],
+        def round_w1(j, a, copy):
+            copy(
+                rounded[j, a][:].rearrange("p (c n i) -> p c i n", n=RUN, i=PACK),
+                raw[j, a][:].rearrange("p i (c n) -> p c i n", n=RUN),
             )
 
-        banks = {}
-        for t in range(PACK):
-            for half in range(HALVES):
-                banks[t, half] = psum.tile([P, BANK], F32, name="bank%d_%d" % (t, half))
+        def quantize_w1(j, a):
+            nc.vector.quantize_mx(
+                out=w1_codes[j, a][:].bitcast(FP8X4), scales=w1_plane[j, a][:], in_=rounded[j, a][:]
+            )
 
-        def project(g, a, t):
-            for half in range(HALVES):
-                cols = slice(half * BANK, (half + 1) * BANK)
-                nc.tensor.matmul_mx(
-                    out=banks[t, half][:],
-                    lhsT=w1_codes[g, a][:, t * P : (t + 1) * P].bitcast(FP8X4),
-                    lhsT_scale=w1_plane[g, a][:, t * P : (t + 1) * P],
-                    rhs=v_codes[a][:, cols].bitcast(FP8X4),
-                    rhs_scale=v_plane[4 * a : P, cols],
-                    start=(a == 0),
-                    stop=(a == K_PASSES - 1),
-                )
+        def prepare_pair(j):
+            for a in range(K_PASSES):
+                round_w1(j, a, nc.vector.tensor_copy if a == K_PASSES - 1 else nc.scalar.copy)
+            for a in range(K_PASSES):
+                quantize_w1(j, a)
 
-        def drain(g, t, second=nc.scalar.copy):
-            nc.scalar.copy(h[g, t][:, 0:BANK], banks[t, 0][:])
-            second(h[g, t][:, BANK:S], banks[t, 1][:])
+        def h_bank(c, half):
+            return high[c % len(high)] if half else low[c % len(low)]
 
-        def gather_end(dst, g, t, pos_sb, e0, e1):
-            nc.vector.tensor_copy(dst, h[g, t][:].indirect(pos_sb[:, e0 // LANES : e1 // LANES]))
+        def project(c, half, a):
+            rows = slice(c % 2 * P, (c % 2 + 1) * P)
+            cols = slice(half * BANK, (half + 1) * BANK)
+            nc.tensor.matmul_mx(
+                out=h_bank(c, half)[:],
+                lhsT=w1_codes[c // 2, a][:, rows].bitcast(FP8X4),
+                lhsT_scale=w1_plane[c // 2, a][:, rows],
+                rhs=v_codes[a][:, cols].bitcast(FP8X4),
+                rhs_scale=v_plane[4 * a : P, cols],
+                start=(a == 0),
+                stop=(a == K_PASSES - 1),
+            )
 
-        def subtract(dst, first, second, engine=None):
-            (engine or sub_engine).tensor_tensor(dst, first, second, ALU.subtract)
+        def project_tile(c):
+            for half in range(2):
+                for a in range(K_PASSES):
+                    project(c, half, a)
 
-        def square(z, diff):
+        def drain(c, copy_high=nc.scalar.copy):
+            nc.scalar.copy(h[c][:, 0:BANK], h_bank(c, 0)[:])
+            copy_high(h[c][:, BANK:S], h_bank(c, 1)[:])
+
+        def gather_ends(c, b0, b1):
+            edges = slice(b0 * P, b1 * P)
+            entries = slice(b0 * P // LANES, b1 * P // LANES)
+            nc.vector.tensor_copy(first[c][:, edges], h[c][:].indirect(pos1_sb[:, entries]))
+            nc.vector.tensor_tensor(
+                second[c][:, edges], h[c][:].indirect(pos2_sb[:, entries]), minus_one[:, 0 : (b1 - b0) * P], ALU.mult
+            )
+
+        def difference(dst, c, b):
+            edges = slice(b * P, (b + 1) * P)
+            nc.tensor.matmul(dst, lhsT=first[c][:, edges], rhs=identity[:], start=True, stop=False, is_transpose=True)
+            nc.tensor.matmul(dst, lhsT=second[c][:, edges], rhs=identity[:], start=False, stop=True, is_transpose=True)
+
+        def square(bank, b0, b1, c0, c1):
+            width = (c1 - c0) * P
+            flat = z_rows[c0 // PACK][:].rearrange("p b w -> p (b w)").bitcast(BF16)
+            r0 = c0 % PACK * P
             nc.scalar.activation(
-                z.rearrange("p (c i t) -> p c t i", i=4, t=PACK),
-                diff.rearrange("p t (c i) -> p c t i", i=4),
+                flat.rearrange("p (b r) -> p b r", b=BLOCKS)[:, b0:b1, r0 : r0 + width],
+                bank[:, 0 : (b1 - b0) * width].rearrange("p (b r) -> p b r", r=width),
                 ACT.Square,
             )
 
-        z_codes = [held([P, E], U32, "z_codes%d" % g) for g in range(R_PASSES)]
-        z_plane = [held([P, E], U8, "z_plane%d" % g) for g in range(R_PASSES)]
+        def square_tile(c, bank):
+            for b in range(BLOCKS):
+                difference(bank[:, b * P : (b + 1) * P], c, b)
+            square(bank, 0, BLOCKS, c, c + 1)
 
-        def quantize_z(g, z, e0, e1):
-            nc.vector.quantize_mx(
-                out=z_codes[g][:, e0:e1].bitcast(FP8X4),
-                scales=z_plane[g][:, e0:e1],
-                in_=z,
+        def square_late_tiles(b0, b1, bank):
+            for c in LATE_TILES:
+                gather_ends(c, b0, b1)
+            for b in range(b0, b1):
+                for c in LATE_TILES:
+                    at = (b - b0) * PAIR + c % 2 * P
+                    difference(bank[:, at : at + P], c, b)
+            square(bank, b0, b1, LATE_TILES[0], TILES)
+
+        def turn_back(g, b0, b1, bank, copy):
+            for b in range(b0, b1):
+                for u in range(2):
+                    at = (2 * (b - b0) + u) * P
+                    nc.tensor.transpose(bank[:, at : at + P], z_rows[g][:, b, u:DUOS:2], identity[:])
+            copy(
+                z_cols[g][:, b0 * P : b1 * P, :].rearrange("p (b e) u -> p b e u", e=P),
+                bank[:, 0 : 2 * (b1 - b0) * P].rearrange("p (b u e) -> p b e u", u=2, e=P),
             )
 
-        def mix(e0):
-            cols = slice(e0, e0 + E_TILE)
-            y = banks[e0 // E_TILE, 0][:].rearrange("p (b e) -> p b e", e=E_TILE)
-            for b in range(N // P):
+        def quantize_z(g, b0, b1):
+            edges = slice(b0 * P, b1 * P)
+            nc.vector.quantize_mx(
+                out=z_codes[g][:, edges].bitcast(FP8X4),
+                scales=z_plane[g][:, edges],
+                in_=z_cols[g][:, edges, :].rearrange("p e u -> p (e u)").bitcast(BF16),
+            )
+
+        def mix_pass(dst, n, g, b):
+            edges = slice(b * P, (b + 1) * P)
+            nc.tensor.matmul_mx(
+                out=dst,
+                lhsT=w2_codes[:, g, :].bitcast(U8)[:, 2 * n * P : 2 * (n + 1) * P].bitcast(FP4X4),
+                lhsT_scale=w2_plane[:, g, :].bitcast(U8)[:, n * P : (n + 1) * P],
+                rhs=z_codes[g][:, edges].bitcast(FP8X4),
+                rhs_scale=z_plane[g][:, edges],
+                start=(g == 0),
+                stop=(g == R_PASSES - 1),
+            )
+
+        def mix(b, bank):
+            for n in range(OUT_TILES):
                 for g in range(R_PASSES):
-                    nc.tensor.matmul_mx(
-                        out=y[:, b, :],
-                        lhsT=w2_codes[:, g, :].bitcast(U8)[:, 2 * b * P : 2 * (b + 1) * P].bitcast(FP4X4),
-                        lhsT_scale=w2_plane[:, g, :].bitcast(U8)[:, b * P : (b + 1) * P],
-                        rhs=z_codes[g][:, cols].bitcast(FP8X4),
-                        rhs_scale=z_plane[g][:, cols],
-                        start=(g == 0),
-                        stop=(g == R_PASSES - 1),
-                    )
-            return y
+                    mix_pass(bank[:, n * P : (n + 1) * P], n, g, b)
 
-        def finish(y, e0):
-            cols = slice(e0, e0 + E_TILE)
-            size = ring.tile([P, N // P, E_TILE], F32, name="size")
-            nc.scalar.activation(size[:], y, ACT.Abs)
-            res = ring.tile([P, N // P, E_TILE], F32, name="res")
-            nc.scalar.activation(res[:], size[:], ACT.Ln, bias=1.0)
-            nc.sync.dma_start(out=out[:, cols].rearrange("(b p) e -> p b e", p=P), in_=res[:])
+        def log_and_store(b, n0, n1):
+            nc.scalar.activation(result[b][:, n0:n1, :], size[b][:, n0:n1, :], ACT.Ln, bias=1.0)
+            nc.sync.dma_start(
+                out=out[n0 * P : n1 * P, b * P : (b + 1) * P].rearrange("(n p) e -> p n e", p=P),
+                in_=result[b][:, n0:n1, :],
+            )
 
-        gather_words(0)
-        gather_scales()
-        round_w1(0, 0, nc.scalar.copy, 0, PACK)
-        gather_words(1)
-        quantize_w1(0, 0, 0, PACK)
-        for t in range(PACK):
-            project(0, 0, t)
-        round_w1(0, 1, nc.scalar.copy, 0, PACK)
-        gather_words(2)
-        quantize_w1(0, 1, 0, PACK)
-        for t in range(PACK):
-            project(0, 1, t)
-        round_w1(0, 2, nc.vector.tensor_copy, 0, 2)
-        round_w1(0, 2, nc.scalar.copy, 2, PACK)
-        quantize_w1(0, 2, 0, 2)
-        project(0, 2, 0)
-        project(0, 2, 1)
-        quantize_w1(0, 2, 2, PACK)
-        project(0, 2, 2)
-        project(0, 2, 3)
-        drain(0, 0, nc.vector.tensor_copy)
-        drain(0, 1)
+        gather_words(0, 0, S)
+        nc.vector.tensor_copy(v_plane[:], tab_plane[:].bitcast(U8).indirect(offs_sb[:]))
+        last_pass = K_PASSES - 1
+        for a in range(last_pass):
+            round_w1(0, a, nc.scalar.copy)
+            if a > 0:
+                gather_words(a, 0, S)
+            quantize_w1(0, a)
+            for c in range(2):
+                for half in range(2):
+                    project(c, half, a)
+        round_w1(0, last_pass, nc.scalar.copy)
+        gather_words(last_pass, 0, BANK)
+        quantize_w1(0, last_pass)
+        project(0, 0, last_pass)
+        gather_words(last_pass, BANK, S)
+        project(0, 1, last_pass)
+        project(1, 0, last_pass)
+        project(1, 1, last_pass)
 
-        casts = [nc.scalar.copy] * 3
-        diff = raw[0, 2]
-        first = [raw[0, 0][:, 0, :], raw[0, 0][:, 1, :], raw[1, 0][:, 0, :], raw[1, 1][:, 0, :]]
-        second = [raw[0, 1][:, 0, :], raw[0, 1][:, 1, :], raw[0, 1][:, 2, :], raw[1, 2][:, 0, :]]
-        for t in range(PACK):
-            if t > 1:
-                a = t - 2
-                round_w1(1, a, casts[a], 0, PACK)
-                quantize_w1(1, a, 0, PACK)
-                drain(0, t)
-                if a == 1:
-                    project(1, 0, PACK - 1)
-                for u in range(t + 1):
-                    project(1, a, u)
-            gather_end(first[t], 0, t, pos1_sb, 0, E)
-            if t > 0:
-                subtract(diff[:, t - 1, :], first[t - 1], second[t - 1])
-            if t == PACK - 1:
-                for t0 in (0, 2):
-                    round_w1(1, 2, casts[2], t0, t0 + 2)
-                    quantize_w1(1, 2, t0, t0 + 2)
-                    project(1, 2, t0)
-                    project(1, 2, t0 + 1)
-            gather_end(second[t], 0, t, pos2_sb, 0, E)
-        subtract(diff[:, PACK - 1, :], first[PACK - 1], second[PACK - 1])
-        for t in range(PACK):
-            drain(1, t)
-        z_low = rounded[1][:]
-        half = E // 2
-        square(z_low[:, 0 : PACK * half], diff[:, :, 0:half])
-        square(z_low[:, PACK * half : PACK * E], diff[:, :, half:E])
+        drain(0, nc.vector.tensor_copy)
+        gather_ends(0, 0, BLOCKS)
+        prepare_pair(1)
+        project_tile(2)
+        for c in range(1, LATE_TILES[0]):
+            if c % 2 == 0:
+                prepare_pair(c // 2 + 1)
+            drain(c)
+            if c >= 2:
+                square_tile(c - 2, h_bank(c, 1))
+            project_tile(c + 2)
+            gather_ends(c, 0, BLOCKS)
+        drain(LATE_TILES[0])
+        for i in range(len(back)):
+            turn_back(0, 2 * i, 2 * i + 2, back[i], nc.scalar.copy)
+        drain(LATE_TILES[1])
+        square_tile(LATE_TILES[0] - 2, high[0])
+        square_tile(LATE_TILES[1] - 2, high[3])
+        quantize_z(0, 0, BLOCKS)
 
-        before = None
-        for e0, e1 in EDGE_BLOCKS:
-            n = e1 - e0
-            first = held([P, PACK, n], F32, "first%d" % e0)
-            second = held([P, PACK, n], F32, "second%d" % e0)
-            diff = held([P, PACK, n], F32, "diff%d" % e0)
-            z = held([P, PACK * n], BF16, "z%d" % e0)
-            late = second[:, 2:PACK, :]
-            if before is not None:
-                late = before[3][:].rearrange("p t e -> p (t e)")[:, 0 : 2 * n].rearrange("p (t e) -> p t e", t=2)
-            for t in range(2):
-                gather_end(first[:, t, :], 1, t, pos1_sb, e0, e1)
-                gather_end(second[:, t, :], 1, t, pos2_sb, e0, e1)
-            gather_end(first[:, 2, :], 1, 2, pos1_sb, e0, e1)
-            subtract(diff[:, 0:2, :], first[:, 0:2, :], second[:, 0:2, :])
-            gather_end(first[:, 3, :], 1, 3, pos1_sb, e0, e1)
-            ready = []
-            if before is not None:
-                if before[1] == 0:
-                    quantize_z(0, z_low, 0, E)
-                quantize_z(1, before[0][:], before[1], before[2])
-                ready = [(mix(e), e) for e in range(before[1], before[2], E_TILE)]
-            gather_end(late[:, 0, :], 1, 2, pos2_sb, e0, e1)
-            gather_end(late[:, 1, :], 1, 3, pos2_sb, e0, e1)
-            subtract(diff[:, 2:PACK, :], first[:, 2:PACK, :], late, nc.vector if e1 == E else None)
-            square(z[:], diff[:])
-            for y, e in ready:
-                finish(y, e)
-            before = (z, e0, e1, diff)
-        quantize_z(1, before[0][:], before[1], before[2])
-        for e in range(before[1], before[2], E_TILE):
-            finish(mix(e), e)
+        last = BLOCKS - 1
+        y_banks = [high[2], high[3], low[0]]
+        square_late_tiles(0, 2, low[0])
+        square_late_tiles(2, last, low[1])
+        turn_back(1, 0, 2, back[0], nc.scalar.copy)
+        square_late_tiles(last, BLOCKS, back[0])
+        quantize_z(1, 0, 2)
+        mix(0, y_banks[0])
+        turn_back(1, 2, last, back[1], nc.vector.tensor_copy)
+        quantize_z(1, 2, last)
+        turn_back(1, last, BLOCKS, high[1], nc.vector.tensor_copy)
+        mix(1, y_banks[1])
+        mix(2, y_banks[2])
+        last_y = [bank[:, 0:P] for bank in (back[0], back[1], low[1], high[0])]
+        for n in range(OUT_TILES):
+            mix_pass(last_y[n], n, 0, last)
+        quantize_z(1, last, BLOCKS)
+        for n in range(OUT_TILES):
+            mix_pass(last_y[n], n, 1, last)
+
+        for b in range(last):
+            y = y_banks[b][:].rearrange("p (n e) -> p n e", e=P)
+            if b == last - 1:
+                nc.vector.tensor_scalar(result[b][:], y, -1.0, None, ALU.mult)
+                nc.vector.tensor_tensor(size[b][:], y, result[b][:], ALU.max)
+            else:
+                nc.scalar.activation(size[b][:], y, ACT.Abs, bias=zero[:])
+            log_and_store(b, 0, OUT_TILES)
+        for n0 in range(0, OUT_TILES, 2):
+            for n in (n0, n0 + 1):
+                nc.scalar.activation(size[last][:, n, :], last_y[n], ACT.Abs, bias=zero[:])
+            log_and_store(last, n0, n0 + 2)

@@ -27,12 +27,13 @@ BANK = 512
 LANES = 16
 RUN = 4
 PAIR = 2 * P
-PAIRS = H // PAIR
 TILES = H // P
 BLOCKS = E // P
 OUT_TILES = N // P
 DUOS = PASS // 2
-LATE_TILES = (TILES - 2, TILES - 1)
+HALF = E // 2
+SHARE = 64
+LATE = 3
 
 
 def tile_list_cloth_edge_strain_kernel(
@@ -43,8 +44,8 @@ def tile_list_cloth_edge_strain_kernel(
         keep = ctx.enter_context(tc.tile_pool(name="keep", bufs=1))
         psum = ctx.enter_context(tc.psum_pool(name="psum", bufs=1))
 
-        def held(shape, dtype, name):
-            return keep.tile(shape, dtype, name=name, align_bytes=64)
+        def held(shape, dtype, name, tag=None):
+            return keep.tile(shape, dtype, name=name, tag=tag or name, align_bytes=64)
 
         offs_sb = keep.tile([P, S // LANES], U16, name="offs_sb")
         pos1_sb = keep.tile([P, E // LANES], U16, name="pos1_sb")
@@ -55,27 +56,23 @@ def tile_list_cloth_edge_strain_kernel(
         table = [held([P, T], I32, "table%d" % a) for a in range(K_PASSES)]
         v_codes = [held([P, S], U32, "v_codes%d" % a) for a in range(K_PASSES)]
         v_plane = held([P, S], U8, "v_plane")
+        part_cols = [(0, PAIR), (PAIR, PASS), (PASS, H)]
         raw, rounded, w1_codes, w1_plane = {}, {}, {}, {}
-        for j in range(PAIRS):
+        for j, (c0, c1) in enumerate(part_cols):
             for a in range(K_PASSES):
-                raw[j, a] = held([P, PACK, PAIR], F32, "raw%d_%d" % (j, a))
-                rounded[j, a] = held([P, PACK * PAIR], BF16, "rounded%d_%d" % (j, a))
-                w1_codes[j, a] = held([P, PAIR], U32, "w1_codes%d_%d" % (j, a))
-                w1_plane[j, a] = held([P, PAIR], U8, "w1_plane%d_%d" % (j, a))
+                raw[j, a] = held([P, PACK, c1 - c0], F32, "raw%d_%d" % (j, a))
+                rounded[j, a] = held([P, PACK * (c1 - c0)], BF16, "rounded%d_%d" % (j, a))
+                w1_codes[j, a] = held([P, c1 - c0], U32, "w1_codes%d_%d" % (j, a))
+                w1_plane[j, a] = held([P, c1 - c0], U8, "w1_plane%d_%d" % (j, a))
         h = [held([P, S], F32, "h%d" % c) for c in range(TILES)]
-        first = [held([P, E], F32, "first%d" % c) for c in range(TILES)]
-        second = [held([P, E], F32, "second%d" % c) for c in range(TILES)]
-        z_rows = [held([P, BLOCKS, DUOS], F32, "z_rows%d" % g) for g in range(R_PASSES)]
-        z_cols = [held([P, E, 2], F32, "z_cols%d" % g) for g in range(R_PASSES)]
+        d_early = [held([P, E], F32, "d_early%d" % c) for c in range(PACK)]
+        d_late = held([P, PACK, E], F32, "d_late")
         z_codes = [held([P, E], U32, "z_codes%d" % g) for g in range(R_PASSES)]
         z_plane = [held([P, E], U8, "z_plane%d" % g) for g in range(R_PASSES)]
         size = [held([P, OUT_TILES, P], F32, "size%d" % b) for b in range(BLOCKS)]
         result = [held([P, OUT_TILES, P], F32, "result%d" % b) for b in range(BLOCKS)]
-        minus_one = held([P, E], F32, "minus_one")
         identity = held([P, P], F32, "identity")
-        low = [psum.tile([P, BANK], F32, name="low%d" % i) for i in range(2)]
-        high = [psum.tile([P, BANK], F32, name="high%d" % i) for i in range(4)]
-        back = [psum.tile([P, BANK], F32, name="back%d" % i) for i in range(2)]
+        bank = [psum.tile([P, BANK], F32, name="bank%d" % i) for i in range(8)]
 
         nc.gpsimd.memset(tab_plane[:], 0)
         one = held([P, 1], F32, "one")
@@ -83,7 +80,6 @@ def tile_list_cloth_edge_strain_kernel(
         nc.vector.memset(one[:], 1.0)
         nc.scalar.activation(zero[:], one[:], ACT.Ln)
         nc.vector.memset(w2_plane[:], 0)
-        nc.vector.memset(minus_one[:], -1.0)
         make_identity(nc, identity[:])
 
         def load_table(a):
@@ -91,7 +87,8 @@ def tile_list_cloth_edge_strain_kernel(
             nc.sync.dma_start(out=table[a][:], in_=words)
 
         def load_w1(j, a):
-            rows = w1[a * PASS : (a + 1) * PASS, j * PAIR : (j + 1) * PAIR]
+            c0, c1 = part_cols[j]
+            rows = w1[a * PASS : (a + 1) * PASS, c0:c1]
             nc.sync.dma_start(out=raw[j, a][:], in_=rows.rearrange("(p i) c -> p i c", i=PACK))
 
         nc.sync.dma_start(offs_sb[:], offs)
@@ -106,7 +103,7 @@ def tile_list_cloth_edge_strain_kernel(
                     )
         nc.sync.dma_start(pos1_sb[:], pos1)
         nc.sync.dma_start(pos2_sb[:], pos2)
-        for j in range(1, PAIRS):
+        for j in range(1, len(part_cols)):
             for a in range(K_PASSES):
                 load_w1(j, a)
         nc.sync.dma_start(out=w2_codes[:], in_=w2_words.bitcast(I32).rearrange("a p c -> p a c"))
@@ -126,96 +123,102 @@ def tile_list_cloth_edge_strain_kernel(
                 raw[j, a][:].rearrange("p i (c n) -> p c i n", n=RUN),
             )
 
+        def round_dealt(a, m0, m1, copy):
+            copy(
+                rounded[2, a][:].rearrange("p (t m i) -> p m i t", t=PACK, i=PACK)[:, m0:m1],
+                raw[2, a][:].rearrange("p i (m t) -> p m i t", t=PACK)[:, m0:m1],
+            )
+
         def quantize_w1(j, a):
             nc.vector.quantize_mx(
                 out=w1_codes[j, a][:].bitcast(FP8X4), scales=w1_plane[j, a][:], in_=rounded[j, a][:]
             )
 
-        def prepare_pair(j):
-            for a in range(K_PASSES):
-                round_w1(j, a, nc.vector.tensor_copy if a == K_PASSES - 1 else nc.scalar.copy)
-            for a in range(K_PASSES):
-                quantize_w1(j, a)
-
         def h_bank(c, half):
-            return high[c % len(high)] if half else low[c % len(low)]
+            return bank[2 * (c % 3) + half]
 
-        def project(c, half, a):
-            rows = slice(c % 2 * P, (c % 2 + 1) * P)
+        def project(c, half, a, order):
+            j = min(c // 2, 2)
+            t = c - 2 * j
+            rows = slice(t * P, (t + 1) * P)
             cols = slice(half * BANK, (half + 1) * BANK)
             nc.tensor.matmul_mx(
                 out=h_bank(c, half)[:],
-                lhsT=w1_codes[c // 2, a][:, rows].bitcast(FP8X4),
-                lhsT_scale=w1_plane[c // 2, a][:, rows],
+                lhsT=w1_codes[j, a][:, rows].bitcast(FP8X4),
+                lhsT_scale=w1_plane[j, a][:, rows],
                 rhs=v_codes[a][:, cols].bitcast(FP8X4),
                 rhs_scale=v_plane[4 * a : P, cols],
-                start=(a == 0),
-                stop=(a == K_PASSES - 1),
+                start=(a == order[0]),
+                stop=(a == order[-1]),
             )
 
-        def project_tile(c):
+        def project_tile(c, order):
             for half in range(2):
-                for a in range(K_PASSES):
-                    project(c, half, a)
+                for a in order:
+                    project(c, half, a, order)
 
         def drain(c, copy_high=nc.scalar.copy):
             nc.scalar.copy(h[c][:, 0:BANK], h_bank(c, 0)[:])
             copy_high(h[c][:, BANK:S], h_bank(c, 1)[:])
 
-        def gather_ends(c, b0, b1):
-            edges = slice(b0 * P, b1 * P)
-            entries = slice(b0 * P // LANES, b1 * P // LANES)
-            nc.vector.tensor_copy(first[c][:, edges], h[c][:].indirect(pos1_sb[:, entries]))
-            nc.vector.tensor_tensor(
-                second[c][:, edges], h[c][:].indirect(pos2_sb[:, entries]), minus_one[:, 0 : (b1 - b0) * P], ALU.mult
-            )
+        def entries(e0, e1):
+            return slice(e0 // LANES, e1 // LANES)
 
-        def difference(dst, c, b):
-            edges = slice(b * P, (b + 1) * P)
-            nc.tensor.matmul(dst, lhsT=first[c][:, edges], rhs=identity[:], start=True, stop=False, is_transpose=True)
-            nc.tensor.matmul(dst, lhsT=second[c][:, edges], rhs=identity[:], start=False, stop=True, is_transpose=True)
+        def gather_second(dst, c, e0, e1):
+            nc.vector.tensor_copy(dst, h[c][:].indirect(pos2_sb[:, entries(e0, e1)]))
 
-        def square(bank, b0, b1, c0, c1):
-            width = (c1 - c0) * P
-            flat = z_rows[c0 // PACK][:].rearrange("p b w -> p (b w)").bitcast(BF16)
-            r0 = c0 % PACK * P
+        def gather_difference(dst, c, e0, e1, second):
+            nc.vector.tensor_tensor(dst, h[c][:].indirect(pos1_sb[:, entries(e0, e1)]), second, ALU.subtract)
+
+        def difference_tile(c, tag=None):
+            second = held([P, E], F32, "second%d" % c, tag)
+            dst = d_early[c][:] if c < PACK else d_late[:, c - PACK, :]
+            for e0 in (0, HALF):
+                gather_second(second[:, e0 : e0 + HALF], c, e0, e0 + HALF)
+            for e0 in (0, HALF):
+                gather_difference(dst[:, e0 : e0 + HALF], c, e0, e0 + HALF, second[:, e0 : e0 + HALF])
+
+        def seconds(b, dst, i0=0):
+            for i in range(i0, len(dst)):
+                gather_second(dst[i], TILES - LATE + i, b * P, (b + 1) * P)
+
+        def differences(b, second):
+            for i in range(LATE):
+                dst = d_late[:, PACK - LATE + i, b * P : (b + 1) * P]
+                gather_difference(dst, TILES - LATE + i, b * P, (b + 1) * P, second[i])
+
+        def turn(c, dst):
+            for b in range(BLOCKS):
+                nc.tensor.transpose(dst[:, b * P : (b + 1) * P], d_early[c][:, b * P : (b + 1) * P], identity[:])
+
+        def square_early(z_rows, c, src):
+            flat = z_rows[:].rearrange("p b w -> p (b w)").bitcast(BF16)
             nc.scalar.activation(
-                flat.rearrange("p (b r) -> p b r", b=BLOCKS)[:, b0:b1, r0 : r0 + width],
-                bank[:, 0 : (b1 - b0) * width].rearrange("p (b r) -> p b r", r=width),
+                flat.rearrange("p (b r) -> p b r", b=BLOCKS)[:, :, c * P : (c + 1) * P],
+                src[:].rearrange("p (b r) -> p b r", r=P),
                 ACT.Square,
             )
 
-        def square_tile(c, bank):
-            for b in range(BLOCKS):
-                difference(bank[:, b * P : (b + 1) * P], c, b)
-            square(bank, 0, BLOCKS, c, c + 1)
-
-        def square_late_tiles(b0, b1, bank):
-            for c in LATE_TILES:
-                gather_ends(c, b0, b1)
-            for b in range(b0, b1):
-                for c in LATE_TILES:
-                    at = (b - b0) * PAIR + c % 2 * P
-                    difference(bank[:, at : at + P], c, b)
-            square(bank, b0, b1, LATE_TILES[0], TILES)
-
-        def turn_back(g, b0, b1, bank, copy):
+        def turn_back(z_rows, z_cols, b0, b1, dst):
             for b in range(b0, b1):
                 for u in range(2):
                     at = (2 * (b - b0) + u) * P
-                    nc.tensor.transpose(bank[:, at : at + P], z_rows[g][:, b, u:DUOS:2], identity[:])
-            copy(
-                z_cols[g][:, b0 * P : b1 * P, :].rearrange("p (b e) u -> p b e u", e=P),
-                bank[:, 0 : 2 * (b1 - b0) * P].rearrange("p (b u e) -> p b e u", u=2, e=P),
+                    nc.tensor.transpose(dst[:, at : at + P], z_rows[:, b, u:DUOS:2], identity[:])
+            nc.scalar.copy(
+                z_cols[:, b0 * P : b1 * P, :].rearrange("p (b e) u -> p b e u", e=P),
+                dst[:, 0 : 2 * (b1 - b0) * P].rearrange("p (b u e) -> p b e u", u=2, e=P),
             )
 
-        def quantize_z(g, b0, b1):
-            edges = slice(b0 * P, b1 * P)
-            nc.vector.quantize_mx(
-                out=z_codes[g][:, edges].bitcast(FP8X4),
-                scales=z_plane[g][:, edges],
-                in_=z_cols[g][:, edges, :].rearrange("p e u -> p (e u)").bitcast(BF16),
+        def square_late(b, z):
+            nc.scalar.activation(
+                z.rearrange("p (c n t) -> p c t n", n=RUN, t=PACK),
+                d_late[:, :, b * P : (b + 1) * P].rearrange("p t (c n) -> p c t n", n=RUN),
+                ACT.Square,
             )
+
+        def quantize_z(g, b0, b1, src):
+            edges = slice(b0 * P, b1 * P)
+            nc.vector.quantize_mx(out=z_codes[g][:, edges].bitcast(FP8X4), scales=z_plane[g][:, edges], in_=src)
 
         def mix_pass(dst, n, g, b):
             edges = slice(b * P, (b + 1) * P)
@@ -229,10 +232,10 @@ def tile_list_cloth_edge_strain_kernel(
                 stop=(g == R_PASSES - 1),
             )
 
-        def mix(b, bank):
+        def mix(b, dst):
             for n in range(OUT_TILES):
                 for g in range(R_PASSES):
-                    mix_pass(bank[:, n * P : (n + 1) * P], n, g, b)
+                    mix_pass(dst[:, n * P : (n + 1) * P], n, g, b)
 
         def log_and_store(b, n0, n1):
             nc.scalar.activation(result[b][:, n0:n1, :], size[b][:, n0:n1, :], ACT.Ln, bias=1.0)
@@ -241,6 +244,12 @@ def tile_list_cloth_edge_strain_kernel(
                 in_=result[b][:, n0:n1, :],
             )
 
+        def finish(b, y_bank):
+            y = y_bank[:].rearrange("p (n e) -> p n e", e=P)
+            nc.scalar.activation(size[b][:], y, ACT.Abs, bias=zero[:])
+            log_and_store(b, 0, OUT_TILES)
+
+        plain = (0, 1, 2)
         gather_words(0, 0, S)
         nc.vector.tensor_copy(v_plane[:], tab_plane[:].bitcast(U8).indirect(offs_sb[:]))
         last_pass = K_PASSES - 1
@@ -251,64 +260,107 @@ def tile_list_cloth_edge_strain_kernel(
             quantize_w1(0, a)
             for c in range(2):
                 for half in range(2):
-                    project(c, half, a)
+                    project(c, half, a, plain)
         round_w1(0, last_pass, nc.scalar.copy)
         gather_words(last_pass, 0, BANK)
         quantize_w1(0, last_pass)
-        project(0, 0, last_pass)
+        project(0, 0, last_pass, plain)
         gather_words(last_pass, BANK, S)
-        project(0, 1, last_pass)
-        project(1, 0, last_pass)
-        project(1, 1, last_pass)
+        project(0, 1, last_pass, plain)
+        project(1, 0, last_pass, plain)
+        project(1, 1, last_pass, plain)
 
-        drain(0, nc.vector.tensor_copy)
-        gather_ends(0, 0, BLOCKS)
-        prepare_pair(1)
-        project_tile(2)
-        for c in range(1, LATE_TILES[0]):
-            if c % 2 == 0:
-                prepare_pair(c // 2 + 1)
-            drain(c)
-            if c >= 2:
-                square_tile(c - 2, h_bank(c, 1))
-            project_tile(c + 2)
-            gather_ends(c, 0, BLOCKS)
-        drain(LATE_TILES[0])
-        for i in range(len(back)):
-            turn_back(0, 2 * i, 2 * i + 2, back[i], nc.scalar.copy)
-        drain(LATE_TILES[1])
-        square_tile(LATE_TILES[0] - 2, high[0])
-        square_tile(LATE_TILES[1] - 2, high[3])
-        quantize_z(0, 0, BLOCKS)
+        round_w1(1, 0, nc.scalar.copy)
+        round_w1(1, 1, nc.scalar.copy)
+        drain(0)
+        drain(1)
+        round_w1(1, 2, nc.vector.tensor_copy)
+        quantize_w1(1, 0)
+        quantize_w1(1, 2)
+        quantize_w1(1, 1)
+        project_tile(2, (0, 2, 1))
+        project_tile(3, plain)
+        difference_tile(0, "rounded1_1")
+        difference_tile(1)
+        round_dealt(0, 0, P // 2, nc.scalar.copy)
+        round_dealt(0, P // 2, P, nc.scalar.copy)
+        drain(2)
+        round_dealt(1, 0, P // 2, nc.scalar.copy)
+        round_dealt(1, P // 2, P, nc.scalar.copy)
+        round_dealt(2, 0, SHARE, nc.scalar.copy)
+        drain(3)
+        quantize_w1(2, 0)
+        difference_tile(2)
+        round_dealt(2, SHARE, P, nc.vector.tensor_copy)
+        quantize_w1(2, 1)
+        quantize_w1(2, 2)
+        turn(0, bank[6])
+        turn(1, bank[7])
+        for a in range(2):
+            for c in (4, 5):
+                for half in range(2):
+                    project(c, half, a, plain)
+        for half in range(2):
+            project(6, half, 0, plain)
+        for c in (4, 5):
+            for half in range(2):
+                project(c, half, 2, plain)
+        for half in range(2):
+            for a in (1, 2):
+                project(6, half, a, plain)
+        difference_tile(3, "rounded2_2")
+        z_rows = held([P, BLOCKS, DUOS], F32, "z_rows", "raw2_2")
+        square_early(z_rows, 0, bank[6])
+        square_early(z_rows, 1, bank[7])
+        drain(4)
+        project_tile(7, plain)
+        turn(2, bank[6])
+        turn(3, bank[7])
+        drain(5)
+        drain(6)
+        drain(7)
+        square_early(z_rows, 2, bank[6])
+        square_early(z_rows, 3, bank[7])
+        difference_tile(4)
+        z_cols = held([P, E, 2], F32, "z_cols")
+        turn_back(z_rows, z_cols, 0, 2, bank[4])
+        turn_back(z_rows, z_cols, 2, 4, bank[5])
 
         last = BLOCKS - 1
-        y_banks = [high[2], high[3], low[0]]
-        square_late_tiles(0, 2, low[0])
-        square_late_tiles(2, last, low[1])
-        turn_back(1, 0, 2, back[0], nc.scalar.copy)
-        square_late_tiles(last, BLOCKS, back[0])
-        quantize_z(1, 0, 2)
+        y_banks = [bank[6], bank[7], bank[2]]
+        last_y = [bank[i][:, 0:P] for i in (0, 1, 4, 5)]
+        z01 = held([P, 2 * P * PACK], BF16, "z01", "raw2_2")
+        for b in range(2):
+            second = held([P, LATE, P], F32, "second_late%d" % b)
+            seconds(b, [second[:, i, :] for i in range(LATE)])
+            differences(b, [second[:, i, :] for i in range(LATE)])
+            square_late(b, z01[:, b * PASS : (b + 1) * PASS])
+        quantize_z(0, 0, BLOCKS, z_cols[:].rearrange("p e u -> p (e u)").bitcast(BF16))
+        quantize_z(1, 0, 2, z01[:])
         mix(0, y_banks[0])
-        turn_back(1, 2, last, back[1], nc.vector.tensor_copy)
-        quantize_z(1, 2, last)
-        turn_back(1, last, BLOCKS, high[1], nc.vector.tensor_copy)
         mix(1, y_banks[1])
-        mix(2, y_banks[2])
-        last_y = [bank[:, 0:P] for bank in (back[0], back[1], low[1], high[0])]
         for n in range(OUT_TILES):
             mix_pass(last_y[n], n, 0, last)
-        quantize_z(1, last, BLOCKS)
+        second = held([P, 2 * LATE - 1, P], F32, "second_late2", "raw2_2")
+        seconds(2, [second[:, i, :] for i in range(LATE)])
+        differences(2, [second[:, i, :] for i in range(LATE)])
+        finish(0, y_banks[0])
+        z2 = held([P, PASS], BF16, "z2", "size0")
+        square_late(2, z2[:])
+        parts = [second[:, LATE + i, :] for i in range(LATE - 1)]
+        seconds(3, parts)
+        quantize_z(1, 2, 3, z2[:])
+        mix(2, y_banks[2])
+        finish(1, y_banks[1])
+        parts.append(held([P, P], F32, "second_late3", "size0")[:])
+        seconds(3, parts, LATE - 1)
+        differences(3, parts)
+        z3 = held([P, PASS], BF16, "z3", "size1")
+        square_late(3, z3[:])
+        quantize_z(1, 3, 4, z3[:])
         for n in range(OUT_TILES):
             mix_pass(last_y[n], n, 1, last)
-
-        for b in range(last):
-            y = y_banks[b][:].rearrange("p (n e) -> p n e", e=P)
-            if b == last - 1:
-                nc.vector.tensor_scalar(result[b][:], y, -1.0, None, ALU.mult)
-                nc.vector.tensor_tensor(size[b][:], y, result[b][:], ALU.max)
-            else:
-                nc.scalar.activation(size[b][:], y, ACT.Abs, bias=zero[:])
-            log_and_store(b, 0, OUT_TILES)
+        finish(2, y_banks[2])
         for n0 in range(0, OUT_TILES, 2):
             for n in (n0, n0 + 1):
                 nc.scalar.activation(size[last][:, n, :], last_y[n], ACT.Abs, bias=zero[:])

@@ -32,7 +32,7 @@ BLOCKS = E // P
 OUT_TILES = N // P
 DUOS = PASS // 2
 HALF = E // 2
-SHARE = 64
+SHARE = 40
 LATE = 3
 
 
@@ -61,18 +61,23 @@ def tile_list_cloth_edge_strain_kernel(
         for j, (c0, c1) in enumerate(part_cols):
             for a in range(K_PASSES):
                 raw[j, a] = held([P, PACK, c1 - c0], F32, "raw%d_%d" % (j, a))
-                rounded[j, a] = held([P, PACK * (c1 - c0)], BF16, "rounded%d_%d" % (j, a))
+                if (j, a) not in ((1, 2), (2, 1)):
+                    rounded[j, a] = held([P, PACK * (c1 - c0)], BF16, "rounded%d_%d" % (j, a))
                 w1_codes[j, a] = held([P, c1 - c0], U32, "w1_codes%d_%d" % (j, a))
                 w1_plane[j, a] = held([P, c1 - c0], U8, "w1_plane%d_%d" % (j, a))
-        h = [held([P, S], F32, "h%d" % c) for c in range(TILES)]
-        d_early = [held([P, E], F32, "d_early%d" % c) for c in range(PACK)]
+        h = {c: held([P, S], F32, "h%d" % c) for c in range(2, TILES)}
+        minus_one = held([P, E], F32, "minus_one")
+        first, second_early = {}, {}
         d_late = held([P, PACK, E], F32, "d_late")
-        z_codes = [held([P, E], U32, "z_codes%d" % g) for g in range(R_PASSES)]
+        early_codes = held([P, E], U32, "early_codes")
+        z_codes = {(0, b): early_codes[:, b * P : (b + 1) * P] for b in range(BLOCKS)}
         z_plane = [held([P, E], U8, "z_plane%d" % g) for g in range(R_PASSES)]
         size = [held([P, OUT_TILES, P], F32, "size%d" % b) for b in range(BLOCKS)]
         result = [held([P, OUT_TILES, P], F32, "result%d" % b) for b in range(BLOCKS)]
         identity = held([P, P], F32, "identity")
         bank = [psum.tile([P, BANK], F32, name="bank%d" % i) for i in range(8)]
+
+        y_banks = [bank[i] for i in (6, 7, 2, 0, 1)]
 
         nc.gpsimd.memset(tab_plane[:], 0)
         one = held([P, 1], F32, "one")
@@ -80,6 +85,7 @@ def tile_list_cloth_edge_strain_kernel(
         nc.vector.memset(one[:], 1.0)
         nc.scalar.activation(zero[:], one[:], ACT.Ln)
         nc.vector.memset(w2_plane[:], 0)
+        nc.vector.memset(minus_one[:], -1.0)
         make_identity(nc, identity[:])
 
         def load_table(a):
@@ -91,16 +97,17 @@ def tile_list_cloth_edge_strain_kernel(
             rows = w1[a * PASS : (a + 1) * PASS, c0:c1]
             nc.sync.dma_start(out=raw[j, a][:], in_=rows.rearrange("(p i) c -> p i c", i=PACK))
 
+        load_table(0)
         nc.sync.dma_start(offs_sb[:], offs)
-        for a in range(K_PASSES):
-            load_table(a)
+        load_w1(0, 0)
+        for q in range(QUADS):
+            nc.sync.dma_start(
+                out=tab_plane[32 * q : 32 * q + 4 * K_PASSES, :],
+                in_=tab_scales[:, 4 * q : 4 * q + 4, :].bitcast(I32),
+            )
+        for a in range(1, K_PASSES):
             load_w1(0, a)
-            if a == 0:
-                for q in range(QUADS):
-                    nc.sync.dma_start(
-                        out=tab_plane[32 * q : 32 * q + 4 * K_PASSES, :],
-                        in_=tab_scales[:, 4 * q : 4 * q + 4, :].bitcast(I32),
-                    )
+            load_table(a)
         nc.sync.dma_start(pos1_sb[:], pos1)
         nc.sync.dma_start(pos2_sb[:], pos2)
         for j in range(1, len(part_cols)):
@@ -170,26 +177,36 @@ def tile_list_cloth_edge_strain_kernel(
         def gather_difference(dst, c, e0, e1, second):
             nc.vector.tensor_tensor(dst, h[c][:].indirect(pos1_sb[:, entries(e0, e1)]), second, ALU.subtract)
 
+        def gather_ends(c, tag=None):
+            ends = held([P, 2 * E], F32, "ends%d" % c, tag)
+            first[c], second_early[c] = ends[:, 0:E], ends[:, E : 2 * E]
+            nc.vector.tensor_copy(first[c], h[c][:].indirect(pos1_sb[:]))
+            nc.vector.tensor_tensor(second_early[c], h[c][:].indirect(pos2_sb[:]), minus_one[:], ALU.mult)
+
         def difference_tile(c, tag=None):
             second = held([P, E], F32, "second%d" % c, tag)
-            dst = d_early[c][:] if c < PACK else d_late[:, c - PACK, :]
+            dst = d_late[:, c - PACK, :]
             for e0 in (0, HALF):
                 gather_second(second[:, e0 : e0 + HALF], c, e0, e0 + HALF)
             for e0 in (0, HALF):
                 gather_difference(dst[:, e0 : e0 + HALF], c, e0, e0 + HALF, second[:, e0 : e0 + HALF])
 
-        def seconds(b, dst, i0=0):
+        def seconds(b0, b1, dst, i0=0):
             for i in range(i0, len(dst)):
-                gather_second(dst[i], TILES - LATE + i, b * P, (b + 1) * P)
+                gather_second(dst[i], TILES - LATE + i, b0 * P, b1 * P)
 
-        def differences(b, second):
+        def differences(b0, b1, second):
             for i in range(LATE):
-                dst = d_late[:, PACK - LATE + i, b * P : (b + 1) * P]
-                gather_difference(dst, TILES - LATE + i, b * P, (b + 1) * P, second[i])
+                dst = d_late[:, PACK - LATE + i, b0 * P : b1 * P]
+                gather_difference(dst, TILES - LATE + i, b0 * P, b1 * P, second[i])
 
         def turn(c, dst):
             for b in range(BLOCKS):
-                nc.tensor.transpose(dst[:, b * P : (b + 1) * P], d_early[c][:, b * P : (b + 1) * P], identity[:])
+                edges = slice(b * P, (b + 1) * P)
+                for i, src in enumerate((first[c], second_early[c])):
+                    nc.tensor.matmul(
+                        dst[:, edges], lhsT=src[:, edges], rhs=identity[:], start=(i == 0), stop=(i == 1), is_transpose=True
+                    )
 
         def square_early(z_rows, c, src):
             flat = z_rows[:].rearrange("p b w -> p (b w)").bitcast(BF16)
@@ -209,33 +226,40 @@ def tile_list_cloth_edge_strain_kernel(
                 dst[:, 0 : 2 * (b1 - b0) * P].rearrange("p (b u e) -> p b e u", u=2, e=P),
             )
 
-        def square_late(b, z):
+        def square_late(b0, b1, z):
             nc.scalar.activation(
                 z.rearrange("p (c n t) -> p c t n", n=RUN, t=PACK),
-                d_late[:, :, b * P : (b + 1) * P].rearrange("p t (c n) -> p c t n", n=RUN),
+                d_late[:, :, b0 * P : b1 * P].rearrange("p t (c n) -> p c t n", n=RUN),
                 ACT.Square,
             )
 
-        def quantize_z(g, b0, b1, src):
-            edges = slice(b0 * P, b1 * P)
-            nc.vector.quantize_mx(out=z_codes[g][:, edges].bitcast(FP8X4), scales=z_plane[g][:, edges], in_=src)
+        def quantize_late(b0, b1, src):
+            codes = held([P, (b1 - b0) * P], U32, "late_codes%d" % b0)
+            for b in range(b0, b1):
+                z_codes[1, b] = codes[:, (b - b0) * P : (b - b0 + 1) * P]
+            nc.vector.quantize_mx(out=codes[:].bitcast(FP8X4), scales=z_plane[1][:, b0 * P : b1 * P], in_=src)
 
-        def mix_pass(dst, n, g, b):
+        def y_group(b, n):
+            if b < BLOCKS - 1:
+                return y_banks[b], 0, OUT_TILES - 1
+            return y_banks[b + n // 2], n - n % 2, n - n % 2 + 1
+
+        def mix_pass(n, g, b):
+            dst, n_first, n_last = y_group(b, n)
             edges = slice(b * P, (b + 1) * P)
             nc.tensor.matmul_mx(
-                out=dst,
+                out=dst[:, n * P : (n + 1) * P],
                 lhsT=w2_codes[:, g, :].bitcast(U8)[:, 2 * n * P : 2 * (n + 1) * P].bitcast(FP4X4),
                 lhsT_scale=w2_plane[:, g, :].bitcast(U8)[:, n * P : (n + 1) * P],
-                rhs=z_codes[g][:, edges].bitcast(FP8X4),
+                rhs=z_codes[g, b].bitcast(FP8X4),
                 rhs_scale=z_plane[g][:, edges],
-                start=(g == 0),
-                stop=(g == R_PASSES - 1),
+                start=(g == 0 and n == n_first),
+                stop=(g == R_PASSES - 1 and n == n_last),
             )
 
-        def mix(b, dst):
+        def mix(g, b):
             for n in range(OUT_TILES):
-                for g in range(R_PASSES):
-                    mix_pass(dst[:, n * P : (n + 1) * P], n, g, b)
+                mix_pass(n, g, b)
 
         def log_and_store(b, n0, n1):
             nc.scalar.activation(result[b][:, n0:n1, :], size[b][:, n0:n1, :], ACT.Ln, bias=1.0)
@@ -244,53 +268,61 @@ def tile_list_cloth_edge_strain_kernel(
                 in_=result[b][:, n0:n1, :],
             )
 
-        def finish(b, y_bank):
-            y = y_bank[:].rearrange("p (n e) -> p n e", e=P)
-            nc.scalar.activation(size[b][:], y, ACT.Abs, bias=zero[:])
-            log_and_store(b, 0, OUT_TILES)
+        def magnitude(b, n0, n1):
+            y = y_group(b, n0)[0][:].rearrange("p (n e) -> p n e", e=P)
+            nc.scalar.activation(size[b][:, n0:n1, :], y[:, n0:n1, :], ACT.Abs, bias=zero[:])
 
         plain = (0, 1, 2)
         gather_words(0, 0, S)
         nc.vector.tensor_copy(v_plane[:], tab_plane[:].bitcast(U8).indirect(offs_sb[:]))
         last_pass = K_PASSES - 1
-        for a in range(last_pass):
+        for a in range(K_PASSES):
             round_w1(0, a, nc.scalar.copy)
-            if a > 0:
-                gather_words(a, 0, S)
+        for a in range(last_pass):
             quantize_w1(0, a)
+        gather_words(1, 0, S)
+        quantize_w1(0, last_pass)
+        for a in range(last_pass):
             for c in range(2):
                 for half in range(2):
                     project(c, half, a, plain)
-        round_w1(0, last_pass, nc.scalar.copy)
         gather_words(last_pass, 0, BANK)
-        quantize_w1(0, last_pass)
-        project(0, 0, last_pass, plain)
         gather_words(last_pass, BANK, S)
+        project(0, 0, last_pass, plain)
         project(0, 1, last_pass, plain)
         project(1, 0, last_pass, plain)
         project(1, 1, last_pass, plain)
 
         round_w1(1, 0, nc.scalar.copy)
-        round_w1(1, 1, nc.scalar.copy)
+        h[0] = held([P, S], F32, "h0", "raw1_0")
         drain(0)
-        drain(1)
-        round_w1(1, 2, nc.vector.tensor_copy)
         quantize_w1(1, 0)
-        quantize_w1(1, 2)
+        h[1] = held([P, S], F32, "h1", "rounded1_0")
+        drain(1)
+        round_w1(1, 1, nc.vector.tensor_copy)
+        for c in (2, 3):
+            for half in range(2):
+                project(c, half, 0, plain)
+        rounded[1, 2] = held([P, PACK * PAIR], BF16, "rounded1_2", "w1_codes1_0")
+        round_w1(1, 2, nc.scalar.copy)
+        gather_ends(0, "raw1_1")
         quantize_w1(1, 1)
-        project_tile(2, (0, 2, 1))
-        project_tile(3, plain)
-        difference_tile(0, "rounded1_1")
-        difference_tile(1)
+        quantize_w1(1, 2)
+        for c in (2, 3):
+            for half in range(2):
+                for a in (1, 2):
+                    project(c, half, a, plain)
+        gather_ends(1, "w1_codes1_0")
+        rounded[2, 1] = held([P, PACK * PASS], BF16, "rounded2_1", "w1_codes1_1")
         round_dealt(0, 0, P // 2, nc.scalar.copy)
-        round_dealt(0, P // 2, P, nc.scalar.copy)
         drain(2)
+        round_dealt(0, P // 2, P, nc.scalar.copy)
         round_dealt(1, 0, P // 2, nc.scalar.copy)
         round_dealt(1, P // 2, P, nc.scalar.copy)
         round_dealt(2, 0, SHARE, nc.scalar.copy)
         drain(3)
         quantize_w1(2, 0)
-        difference_tile(2)
+        gather_ends(2)
         round_dealt(2, SHARE, P, nc.vector.tensor_copy)
         quantize_w1(2, 1)
         quantize_w1(2, 2)
@@ -308,7 +340,7 @@ def tile_list_cloth_edge_strain_kernel(
         for half in range(2):
             for a in (1, 2):
                 project(6, half, a, plain)
-        difference_tile(3, "rounded2_2")
+        gather_ends(3, "rounded2_2")
         z_rows = held([P, BLOCKS, DUOS], F32, "z_rows", "raw2_2")
         square_early(z_rows, 0, bank[6])
         square_early(z_rows, 1, bank[7])
@@ -326,42 +358,53 @@ def tile_list_cloth_edge_strain_kernel(
         turn_back(z_rows, z_cols, 0, 2, bank[4])
         turn_back(z_rows, z_cols, 2, 4, bank[5])
 
-        last = BLOCKS - 1
-        y_banks = [bank[6], bank[7], bank[2]]
-        last_y = [bank[i][:, 0:P] for i in (0, 1, 4, 5)]
+        second = held([P, LATE, 2 * P], F32, "second_late0")
+        parts = [second[:, i, :] for i in range(LATE)]
+        seconds(0, 2, parts)
+        differences(0, 2, parts)
         z01 = held([P, 2 * P * PACK], BF16, "z01", "raw2_2")
-        for b in range(2):
-            second = held([P, LATE, P], F32, "second_late%d" % b)
-            seconds(b, [second[:, i, :] for i in range(LATE)])
-            differences(b, [second[:, i, :] for i in range(LATE)])
-            square_late(b, z01[:, b * PASS : (b + 1) * PASS])
-        quantize_z(0, 0, BLOCKS, z_cols[:].rearrange("p e u -> p (e u)").bitcast(BF16))
-        quantize_z(1, 0, 2, z01[:])
-        mix(0, y_banks[0])
-        mix(1, y_banks[1])
-        for n in range(OUT_TILES):
-            mix_pass(last_y[n], n, 0, last)
-        second = held([P, 2 * LATE - 1, P], F32, "second_late2", "raw2_2")
-        seconds(2, [second[:, i, :] for i in range(LATE)])
-        differences(2, [second[:, i, :] for i in range(LATE)])
-        finish(0, y_banks[0])
-        z2 = held([P, PASS], BF16, "z2", "size0")
-        square_late(2, z2[:])
-        parts = [second[:, LATE + i, :] for i in range(LATE - 1)]
-        seconds(3, parts)
-        quantize_z(1, 2, 3, z2[:])
-        mix(2, y_banks[2])
-        finish(1, y_banks[1])
-        parts.append(held([P, P], F32, "second_late3", "size0")[:])
-        seconds(3, parts, LATE - 1)
-        differences(3, parts)
-        z3 = held([P, PASS], BF16, "z3", "size1")
-        square_late(3, z3[:])
-        quantize_z(1, 3, 4, z3[:])
-        for n in range(OUT_TILES):
-            mix_pass(last_y[n], n, 1, last)
-        finish(2, y_banks[2])
-        for n0 in range(0, OUT_TILES, 2):
-            for n in (n0, n0 + 1):
-                nc.scalar.activation(size[last][:, n, :], last_y[n], ACT.Abs, bias=zero[:])
-            log_and_store(last, n0, n0 + 2)
+        square_late(0, 2, z01[:])
+        nc.vector.quantize_mx(
+            out=early_codes[:].bitcast(FP8X4),
+            scales=z_plane[0][:],
+            in_=z_cols[:].rearrange("p e u -> p (e u)").bitcast(BF16),
+        )
+        mix(0, 0)
+        second = held([P, LATE - 1, P], F32, "second_late2", "z_cols")
+        parts = [second[:, i, :] for i in range(LATE - 1)]
+        seconds(2, 3, parts)
+        quantize_late(0, 2, z01[:])
+        mix(1, 0)
+        mix(0, 1)
+        mix(1, 1)
+        mix(0, 2)
+        second = held([P, LATE, P], F32, "second_late3", "raw2_2")
+        parts.append(second[:, 0, :])
+        seconds(2, 3, parts, LATE - 1)
+        differences(2, 3, parts)
+        z2 = held([P, PASS], BF16, "z2")
+        square_late(2, 3, z2[:])
+        magnitude(0, 0, OUT_TILES)
+        log_and_store(0, 0, OUT_TILES)
+        parts = [second[:, i, :] for i in range(1, LATE)]
+        seconds(3, 4, parts)
+        quantize_late(2, 3, z2[:])
+        mix(1, 2)
+        mix(0, 3)
+        parts.append(held([P, P], F32, "second_late4", "z2")[:])
+        seconds(3, 4, parts, LATE - 1)
+        differences(3, 4, parts)
+        magnitude(1, 0, OUT_TILES)
+        z3 = held([P, PASS], BF16, "z3", "size0")
+        square_late(3, 4, z3[:])
+        log_and_store(1, 0, OUT_TILES)
+        quantize_late(3, 4, z3[:])
+        mix(1, 3)
+        y = y_banks[2][:].rearrange("p (n e) -> p n e", e=P)
+        nc.vector.tensor_scalar(result[2][:], y, -1.0, None, ALU.mult)
+        nc.vector.tensor_tensor(size[2][:], y, result[2][:], ALU.max)
+        magnitude(3, 0, 2)
+        log_and_store(3, 0, 2)
+        log_and_store(2, 0, OUT_TILES)
+        magnitude(3, 2, 4)
+        log_and_store(3, 2, 4)

@@ -32,7 +32,7 @@ BLOCKS = E // P
 OUT_TILES = N // P
 DUOS = PASS // 2
 HALF = E // 2
-SHARE = 40
+SHARE = 64
 LATE = 3
 
 
@@ -177,10 +177,12 @@ def tile_list_cloth_edge_strain_kernel(
         def gather_difference(dst, c, e0, e1, second):
             nc.vector.tensor_tensor(dst, h[c][:].indirect(pos1_sb[:, entries(e0, e1)]), second, ALU.subtract)
 
-        def gather_ends(c, tag=None):
+        def gather_ends(c, tag=None, between=None):
             ends = held([P, 2 * E], F32, "ends%d" % c, tag)
             first[c], second_early[c] = ends[:, 0:E], ends[:, E : 2 * E]
             nc.vector.tensor_copy(first[c], h[c][:].indirect(pos1_sb[:]))
+            if between:
+                between()
             nc.vector.tensor_tensor(second_early[c], h[c][:].indirect(pos2_sb[:]), minus_one[:], ALU.mult)
 
         def difference_tile(c, tag=None):
@@ -226,10 +228,10 @@ def tile_list_cloth_edge_strain_kernel(
                 dst[:, 0 : 2 * (b1 - b0) * P].rearrange("p (b u e) -> p b e u", u=2, e=P),
             )
 
-        def square_late(b0, b1, z):
+        def square_late(b0, b1, z, t0=0, t1=PACK):
             nc.scalar.activation(
-                z.rearrange("p (c n t) -> p c t n", n=RUN, t=PACK),
-                d_late[:, :, b0 * P : b1 * P].rearrange("p t (c n) -> p c t n", n=RUN),
+                z.rearrange("p (c n t) -> p c t n", n=RUN, t=PACK)[:, :, t0:t1],
+                d_late[:, t0:t1, b0 * P : b1 * P].rearrange("p t (c n) -> p c t n", n=RUN),
                 ACT.Square,
             )
 
@@ -321,38 +323,29 @@ def tile_list_cloth_edge_strain_kernel(
         round_dealt(1, P // 2, P, nc.scalar.copy)
         round_dealt(2, 0, SHARE, nc.scalar.copy)
         drain(3)
-        quantize_w1(2, 0)
-        gather_ends(2)
+        gather_ends(2, None, lambda: quantize_w1(2, 0))
         round_dealt(2, SHARE, P, nc.vector.tensor_copy)
         quantize_w1(2, 1)
         quantize_w1(2, 2)
         turn(0, bank[6])
         turn(1, bank[7])
-        for a in range(2):
-            for c in (4, 5):
-                for half in range(2):
-                    project(c, half, a, plain)
-        for half in range(2):
-            project(6, half, 0, plain)
-        for c in (4, 5):
+        for c, a in ((4, 0), (5, 0), (4, 1), (4, 2), (5, 1), (5, 2)):
             for half in range(2):
-                project(c, half, 2, plain)
-        for half in range(2):
-            for a in (1, 2):
-                project(6, half, a, plain)
+                project(c, half, a, plain)
+        project_tile(6, plain)
         gather_ends(3, "rounded2_2")
         z_rows = held([P, BLOCKS, DUOS], F32, "z_rows", "raw2_2")
         square_early(z_rows, 0, bank[6])
         square_early(z_rows, 1, bank[7])
         drain(4)
-        project_tile(7, plain)
         turn(2, bank[6])
         turn(3, bank[7])
+        project_tile(7, plain)
         drain(5)
         drain(6)
-        drain(7)
         square_early(z_rows, 2, bank[6])
         square_early(z_rows, 3, bank[7])
+        drain(7)
         difference_tile(4)
         z_cols = held([P, E, 2], F32, "z_cols")
         turn_back(z_rows, z_cols, 0, 2, bank[4])
@@ -364,29 +357,29 @@ def tile_list_cloth_edge_strain_kernel(
         differences(0, 2, parts)
         z01 = held([P, 2 * P * PACK], BF16, "z01", "raw2_2")
         square_late(0, 2, z01[:])
+        second = held([P, LATE - 1, P], F32, "second_late2")
+        parts = [second[:, i, :] for i in range(LATE - 1)]
+        seconds(2, 3, parts)
         nc.vector.quantize_mx(
             out=early_codes[:].bitcast(FP8X4),
             scales=z_plane[0][:],
             in_=z_cols[:].rearrange("p e u -> p (e u)").bitcast(BF16),
         )
         mix(0, 0)
-        second = held([P, LATE - 1, P], F32, "second_late2", "z_cols")
-        parts = [second[:, i, :] for i in range(LATE - 1)]
-        seconds(2, 3, parts)
         quantize_late(0, 2, z01[:])
         mix(1, 0)
         mix(0, 1)
         mix(1, 1)
         mix(0, 2)
-        second = held([P, LATE, P], F32, "second_late3", "raw2_2")
-        parts.append(second[:, 0, :])
+        second = held([P, LATE - 1, P], F32, "second_late3", "raw2_2")
+        parts.append(held([P, P], F32, "second_late5", "z_cols")[:])
         seconds(2, 3, parts, LATE - 1)
         differences(2, 3, parts)
         z2 = held([P, PASS], BF16, "z2")
         square_late(2, 3, z2[:])
         magnitude(0, 0, OUT_TILES)
         log_and_store(0, 0, OUT_TILES)
-        parts = [second[:, i, :] for i in range(1, LATE)]
+        parts = [second[:, i, :] for i in range(LATE - 1)]
         seconds(3, 4, parts)
         quantize_late(2, 3, z2[:])
         mix(1, 2)
@@ -396,7 +389,8 @@ def tile_list_cloth_edge_strain_kernel(
         differences(3, 4, parts)
         magnitude(1, 0, OUT_TILES)
         z3 = held([P, PASS], BF16, "z3", "size0")
-        square_late(3, 4, z3[:])
+        square_late(3, 4, z3[:], 0, 2)
+        square_late(3, 4, z3[:], 2, PACK)
         log_and_store(1, 0, OUT_TILES)
         quantize_late(3, 4, z3[:])
         mix(1, 3)

@@ -24,16 +24,18 @@ K_PASSES = K // PASS
 R_PASSES = H // PASS
 QUADS = 4
 BANK = 512
+BANKS = 8
+H_SETS = 3
 LANES = 16
 RUN = 4
-PAIR = 2 * P
 TILES = H // P
 BLOCKS = E // P
 OUT_TILES = N // P
 DUOS = PASS // 2
-HALF = E // 2
-SHARE = 64
-LATE = 3
+PARTS = ((0, 2 * P), (2 * P, PASS), (PASS, H))
+DEALT = 2
+BY_BLOCKS = 3
+SCALAR_SHARE = 56
 
 
 def tile_list_cloth_edge_strain_kernel(
@@ -44,8 +46,8 @@ def tile_list_cloth_edge_strain_kernel(
         keep = ctx.enter_context(tc.tile_pool(name="keep", bufs=1))
         psum = ctx.enter_context(tc.psum_pool(name="psum", bufs=1))
 
-        def held(shape, dtype, name, tag=None):
-            return keep.tile(shape, dtype, name=name, tag=tag or name, align_bytes=64)
+        def held(shape, dtype, name, reuse=None):
+            return keep.tile(shape, dtype, name=name, tag=reuse or name, align_bytes=64)
 
         offs_sb = keep.tile([P, S // LANES], U16, name="offs_sb")
         pos1_sb = keep.tile([P, E // LANES], U16, name="pos1_sb")
@@ -56,27 +58,24 @@ def tile_list_cloth_edge_strain_kernel(
         table = [held([P, T], I32, "table%d" % a) for a in range(K_PASSES)]
         v_codes = [held([P, S], U32, "v_codes%d" % a) for a in range(K_PASSES)]
         v_plane = held([P, S], U8, "v_plane")
-        part_cols = [(0, PAIR), (PAIR, PASS), (PASS, H)]
         raw, rounded, w1_codes, w1_plane = {}, {}, {}, {}
-        for j, (c0, c1) in enumerate(part_cols):
+        for j, (c0, c1) in enumerate(PARTS):
             for a in range(K_PASSES):
                 raw[j, a] = held([P, PACK, c1 - c0], F32, "raw%d_%d" % (j, a))
-                if (j, a) not in ((1, 2), (2, 1)):
+                if (j, a) not in ((1, 2), (DEALT, 1)):
                     rounded[j, a] = held([P, PACK * (c1 - c0)], BF16, "rounded%d_%d" % (j, a))
                 w1_codes[j, a] = held([P, c1 - c0], U32, "w1_codes%d_%d" % (j, a))
                 w1_plane[j, a] = held([P, c1 - c0], U8, "w1_plane%d_%d" % (j, a))
         h = {c: held([P, S], F32, "h%d" % c) for c in range(2, TILES)}
         minus_one = held([P, E], F32, "minus_one")
-        first, second_early = {}, {}
-        d_late = held([P, PACK, E], F32, "d_late")
+        ends = {}
         early_codes = held([P, E], U32, "early_codes")
         z_codes = {(0, b): early_codes[:, b * P : (b + 1) * P] for b in range(BLOCKS)}
         z_plane = [held([P, E], U8, "z_plane%d" % g) for g in range(R_PASSES)]
         size = [held([P, OUT_TILES, P], F32, "size%d" % b) for b in range(BLOCKS)]
         result = [held([P, OUT_TILES, P], F32, "result%d" % b) for b in range(BLOCKS)]
         identity = held([P, P], F32, "identity")
-        bank = [psum.tile([P, BANK], F32, name="bank%d" % i) for i in range(8)]
-
+        bank = [psum.tile([P, BANK], F32, name="bank%d" % i) for i in range(BANKS)]
         y_banks = [bank[i] for i in (6, 7, 2, 0, 1)]
 
         nc.gpsimd.memset(tab_plane[:], 0)
@@ -93,7 +92,7 @@ def tile_list_cloth_edge_strain_kernel(
             nc.sync.dma_start(out=table[a][:], in_=words)
 
         def load_w1(j, a):
-            c0, c1 = part_cols[j]
+            c0, c1 = PARTS[j]
             rows = w1[a * PASS : (a + 1) * PASS, c0:c1]
             nc.sync.dma_start(out=raw[j, a][:], in_=rows.rearrange("(p i) c -> p i c", i=PACK))
 
@@ -110,7 +109,7 @@ def tile_list_cloth_edge_strain_kernel(
             load_table(a)
         nc.sync.dma_start(pos1_sb[:], pos1)
         nc.sync.dma_start(pos2_sb[:], pos2)
-        for j in range(1, len(part_cols)):
+        for j in range(1, len(PARTS)):
             for a in range(K_PASSES):
                 load_w1(j, a)
         nc.sync.dma_start(out=w2_codes[:], in_=w2_words.bitcast(I32).rearrange("a p c -> p a c"))
@@ -120,9 +119,12 @@ def tile_list_cloth_edge_strain_kernel(
                 in_=w2_scales[:, 4 * q : 4 * q + 4, :].bitcast(I32).rearrange("a r c -> r a c"),
             )
 
+        def entries(e0, e1):
+            return slice(e0 // LANES, e1 // LANES)
+
         def gather_words(a, s0, s1):
             window = table[a][:].bitcast(U32)
-            nc.vector.tensor_copy(v_codes[a][:, s0:s1], window.indirect(offs_sb[:, s0 // LANES : s1 // LANES]))
+            nc.vector.tensor_copy(v_codes[a][:, s0:s1], window.indirect(offs_sb[:, entries(s0, s1)]))
 
         def round_w1(j, a, copy):
             copy(
@@ -132,8 +134,8 @@ def tile_list_cloth_edge_strain_kernel(
 
         def round_dealt(a, m0, m1, copy):
             copy(
-                rounded[2, a][:].rearrange("p (t m i) -> p m i t", t=PACK, i=PACK)[:, m0:m1],
-                raw[2, a][:].rearrange("p i (m t) -> p m i t", t=PACK)[:, m0:m1],
+                rounded[DEALT, a][:].rearrange("p (t m i) -> p m i t", t=PACK, i=PACK)[:, m0:m1],
+                raw[DEALT, a][:].rearrange("p i (m t) -> p m i t", t=PACK)[:, m0:m1],
             )
 
         def quantize_w1(j, a):
@@ -142,12 +144,11 @@ def tile_list_cloth_edge_strain_kernel(
             )
 
         def h_bank(c, half):
-            return bank[2 * (c % 3) + half]
+            return bank[2 * (c % H_SETS) + half]
 
-        def project(c, half, a, order):
-            j = min(c // 2, 2)
-            t = c - 2 * j
-            rows = slice(t * P, (t + 1) * P)
+        def project(c, half, a):
+            j = min(c // 2, DEALT)
+            rows = slice((c - 2 * j) * P, (c - 2 * j + 1) * P)
             cols = slice(half * BANK, (half + 1) * BANK)
             nc.tensor.matmul_mx(
                 out=h_bank(c, half)[:],
@@ -155,113 +156,112 @@ def tile_list_cloth_edge_strain_kernel(
                 lhsT_scale=w1_plane[j, a][:, rows],
                 rhs=v_codes[a][:, cols].bitcast(FP8X4),
                 rhs_scale=v_plane[4 * a : P, cols],
-                start=(a == order[0]),
-                stop=(a == order[-1]),
+                start=(a == 0),
+                stop=(a == K_PASSES - 1),
             )
 
-        def project_tile(c, order):
-            for half in range(2):
-                for a in order:
-                    project(c, half, a, order)
+        def project_passes(tiles, passes):
+            for c in tiles:
+                for half in range(2):
+                    for a in passes:
+                        project(c, half, a)
 
-        def drain(c, copy_high=nc.scalar.copy):
+        def drain(c):
             nc.scalar.copy(h[c][:, 0:BANK], h_bank(c, 0)[:])
-            copy_high(h[c][:, BANK:S], h_bank(c, 1)[:])
+            nc.scalar.copy(h[c][:, BANK:S], h_bank(c, 1)[:])
 
-        def entries(e0, e1):
-            return slice(e0 // LANES, e1 // LANES)
+        def gather_first_end(c, reuse=None):
+            ends[c] = held([P, 2 * E], F32, "ends%d" % c, reuse)
+            nc.vector.tensor_copy(ends[c][:, 0:E], h[c][:].indirect(pos1_sb[:]))
 
-        def gather_second(dst, c, e0, e1):
-            nc.vector.tensor_copy(dst, h[c][:].indirect(pos2_sb[:, entries(e0, e1)]))
+        def gather_negated_end(c):
+            nc.vector.tensor_tensor(ends[c][:, E : 2 * E], h[c][:].indirect(pos2_sb[:]), minus_one[:], ALU.mult)
 
-        def gather_difference(dst, c, e0, e1, second):
-            nc.vector.tensor_tensor(dst, h[c][:].indirect(pos1_sb[:, entries(e0, e1)]), second, ALU.subtract)
-
-        def gather_ends(c, tag=None, between=None):
-            ends = held([P, 2 * E], F32, "ends%d" % c, tag)
-            first[c], second_early[c] = ends[:, 0:E], ends[:, E : 2 * E]
-            nc.vector.tensor_copy(first[c], h[c][:].indirect(pos1_sb[:]))
-            if between:
-                between()
-            nc.vector.tensor_tensor(second_early[c], h[c][:].indirect(pos2_sb[:]), minus_one[:], ALU.mult)
-
-        def difference_tile(c, tag=None):
-            second = held([P, E], F32, "second%d" % c, tag)
-            dst = d_late[:, c - PACK, :]
-            for e0 in (0, HALF):
-                gather_second(second[:, e0 : e0 + HALF], c, e0, e0 + HALF)
-            for e0 in (0, HALF):
-                gather_difference(dst[:, e0 : e0 + HALF], c, e0, e0 + HALF, second[:, e0 : e0 + HALF])
-
-        def seconds(b0, b1, dst, i0=0):
-            for i in range(i0, len(dst)):
-                gather_second(dst[i], TILES - LATE + i, b0 * P, b1 * P)
-
-        def differences(b0, b1, second):
-            for i in range(LATE):
-                dst = d_late[:, PACK - LATE + i, b0 * P : b1 * P]
-                gather_difference(dst, TILES - LATE + i, b0 * P, b1 * P, second[i])
+        def gather_ends(c, reuse):
+            gather_first_end(c, reuse)
+            gather_negated_end(c)
 
         def turn(c, dst):
             for b in range(BLOCKS):
-                edges = slice(b * P, (b + 1) * P)
-                for i, src in enumerate((first[c], second_early[c])):
+                for i in range(2):
                     nc.tensor.matmul(
-                        dst[:, edges], lhsT=src[:, edges], rhs=identity[:], start=(i == 0), stop=(i == 1), is_transpose=True
+                        dst[:, b * P : (b + 1) * P],
+                        lhsT=ends[c][:, i * E + b * P : i * E + (b + 1) * P],
+                        rhs=identity[:],
+                        start=(i == 0),
+                        stop=(i == 1),
+                        is_transpose=True,
                     )
 
-        def square_early(z_rows, c, src):
+        def square_early(c, src):
             flat = z_rows[:].rearrange("p b w -> p (b w)").bitcast(BF16)
             nc.scalar.activation(
-                flat.rearrange("p (b r) -> p b r", b=BLOCKS)[:, :, c * P : (c + 1) * P],
-                src[:].rearrange("p (b r) -> p b r", r=P),
+                flat.rearrange("p (b u c q j) -> p c u b q j", b=BLOCKS, u=2, c=PACK, j=2)[:, c],
+                src[:].rearrange("p (b q u j) -> p u b q j", b=BLOCKS, u=2, j=2),
                 ACT.Square,
             )
 
-        def turn_back(z_rows, z_cols, b0, b1, dst):
+        def turn_back(b0, b1, dst):
             for b in range(b0, b1):
                 for u in range(2):
                     at = (2 * (b - b0) + u) * P
-                    nc.tensor.transpose(dst[:, at : at + P], z_rows[:, b, u:DUOS:2], identity[:])
+                    nc.tensor.transpose(dst[:, at : at + P], z_rows[:, b, u * P : (u + 1) * P], identity[:])
             nc.scalar.copy(
                 z_cols[:, b0 * P : b1 * P, :].rearrange("p (b e) u -> p b e u", e=P),
                 dst[:, 0 : 2 * (b1 - b0) * P].rearrange("p (b u e) -> p b e u", u=2, e=P),
             )
 
-        def square_late(b0, b1, z, t0=0, t1=PACK):
+        def gather_second(dst, c, b0, b1):
+            nc.vector.tensor_copy(dst, h[c][:].indirect(pos2_sb[:, entries(b0 * P, b1 * P)]))
+
+        def gather_difference(second, c, b0, b1):
+            window = h[c][:].indirect(pos1_sb[:, entries(b0 * P, b1 * P)])
+            nc.vector.tensor_tensor(d_late[:, c - PACK, b0 * P : b1 * P], window, second, ALU.subtract)
+
+        def gather_seconds(b0, b1, i0, i1, name, reuse=None):
+            rows = held([P, i1 - i0, (b1 - b0) * P], F32, name, reuse)
+            for i in range(i0, i1):
+                gather_second(rows[:, i - i0, :], TILES - BY_BLOCKS + i, b0, b1)
+            return [rows[:, i - i0, :] for i in range(i0, i1)]
+
+        def gather_differences(b0, b1, seconds):
+            for i, second in enumerate(seconds):
+                gather_difference(second, TILES - BY_BLOCKS + i, b0, b1)
+
+        def square_late(z, b0, b1, t0, t1):
             nc.scalar.activation(
-                z.rearrange("p (c n t) -> p c t n", n=RUN, t=PACK)[:, :, t0:t1],
+                z[:].rearrange("p (c n t) -> p c t n", n=RUN, t=PACK)[:, :, t0:t1],
                 d_late[:, t0:t1, b0 * P : b1 * P].rearrange("p t (c n) -> p c t n", n=RUN),
                 ACT.Square,
             )
 
-        def quantize_late(b0, b1, src):
+        def quantize_late(z, b0, b1):
             codes = held([P, (b1 - b0) * P], U32, "late_codes%d" % b0)
             for b in range(b0, b1):
                 z_codes[1, b] = codes[:, (b - b0) * P : (b - b0 + 1) * P]
-            nc.vector.quantize_mx(out=codes[:].bitcast(FP8X4), scales=z_plane[1][:, b0 * P : b1 * P], in_=src)
+            nc.vector.quantize_mx(out=codes[:].bitcast(FP8X4), scales=z_plane[1][:, b0 * P : b1 * P], in_=z[:])
 
         def y_group(b, n):
             if b < BLOCKS - 1:
                 return y_banks[b], 0, OUT_TILES - 1
             return y_banks[b + n // 2], n - n % 2, n - n % 2 + 1
 
-        def mix_pass(n, g, b):
-            dst, n_first, n_last = y_group(b, n)
-            edges = slice(b * P, (b + 1) * P)
-            nc.tensor.matmul_mx(
-                out=dst[:, n * P : (n + 1) * P],
-                lhsT=w2_codes[:, g, :].bitcast(U8)[:, 2 * n * P : 2 * (n + 1) * P].bitcast(FP4X4),
-                lhsT_scale=w2_plane[:, g, :].bitcast(U8)[:, n * P : (n + 1) * P],
-                rhs=z_codes[g, b].bitcast(FP8X4),
-                rhs_scale=z_plane[g][:, edges],
-                start=(g == 0 and n == n_first),
-                stop=(g == R_PASSES - 1 and n == n_last),
-            )
-
         def mix(g, b):
             for n in range(OUT_TILES):
-                mix_pass(n, g, b)
+                dst, n_first, n_last = y_group(b, n)
+                nc.tensor.matmul_mx(
+                    out=dst[:, n * P : (n + 1) * P],
+                    lhsT=w2_codes[:, g, :].bitcast(U8)[:, 2 * n * P : 2 * (n + 1) * P].bitcast(FP4X4),
+                    lhsT_scale=w2_plane[:, g, :].bitcast(U8)[:, n * P : (n + 1) * P],
+                    rhs=z_codes[g, b].bitcast(FP8X4),
+                    rhs_scale=z_plane[g][:, b * P : (b + 1) * P],
+                    start=(g == 0 and n == n_first),
+                    stop=(g == R_PASSES - 1 and n == n_last),
+                )
+
+        def magnitude(b, n0, n1):
+            y = y_group(b, n0)[0][:].rearrange("p (n e) -> p n e", e=P)
+            nc.scalar.activation(size[b][:, n0:n1, :], y[:, n0:n1, :], ACT.Abs, bias=zero[:])
 
         def log_and_store(b, n0, n1):
             nc.scalar.activation(result[b][:, n0:n1, :], size[b][:, n0:n1, :], ACT.Ln, bias=1.0)
@@ -270,14 +270,9 @@ def tile_list_cloth_edge_strain_kernel(
                 in_=result[b][:, n0:n1, :],
             )
 
-        def magnitude(b, n0, n1):
-            y = y_group(b, n0)[0][:].rearrange("p (n e) -> p n e", e=P)
-            nc.scalar.activation(size[b][:, n0:n1, :], y[:, n0:n1, :], ACT.Abs, bias=zero[:])
-
-        plain = (0, 1, 2)
+        last_pass = K_PASSES - 1
         gather_words(0, 0, S)
         nc.vector.tensor_copy(v_plane[:], tab_plane[:].bitcast(U8).indirect(offs_sb[:]))
-        last_pass = K_PASSES - 1
         for a in range(K_PASSES):
             round_w1(0, a, nc.scalar.copy)
         for a in range(last_pass):
@@ -285,120 +280,110 @@ def tile_list_cloth_edge_strain_kernel(
         gather_words(1, 0, S)
         quantize_w1(0, last_pass)
         for a in range(last_pass):
-            for c in range(2):
-                for half in range(2):
-                    project(c, half, a, plain)
+            project_passes((0, 1), (a,))
         gather_words(last_pass, 0, BANK)
         gather_words(last_pass, BANK, S)
-        project(0, 0, last_pass, plain)
-        project(0, 1, last_pass, plain)
-        project(1, 0, last_pass, plain)
-        project(1, 1, last_pass, plain)
+        project_passes((0, 1), (last_pass,))
 
         round_w1(1, 0, nc.scalar.copy)
-        h[0] = held([P, S], F32, "h0", "raw1_0")
+        h[0] = held([P, S], F32, "h0", reuse="raw1_0")
         drain(0)
         quantize_w1(1, 0)
-        h[1] = held([P, S], F32, "h1", "rounded1_0")
+        h[1] = held([P, S], F32, "h1", reuse="rounded1_0")
         drain(1)
         round_w1(1, 1, nc.vector.tensor_copy)
-        for c in (2, 3):
-            for half in range(2):
-                project(c, half, 0, plain)
-        rounded[1, 2] = held([P, PACK * PAIR], BF16, "rounded1_2", "w1_codes1_0")
+        project_passes((2, 3), (0,))
+        rounded[1, 2] = held([P, PACK * 2 * P], BF16, "rounded1_2", reuse="w1_codes1_0")
         round_w1(1, 2, nc.scalar.copy)
-        gather_ends(0, "raw1_1")
+        gather_ends(0, reuse="raw1_1")
         quantize_w1(1, 1)
         quantize_w1(1, 2)
-        for c in (2, 3):
-            for half in range(2):
-                for a in (1, 2):
-                    project(c, half, a, plain)
-        gather_ends(1, "w1_codes1_0")
-        rounded[2, 1] = held([P, PACK * PASS], BF16, "rounded2_1", "w1_codes1_1")
+        project_passes((2, 3), (1, 2))
+        gather_ends(1, reuse="w1_codes1_0")
+
+        rounded[DEALT, 1] = held([P, PACK * PASS], BF16, "rounded2_1", reuse="w1_codes1_1")
         round_dealt(0, 0, P // 2, nc.scalar.copy)
         drain(2)
         round_dealt(0, P // 2, P, nc.scalar.copy)
         round_dealt(1, 0, P // 2, nc.scalar.copy)
         round_dealt(1, P // 2, P, nc.scalar.copy)
-        round_dealt(2, 0, SHARE, nc.scalar.copy)
+        round_dealt(2, 0, SCALAR_SHARE, nc.scalar.copy)
         drain(3)
-        gather_ends(2, None, lambda: quantize_w1(2, 0))
-        round_dealt(2, SHARE, P, nc.vector.tensor_copy)
-        quantize_w1(2, 1)
-        quantize_w1(2, 2)
+        gather_first_end(2)
+        quantize_w1(DEALT, 0)
+        gather_negated_end(2)
+        round_dealt(2, SCALAR_SHARE, P, nc.vector.tensor_copy)
+        quantize_w1(DEALT, 1)
+        quantize_w1(DEALT, 2)
         turn(0, bank[6])
         turn(1, bank[7])
-        for c, a in ((4, 0), (5, 0), (4, 1), (4, 2), (5, 1), (5, 2)):
-            for half in range(2):
-                project(c, half, a, plain)
-        project_tile(6, plain)
-        gather_ends(3, "rounded2_2")
-        z_rows = held([P, BLOCKS, DUOS], F32, "z_rows", "raw2_2")
-        square_early(z_rows, 0, bank[6])
-        square_early(z_rows, 1, bank[7])
+        project_passes((4, 5), (0,))
+        for c in (4, 5):
+            for a in (1, 2):
+                project_passes((c,), (a,))
+        project_passes((6,), range(K_PASSES))
+        gather_ends(3, reuse="rounded2_2")
+
+        z_rows = held([P, BLOCKS, DUOS], F32, "z_rows", reuse="raw2_2")
+        square_early(0, bank[6])
+        square_early(1, bank[7])
         drain(4)
         turn(2, bank[6])
         turn(3, bank[7])
-        project_tile(7, plain)
+        project_passes((7,), range(K_PASSES))
         drain(5)
         drain(6)
-        square_early(z_rows, 2, bank[6])
-        square_early(z_rows, 3, bank[7])
+        square_early(2, bank[6])
+        square_early(3, bank[7])
         drain(7)
-        difference_tile(4)
+        d_late = held([P, PACK, E], F32, "d_late", reuse="ends2")
+        second_of_4 = held([P, E], F32, "second_of_4")
+        gather_second(second_of_4[:], PACK, 0, BLOCKS)
+        gather_difference(second_of_4[:], PACK, 0, BLOCKS)
         z_cols = held([P, E, 2], F32, "z_cols")
-        turn_back(z_rows, z_cols, 0, 2, bank[4])
-        turn_back(z_rows, z_cols, 2, 4, bank[5])
+        turn_back(0, 2, bank[4])
+        turn_back(2, BLOCKS, bank[5])
 
-        second = held([P, LATE, 2 * P], F32, "second_late0")
-        parts = [second[:, i, :] for i in range(LATE)]
-        seconds(0, 2, parts)
-        differences(0, 2, parts)
-        z01 = held([P, 2 * P * PACK], BF16, "z01", "raw2_2")
-        square_late(0, 2, z01[:])
-        second = held([P, LATE - 1, P], F32, "second_late2")
-        parts = [second[:, i, :] for i in range(LATE - 1)]
-        seconds(2, 3, parts)
+        but_last = BY_BLOCKS - 1
+        gather_differences(0, 2, gather_seconds(0, 2, 0, BY_BLOCKS, "seconds_01"))
+        z_01 = held([P, 2 * PASS], BF16, "z_01", reuse="raw2_2")
+        square_late(z_01, 0, 2, 0, PACK)
+        seconds_2 = gather_seconds(2, 3, 0, but_last, "seconds_2")
         nc.vector.quantize_mx(
             out=early_codes[:].bitcast(FP8X4),
             scales=z_plane[0][:],
             in_=z_cols[:].rearrange("p e u -> p (e u)").bitcast(BF16),
         )
         mix(0, 0)
-        quantize_late(0, 2, z01[:])
+        quantize_late(z_01, 0, 2)
         mix(1, 0)
         mix(0, 1)
         mix(1, 1)
         mix(0, 2)
-        second = held([P, LATE - 1, P], F32, "second_late3", "raw2_2")
-        parts.append(held([P, P], F32, "second_late5", "z_cols")[:])
-        seconds(2, 3, parts, LATE - 1)
-        differences(2, 3, parts)
-        z2 = held([P, PASS], BF16, "z2")
-        square_late(2, 3, z2[:])
+        seconds_2.extend(gather_seconds(2, 3, but_last, BY_BLOCKS, "second_2_last", reuse="z_cols"))
+        gather_differences(2, 3, seconds_2)
+        z_2 = held([P, PASS], BF16, "z_2")
+        square_late(z_2, 2, 3, 0, PACK)
         magnitude(0, 0, OUT_TILES)
         log_and_store(0, 0, OUT_TILES)
-        parts = [second[:, i, :] for i in range(LATE - 1)]
-        seconds(3, 4, parts)
-        quantize_late(2, 3, z2[:])
+        seconds_3 = gather_seconds(3, BLOCKS, 0, but_last, "seconds_3", reuse="raw2_2")
+        quantize_late(z_2, 2, 3)
         mix(1, 2)
         mix(0, 3)
-        parts.append(held([P, P], F32, "second_late4", "z2")[:])
-        seconds(3, 4, parts, LATE - 1)
-        differences(3, 4, parts)
+        seconds_3.extend(gather_seconds(3, BLOCKS, but_last, BY_BLOCKS, "second_3_last", reuse="z_2"))
+        gather_differences(3, BLOCKS, seconds_3)
         magnitude(1, 0, OUT_TILES)
-        z3 = held([P, PASS], BF16, "z3", "size0")
-        square_late(3, 4, z3[:], 0, 2)
-        square_late(3, 4, z3[:], 2, PACK)
+        z_3 = held([P, PASS], BF16, "z_3", reuse="size0")
+        square_late(z_3, 3, BLOCKS, 0, 2)
+        square_late(z_3, 3, BLOCKS, 2, PACK)
         log_and_store(1, 0, OUT_TILES)
-        quantize_late(3, 4, z3[:])
+        quantize_late(z_3, 3, BLOCKS)
         mix(1, 3)
-        y = y_banks[2][:].rearrange("p (n e) -> p n e", e=P)
-        nc.vector.tensor_scalar(result[2][:], y, -1.0, None, ALU.mult)
-        nc.vector.tensor_tensor(size[2][:], y, result[2][:], ALU.max)
+        y_2 = y_banks[2][:].rearrange("p (n e) -> p n e", e=P)
+        nc.vector.tensor_scalar(result[2][:], y_2, -1.0, None, ALU.mult)
+        nc.vector.tensor_tensor(size[2][:], y_2, result[2][:], ALU.max)
         magnitude(3, 0, 2)
         log_and_store(3, 0, 2)
         log_and_store(2, 0, OUT_TILES)
-        magnitude(3, 2, 4)
-        log_and_store(3, 2, 4)
+        magnitude(3, 2, OUT_TILES)
+        log_and_store(3, 2, OUT_TILES)

@@ -128,14 +128,14 @@ def tile_list_cloth_edge_strain_kernel(
 
         def round_w1(j, a, copy):
             copy(
-                rounded[j, a][:].rearrange("p (c n i) -> p c i n", n=RUN, i=PACK),
-                raw[j, a][:].rearrange("p i (c n) -> p c i n", n=RUN),
+                rounded[j, a][:].rearrange("p (c n u i) -> p c u n i", n=RUN, u=2, i=2),
+                raw[j, a][:].rearrange("p (u i) (c n) -> p c u n i", n=RUN, i=2),
             )
 
         def round_dealt(a, m0, m1, copy):
             copy(
-                rounded[DEALT, a][:].rearrange("p (t m i) -> p m i t", t=PACK, i=PACK)[:, m0:m1],
-                raw[DEALT, a][:].rearrange("p i (m t) -> p m i t", t=PACK)[:, m0:m1],
+                rounded[DEALT, a][:].rearrange("p (t m u i) -> p m u t i", t=PACK, u=2, i=2)[:, m0:m1],
+                raw[DEALT, a][:].rearrange("p (u i) (m t) -> p m u t i", t=PACK, i=2)[:, m0:m1],
             )
 
         def quantize_w1(j, a):
@@ -230,8 +230,8 @@ def tile_list_cloth_edge_strain_kernel(
 
         def square_late(z, b0, b1, t0, t1):
             nc.scalar.activation(
-                z[:].rearrange("p (c n t) -> p c t n", n=RUN, t=PACK)[:, :, t0:t1],
-                d_late[:, t0:t1, b0 * P : b1 * P].rearrange("p t (c n) -> p c t n", n=RUN),
+                z[:].rearrange("p (c n t) -> p c t n", n=2, t=PACK)[:, :, t0:t1],
+                d_late[:, t0:t1, b0 * P : b1 * P].rearrange("p t (c n) -> p c t n", n=2),
                 ACT.Square,
             )
 

@@ -24,6 +24,7 @@ K_PASSES = K // PASS
 R_PASSES = H // PASS
 QUADS = 4
 BANK = 512
+CUT = 768
 BANKS = 8
 H_SETS = 3
 LANES = 16
@@ -35,7 +36,7 @@ DUOS = PASS // 2
 PARTS = ((0, 2 * P), (2 * P, PASS), (PASS, H))
 DEALT = 2
 BY_BLOCKS = 3
-SCALAR_SHARE = 56
+SCALAR_SHARE = 76
 
 
 def tile_list_cloth_edge_strain_kernel(
@@ -62,10 +63,21 @@ def tile_list_cloth_edge_strain_kernel(
         for j, (c0, c1) in enumerate(PARTS):
             for a in range(K_PASSES):
                 raw[j, a] = held([P, PACK, c1 - c0], F32, "raw%d_%d" % (j, a))
-                if (j, a) not in ((1, 2), (DEALT, 1)):
+                if a == 0 or (j, a) == (DEALT, 2):
                     rounded[j, a] = held([P, PACK * (c1 - c0)], BF16, "rounded%d_%d" % (j, a))
-                w1_codes[j, a] = held([P, c1 - c0], U32, "w1_codes%d_%d" % (j, a))
-                w1_plane[j, a] = held([P, c1 - c0], U8, "w1_plane%d_%d" % (j, a))
+                if a == 0 or j == DEALT:
+                    w1_codes[j, a] = held([P, c1 - c0], U32, "w1_codes%d_%d" % (j, a))
+                    w1_plane[j, a] = held([P, c1 - c0], U8, "w1_plane%d_%d" % (j, a))
+        later = {}
+        for j in range(DEALT):
+            later[j] = held([P, 4 * PASS], BF16, "rounded%d_12" % j)
+            codes = held([P, 4 * P], U32, "w1_codes%d_12" % j)
+            plane = held([P, 4 * P], U8, "w1_plane%d_12" % j)
+            later[j] = (later[j], codes, plane)
+            for a in (1, 2):
+                rounded[j, a] = later[j][0][:, (a - 1) * 2 * PASS : a * 2 * PASS]
+                w1_codes[j, a] = codes[:, (a - 1) * 2 * P : a * 2 * P]
+                w1_plane[j, a] = plane[:, (a - 1) * 2 * P : a * 2 * P]
         h = {c: held([P, S], F32, "h%d" % c) for c in range(2, TILES)}
         minus_one = held([P, E], F32, "minus_one")
         ends = {}
@@ -76,7 +88,7 @@ def tile_list_cloth_edge_strain_kernel(
         result = [held([P, OUT_TILES, P], F32, "result%d" % b) for b in range(BLOCKS)]
         identity = held([P, P], F32, "identity")
         bank = [psum.tile([P, BANK], F32, name="bank%d" % i) for i in range(BANKS)]
-        y_banks = [bank[i] for i in (6, 7, 2, 0, 1)]
+        y_banks = [bank[i] for i in (6, 7, 2, 6, 7)]
 
         nc.gpsimd.memset(tab_plane[:], 0)
         one = held([P, 1], F32, "one")
@@ -143,6 +155,10 @@ def tile_list_cloth_edge_strain_kernel(
                 out=w1_codes[j, a][:].bitcast(FP8X4), scales=w1_plane[j, a][:], in_=rounded[j, a][:]
             )
 
+        def quantize_later(j):
+            both, codes, plane = later[j]
+            nc.vector.quantize_mx(out=codes[:].bitcast(FP8X4), scales=plane[:], in_=both[:])
+
         def h_bank(c, half):
             return bank[2 * (c % H_SETS) + half]
 
@@ -156,6 +172,18 @@ def tile_list_cloth_edge_strain_kernel(
                 lhsT_scale=w1_plane[j, a][:, rows],
                 rhs=v_codes[a][:, cols].bitcast(FP8X4),
                 rhs_scale=v_plane[4 * a : P, cols],
+                start=(a == 0),
+                stop=(a == K_PASSES - 1),
+            )
+
+        def project_first(piece, a):
+            dst, s0, s1 = piece
+            nc.tensor.matmul_mx(
+                out=dst[:, 0 : s1 - s0],
+                lhsT=w1_codes[0, a][:, 0:P].bitcast(FP8X4),
+                lhsT_scale=w1_plane[0, a][:, 0:P],
+                rhs=v_codes[a][:, s0:s1].bitcast(FP8X4),
+                rhs_scale=v_plane[4 * a : P, s0:s1],
                 start=(a == 0),
                 stop=(a == K_PASSES - 1),
             )
@@ -246,7 +274,7 @@ def tile_list_cloth_edge_strain_kernel(
                 return y_banks[b], 0, OUT_TILES - 1
             return y_banks[b + n // 2], n - n % 2, n - n % 2 + 1
 
-        def mix(g, b):
+        def mix(g, b, first=0):
             for n in range(OUT_TILES):
                 dst, n_first, n_last = y_group(b, n)
                 nc.tensor.matmul_mx(
@@ -255,8 +283,8 @@ def tile_list_cloth_edge_strain_kernel(
                     lhsT_scale=w2_plane[:, g, :].bitcast(U8)[:, n * P : (n + 1) * P],
                     rhs=z_codes[g, b].bitcast(FP8X4),
                     rhs_scale=z_plane[g][:, b * P : (b + 1) * P],
-                    start=(g == 0 and n == n_first),
-                    stop=(g == R_PASSES - 1 and n == n_last),
+                    start=(g == first and n == n_first),
+                    stop=(g != first and n == n_last),
                 )
 
         def magnitude(b, n0, n1):
@@ -275,38 +303,39 @@ def tile_list_cloth_edge_strain_kernel(
         nc.vector.tensor_copy(v_plane[:], tab_plane[:].bitcast(U8).indirect(offs_sb[:]))
         for a in range(K_PASSES):
             round_w1(0, a, nc.scalar.copy)
-        for a in range(last_pass):
-            quantize_w1(0, a)
+        quantize_w1(0, 0)
         gather_words(1, 0, S)
-        quantize_w1(0, last_pass)
+        quantize_later(0)
+        pieces = ((bank[0], 0, BANK), (bank[1], BANK, CUT), (bank[6], CUT, S))
         for a in range(last_pass):
-            project_passes((0, 1), (a,))
-        gather_words(last_pass, 0, BANK)
-        gather_words(last_pass, BANK, S)
-        project_passes((0, 1), (last_pass,))
+            for piece in pieces:
+                project_first(piece, a)
+            project_passes((1,), (a,))
+        gather_words(last_pass, 0, CUT)
+        gather_words(last_pass, CUT, S)
+        for piece in pieces:
+            project_first(piece, last_pass)
+        project_passes((1,), (last_pass,))
 
         round_w1(1, 0, nc.scalar.copy)
         h[0] = held([P, S], F32, "h0", reuse="raw1_0")
-        drain(0)
-        quantize_w1(1, 0)
-        h[1] = held([P, S], F32, "h1", reuse="rounded1_0")
-        drain(1)
         round_w1(1, 1, nc.vector.tensor_copy)
+        for (src, s0, s1), copy in zip(pieces, (nc.scalar.copy, nc.scalar.copy, nc.vector.tensor_copy)):
+            copy(h[0][:, s0:s1], src[:, 0 : s1 - s0])
+        quantize_w1(1, 0)
         project_passes((2, 3), (0,))
-        rounded[1, 2] = held([P, PACK * 2 * P], BF16, "rounded1_2", reuse="w1_codes1_0")
         round_w1(1, 2, nc.scalar.copy)
+        h[1] = held([P, S], F32, "h1", reuse="raw1_2")
+        drain(1)
         gather_ends(0, reuse="raw1_1")
-        quantize_w1(1, 1)
-        quantize_w1(1, 2)
+        quantize_later(1)
         project_passes((2, 3), (1, 2))
-        gather_ends(1, reuse="w1_codes1_0")
+        gather_ends(1, reuse=None)
 
-        rounded[DEALT, 1] = held([P, PACK * PASS], BF16, "rounded2_1", reuse="w1_codes1_1")
-        round_dealt(0, 0, P // 2, nc.scalar.copy)
+        rounded[DEALT, 1] = held([P, PACK * PASS], BF16, "rounded2_1")
+        round_dealt(0, 0, P, nc.scalar.copy)
         drain(2)
-        round_dealt(0, P // 2, P, nc.scalar.copy)
-        round_dealt(1, 0, P // 2, nc.scalar.copy)
-        round_dealt(1, P // 2, P, nc.scalar.copy)
+        round_dealt(1, 0, P, nc.scalar.copy)
         round_dealt(2, 0, SCALAR_SHARE, nc.scalar.copy)
         drain(3)
         gather_first_end(2)
@@ -345,45 +374,51 @@ def tile_list_cloth_edge_strain_kernel(
         turn_back(2, BLOCKS, bank[5])
 
         but_last = BY_BLOCKS - 1
-        gather_differences(0, 2, gather_seconds(0, 2, 0, BY_BLOCKS, "seconds_01"))
-        z_01 = held([P, 2 * PASS], BF16, "z_01", reuse="raw2_2")
-        square_late(z_01, 0, 2, 0, PACK)
-        seconds_2 = gather_seconds(2, 3, 0, but_last, "seconds_2")
+        for c in range(TILES - BY_BLOCKS, TILES):
+            second = held([P, 3 * P], F32, "second_of_%d" % c)
+            for b0, b1 in ((0, 2), (2, 3)):
+                gather_second(second[:, b0 * P : b1 * P], c, b0, b1)
+            if c == TILES - 1:
+                z_01 = held([P, 2 * PASS], BF16, "z_01", reuse="raw2_2")
+                square_late(z_01, 0, 2, 0, BY_BLOCKS)
+            for b0, b1 in ((0, 2), (2, 3)):
+                gather_difference(second[:, b0 * P : b1 * P], c, b0, b1)
+        square_late(z_01, 0, 2, BY_BLOCKS, PACK)
         nc.vector.quantize_mx(
             out=early_codes[:].bitcast(FP8X4),
             scales=z_plane[0][:],
             in_=z_cols[:].rearrange("p e u -> p (e u)").bitcast(BF16),
         )
         mix(0, 0)
+        z_2 = held([P, PASS], BF16, "z_2", reuse="z_cols")
+        square_late(z_2, 2, 3, 0, PACK)
         quantize_late(z_01, 0, 2)
         mix(1, 0)
-        mix(0, 1)
-        mix(1, 1)
-        mix(0, 2)
-        seconds_2.extend(gather_seconds(2, 3, but_last, BY_BLOCKS, "second_2_last", reuse="z_cols"))
-        gather_differences(2, 3, seconds_2)
-        z_2 = held([P, PASS], BF16, "z_2")
-        square_late(z_2, 2, 3, 0, PACK)
-        magnitude(0, 0, OUT_TILES)
-        log_and_store(0, 0, OUT_TILES)
-        seconds_3 = gather_seconds(3, BLOCKS, 0, but_last, "seconds_3", reuse="raw2_2")
+        mix(1, 1, first=1)
+        mix(0, 1, first=1)
+        seconds_3 = gather_seconds(3, BLOCKS, 0, BY_BLOCKS, "seconds_3", reuse="raw2_2")
         quantize_late(z_2, 2, 3)
-        mix(1, 2)
-        mix(0, 3)
-        seconds_3.extend(gather_seconds(3, BLOCKS, but_last, BY_BLOCKS, "second_3_last", reuse="z_2"))
+        mix(1, 2, first=1)
+        mix(0, 2, first=1)
         gather_differences(3, BLOCKS, seconds_3)
+        magnitude(0, 0, OUT_TILES)
         magnitude(1, 0, OUT_TILES)
-        z_3 = held([P, PASS], BF16, "z_3", reuse="size0")
-        square_late(z_3, 3, BLOCKS, 0, 2)
-        square_late(z_3, 3, BLOCKS, 2, PACK)
+        mix(0, 3)
+        log_and_store(0, 0, OUT_TILES)
+        magnitude(2, 0, OUT_TILES)
         log_and_store(1, 0, OUT_TILES)
+        log_and_store(2, 0, OUT_TILES)
+        z_3 = held([P, PASS], BF16, "z_3")
+        d_3 = d_late[:, :, 3 * P : E].rearrange("p t (c n) -> p c t n", n=2)
+        nc.vector.tensor_tensor(z_3[:].rearrange("p (c n t) -> p c t n", n=2, t=PACK), d_3, d_3, ALU.mult)
         quantize_late(z_3, 3, BLOCKS)
         mix(1, 3)
-        y_2 = y_banks[2][:].rearrange("p (n e) -> p n e", e=P)
-        nc.vector.tensor_scalar(result[2][:], y_2, -1.0, None, ALU.mult)
-        nc.vector.tensor_tensor(size[2][:], y_2, result[2][:], ALU.max)
-        magnitude(3, 0, 2)
+        halves = ((0, 2), (2, OUT_TILES))
+        y_3 = [y_group(3, n0)[0][:].rearrange("p (n e) -> p n e", e=P)[:, n0:n1, :] for n0, n1 in halves]
+        negated = held([P, OUT_TILES, P], F32, "negated")
+        for y, (n0, n1) in zip(y_3, halves):
+            nc.vector.tensor_scalar(negated[:, n0:n1, :], y, -1.0, None, ALU.mult)
+        for y, (n0, n1) in zip(y_3, halves):
+            nc.vector.tensor_tensor(size[3][:, n0:n1, :], y, negated[:, n0:n1, :], ALU.max)
         log_and_store(3, 0, 2)
-        log_and_store(2, 0, OUT_TILES)
-        magnitude(3, 2, OUT_TILES)
         log_and_store(3, 2, OUT_TILES)

@@ -29,6 +29,7 @@ BANKS = 8
 H_SETS = 3
 LANES = 16
 RUN = 4
+LINE = 2
 TILES = H // P
 BLOCKS = E // P
 OUT_TILES = N // P
@@ -36,7 +37,8 @@ DUOS = PASS // 2
 PARTS = ((0, 2 * P), (2 * P, PASS), (PASS, H))
 DEALT = 2
 BY_BLOCKS = 3
-SCALAR_SHARE = 76
+LAST = BLOCKS - 1
+SCALAR_SHARE = 56
 
 
 def tile_list_cloth_edge_strain_kernel(
@@ -59,25 +61,24 @@ def tile_list_cloth_edge_strain_kernel(
         table = [held([P, T], I32, "table%d" % a) for a in range(K_PASSES)]
         v_codes = [held([P, S], U32, "v_codes%d" % a) for a in range(K_PASSES)]
         v_plane = held([P, S], U8, "v_plane")
-        raw, rounded, w1_codes, w1_plane = {}, {}, {}, {}
+        raw, rounded, w1_codes, w1_plane, joint = {}, {}, {}, {}, {}
         for j, (c0, c1) in enumerate(PARTS):
             for a in range(K_PASSES):
                 raw[j, a] = held([P, PACK, c1 - c0], F32, "raw%d_%d" % (j, a))
-                if a == 0 or (j, a) == (DEALT, 2):
-                    rounded[j, a] = held([P, PACK * (c1 - c0)], BF16, "rounded%d_%d" % (j, a))
                 if a == 0 or j == DEALT:
+                    rounded[j, a] = held([P, PACK * (c1 - c0)], BF16, "rounded%d_%d" % (j, a))
                     w1_codes[j, a] = held([P, c1 - c0], U32, "w1_codes%d_%d" % (j, a))
                     w1_plane[j, a] = held([P, c1 - c0], U8, "w1_plane%d_%d" % (j, a))
-        later = {}
         for j in range(DEALT):
-            later[j] = held([P, 4 * PASS], BF16, "rounded%d_12" % j)
-            codes = held([P, 4 * P], U32, "w1_codes%d_12" % j)
-            plane = held([P, 4 * P], U8, "w1_plane%d_12" % j)
-            later[j] = (later[j], codes, plane)
+            width = PARTS[j][1] - PARTS[j][0]
+            both = held([P, 2 * PACK * width], BF16, "rounded%d_12" % j)
+            codes = held([P, 2 * width], U32, "w1_codes%d_12" % j)
+            plane = held([P, 2 * width], U8, "w1_plane%d_12" % j)
+            joint[j] = (both, codes, plane)
             for a in (1, 2):
-                rounded[j, a] = later[j][0][:, (a - 1) * 2 * PASS : a * 2 * PASS]
-                w1_codes[j, a] = codes[:, (a - 1) * 2 * P : a * 2 * P]
-                w1_plane[j, a] = plane[:, (a - 1) * 2 * P : a * 2 * P]
+                rounded[j, a] = both[:, (a - 1) * PACK * width : a * PACK * width]
+                w1_codes[j, a] = codes[:, (a - 1) * width : a * width]
+                w1_plane[j, a] = plane[:, (a - 1) * width : a * width]
         h = {c: held([P, S], F32, "h%d" % c) for c in range(2, TILES)}
         minus_one = held([P, E], F32, "minus_one")
         ends = {}
@@ -155,8 +156,8 @@ def tile_list_cloth_edge_strain_kernel(
                 out=w1_codes[j, a][:].bitcast(FP8X4), scales=w1_plane[j, a][:], in_=rounded[j, a][:]
             )
 
-        def quantize_later(j):
-            both, codes, plane = later[j]
+        def quantize_joint(j):
+            both, codes, plane = joint[j]
             nc.vector.quantize_mx(out=codes[:].bitcast(FP8X4), scales=plane[:], in_=both[:])
 
         def h_bank(c, half):
@@ -205,7 +206,7 @@ def tile_list_cloth_edge_strain_kernel(
         def gather_negated_end(c):
             nc.vector.tensor_tensor(ends[c][:, E : 2 * E], h[c][:].indirect(pos2_sb[:]), minus_one[:], ALU.mult)
 
-        def gather_ends(c, reuse):
+        def gather_ends(c, reuse=None):
             gather_first_end(c, reuse)
             gather_negated_end(c)
 
@@ -246,20 +247,10 @@ def tile_list_cloth_edge_strain_kernel(
             window = h[c][:].indirect(pos1_sb[:, entries(b0 * P, b1 * P)])
             nc.vector.tensor_tensor(d_late[:, c - PACK, b0 * P : b1 * P], window, second, ALU.subtract)
 
-        def gather_seconds(b0, b1, i0, i1, name, reuse=None):
-            rows = held([P, i1 - i0, (b1 - b0) * P], F32, name, reuse)
-            for i in range(i0, i1):
-                gather_second(rows[:, i - i0, :], TILES - BY_BLOCKS + i, b0, b1)
-            return [rows[:, i - i0, :] for i in range(i0, i1)]
-
-        def gather_differences(b0, b1, seconds):
-            for i, second in enumerate(seconds):
-                gather_difference(second, TILES - BY_BLOCKS + i, b0, b1)
-
         def square_late(z, b0, b1, t0, t1):
             nc.scalar.activation(
-                z[:].rearrange("p (c n t) -> p c t n", n=2, t=PACK)[:, :, t0:t1],
-                d_late[:, t0:t1, b0 * P : b1 * P].rearrange("p t (c n) -> p c t n", n=2),
+                z[:].rearrange("p (c n t) -> p c t n", n=LINE, t=PACK)[:, :, t0:t1],
+                d_late[:, t0:t1, b0 * P : b1 * P].rearrange("p t (c n) -> p c t n", n=LINE),
                 ACT.Square,
             )
 
@@ -270,7 +261,7 @@ def tile_list_cloth_edge_strain_kernel(
             nc.vector.quantize_mx(out=codes[:].bitcast(FP8X4), scales=z_plane[1][:, b0 * P : b1 * P], in_=z[:])
 
         def y_group(b, n):
-            if b < BLOCKS - 1:
+            if b < LAST:
                 return y_banks[b], 0, OUT_TILES - 1
             return y_banks[b + n // 2], n - n % 2, n - n % 2 + 1
 
@@ -287,9 +278,9 @@ def tile_list_cloth_edge_strain_kernel(
                     stop=(g != first and n == n_last),
                 )
 
-        def magnitude(b, n0, n1):
-            y = y_group(b, n0)[0][:].rearrange("p (n e) -> p n e", e=P)
-            nc.scalar.activation(size[b][:, n0:n1, :], y[:, n0:n1, :], ACT.Abs, bias=zero[:])
+        def magnitude(b):
+            y = y_banks[b][:].rearrange("p (n e) -> p n e", e=P)
+            nc.scalar.activation(size[b][:], y, ACT.Abs, bias=zero[:])
 
         def log_and_store(b, n0, n1):
             nc.scalar.activation(result[b][:, n0:n1, :], size[b][:, n0:n1, :], ACT.Ln, bias=1.0)
@@ -305,7 +296,7 @@ def tile_list_cloth_edge_strain_kernel(
             round_w1(0, a, nc.scalar.copy)
         quantize_w1(0, 0)
         gather_words(1, 0, S)
-        quantize_later(0)
+        quantize_joint(0)
         pieces = ((bank[0], 0, BANK), (bank[1], BANK, CUT), (bank[6], CUT, S))
         for a in range(last_pass):
             for piece in pieces:
@@ -328,11 +319,10 @@ def tile_list_cloth_edge_strain_kernel(
         h[1] = held([P, S], F32, "h1", reuse="raw1_2")
         drain(1)
         gather_ends(0, reuse="raw1_1")
-        quantize_later(1)
+        quantize_joint(1)
         project_passes((2, 3), (1, 2))
-        gather_ends(1, reuse=None)
+        gather_ends(1)
 
-        rounded[DEALT, 1] = held([P, PACK * PASS], BF16, "rounded2_1")
         round_dealt(0, 0, P, nc.scalar.copy)
         drain(2)
         round_dealt(1, 0, P, nc.scalar.copy)
@@ -351,7 +341,7 @@ def tile_list_cloth_edge_strain_kernel(
             for a in (1, 2):
                 project_passes((c,), (a,))
         project_passes((6,), range(K_PASSES))
-        gather_ends(3, reuse="rounded2_2")
+        gather_ends(3)
 
         z_rows = held([P, BLOCKS, DUOS], F32, "z_rows", reuse="raw2_2")
         square_early(0, bank[6])
@@ -373,17 +363,18 @@ def tile_list_cloth_edge_strain_kernel(
         turn_back(0, 2, bank[4])
         turn_back(2, BLOCKS, bank[5])
 
-        but_last = BY_BLOCKS - 1
-        for c in range(TILES - BY_BLOCKS, TILES):
-            second = held([P, 3 * P], F32, "second_of_%d" % c)
-            for b0, b1 in ((0, 2), (2, 3)):
+        late_tiles = range(TILES - BY_BLOCKS, TILES)
+        for c in late_tiles:
+            second = held([P, LAST * P], F32, "second_of_%d" % c)
+            cuts = ((0, LAST),) if c == late_tiles[0] else ((0, 2), (2, LAST))
+            for b0, b1 in cuts:
                 gather_second(second[:, b0 * P : b1 * P], c, b0, b1)
-            if c == TILES - 1:
+            if c == late_tiles[-1]:
                 z_01 = held([P, 2 * PASS], BF16, "z_01", reuse="raw2_2")
-                square_late(z_01, 0, 2, 0, BY_BLOCKS)
-            for b0, b1 in ((0, 2), (2, 3)):
+                square_late(z_01, 0, 2, 0, PACK - 1)
+            for b0, b1 in cuts:
                 gather_difference(second[:, b0 * P : b1 * P], c, b0, b1)
-        square_late(z_01, 0, 2, BY_BLOCKS, PACK)
+        square_late(z_01, 0, 2, PACK - 1, PACK)
         nc.vector.quantize_mx(
             out=early_codes[:].bitcast(FP8X4),
             scales=z_plane[0][:],
@@ -391,34 +382,38 @@ def tile_list_cloth_edge_strain_kernel(
         )
         mix(0, 0)
         z_2 = held([P, PASS], BF16, "z_2", reuse="z_cols")
-        square_late(z_2, 2, 3, 0, PACK)
+        square_late(z_2, 2, LAST, 0, PACK)
         quantize_late(z_01, 0, 2)
         mix(1, 0)
         mix(1, 1, first=1)
         mix(0, 1, first=1)
-        seconds_3 = gather_seconds(3, BLOCKS, 0, BY_BLOCKS, "seconds_3", reuse="raw2_2")
-        quantize_late(z_2, 2, 3)
+        last_seconds = held([P, BY_BLOCKS, P], F32, "last_seconds", reuse="raw2_2")
+        for i, c in enumerate(late_tiles):
+            gather_second(last_seconds[:, i, :], c, LAST, BLOCKS)
+        quantize_late(z_2, 2, LAST)
         mix(1, 2, first=1)
         mix(0, 2, first=1)
-        gather_differences(3, BLOCKS, seconds_3)
-        magnitude(0, 0, OUT_TILES)
-        magnitude(1, 0, OUT_TILES)
-        mix(0, 3)
+        for i, c in enumerate(late_tiles):
+            gather_difference(last_seconds[:, i, :], c, LAST, BLOCKS)
+        magnitude(0)
+        magnitude(1)
+        mix(0, LAST)
         log_and_store(0, 0, OUT_TILES)
-        magnitude(2, 0, OUT_TILES)
+        magnitude(2)
         log_and_store(1, 0, OUT_TILES)
         log_and_store(2, 0, OUT_TILES)
+
         z_3 = held([P, PASS], BF16, "z_3")
-        d_3 = d_late[:, :, 3 * P : E].rearrange("p t (c n) -> p c t n", n=2)
-        nc.vector.tensor_tensor(z_3[:].rearrange("p (c n t) -> p c t n", n=2, t=PACK), d_3, d_3, ALU.mult)
-        quantize_late(z_3, 3, BLOCKS)
-        mix(1, 3)
-        halves = ((0, 2), (2, OUT_TILES))
-        y_3 = [y_group(3, n0)[0][:].rearrange("p (n e) -> p n e", e=P)[:, n0:n1, :] for n0, n1 in halves]
+        d_3 = d_late[:, :, LAST * P : E].rearrange("p t (c n) -> p c t n", n=LINE)
+        nc.vector.tensor_tensor(z_3[:].rearrange("p (c n t) -> p c t n", n=LINE, t=PACK), d_3, d_3, ALU.mult)
+        quantize_late(z_3, LAST, BLOCKS)
+        mix(1, LAST)
+        halves = ((0, OUT_TILES // 2), (OUT_TILES // 2, OUT_TILES))
+        y_3 = [y_group(LAST, n0)[0][:].rearrange("p (n e) -> p n e", e=P)[:, n0:n1, :] for n0, n1 in halves]
         negated = held([P, OUT_TILES, P], F32, "negated")
         for y, (n0, n1) in zip(y_3, halves):
             nc.vector.tensor_scalar(negated[:, n0:n1, :], y, -1.0, None, ALU.mult)
         for y, (n0, n1) in zip(y_3, halves):
-            nc.vector.tensor_tensor(size[3][:, n0:n1, :], y, negated[:, n0:n1, :], ALU.max)
-        log_and_store(3, 0, 2)
-        log_and_store(3, 2, OUT_TILES)
+            nc.vector.tensor_tensor(size[LAST][:, n0:n1, :], y, negated[:, n0:n1, :], ALU.max)
+        for n0, n1 in halves:
+            log_and_store(LAST, n0, n1)

@@ -35,6 +35,7 @@ BLOCKS = E // P
 OUT_TILES = N // P
 DUOS = PASS // 2
 PARTS = ((0, 2 * P), (2 * P, PASS), (PASS, H))
+JOINT = 1
 DEALT = 2
 BY_BLOCKS = 3
 LAST = BLOCKS - 1
@@ -59,26 +60,25 @@ def tile_list_cloth_edge_strain_kernel(
         w2_plane = held([P, R_PASSES, N // 4], I32, "w2_plane")
         w2_codes = held([P, R_PASSES, N // 2], I32, "w2_codes")
         table = [held([P, T], I32, "table%d" % a) for a in range(K_PASSES)]
-        v_codes = [held([P, S], U32, "v_codes%d" % a) for a in range(K_PASSES)]
+        last_pass = K_PASSES - 1
+        v_codes = [held([P, CUT if a == last_pass else S], U32, "v_codes%d" % a) for a in range(K_PASSES)]
         v_plane = held([P, S], U8, "v_plane")
-        raw, rounded, w1_codes, w1_plane, joint = {}, {}, {}, {}, {}
+        raw, rounded, w1_codes, w1_plane = {}, {}, {}, {}
         for j, (c0, c1) in enumerate(PARTS):
             for a in range(K_PASSES):
                 raw[j, a] = held([P, PACK, c1 - c0], F32, "raw%d_%d" % (j, a))
-                if a == 0 or j == DEALT:
+                if a == 0 or j != JOINT:
                     rounded[j, a] = held([P, PACK * (c1 - c0)], BF16, "rounded%d_%d" % (j, a))
                     w1_codes[j, a] = held([P, c1 - c0], U32, "w1_codes%d_%d" % (j, a))
                     w1_plane[j, a] = held([P, c1 - c0], U8, "w1_plane%d_%d" % (j, a))
-        for j in range(DEALT):
-            width = PARTS[j][1] - PARTS[j][0]
-            both = held([P, 2 * PACK * width], BF16, "rounded%d_12" % j)
-            codes = held([P, 2 * width], U32, "w1_codes%d_12" % j)
-            plane = held([P, 2 * width], U8, "w1_plane%d_12" % j)
-            joint[j] = (both, codes, plane)
-            for a in (1, 2):
-                rounded[j, a] = both[:, (a - 1) * PACK * width : a * PACK * width]
-                w1_codes[j, a] = codes[:, (a - 1) * width : a * width]
-                w1_plane[j, a] = plane[:, (a - 1) * width : a * width]
+        width = PARTS[JOINT][1] - PARTS[JOINT][0]
+        joint_rounded = held([P, 2 * PACK * width], BF16, "joint_rounded")
+        joint_codes = held([P, 2 * width], U32, "joint_codes")
+        joint_plane = held([P, 2 * width], U8, "joint_plane")
+        for a in (1, 2):
+            rounded[JOINT, a] = joint_rounded[:, (a - 1) * PACK * width : a * PACK * width]
+            w1_codes[JOINT, a] = joint_codes[:, (a - 1) * width : a * width]
+            w1_plane[JOINT, a] = joint_plane[:, (a - 1) * width : a * width]
         h = {c: held([P, S], F32, "h%d" % c) for c in range(2, TILES)}
         minus_one = held([P, E], F32, "minus_one")
         ends = {}
@@ -118,8 +118,8 @@ def tile_list_cloth_edge_strain_kernel(
                 in_=tab_scales[:, 4 * q : 4 * q + 4, :].bitcast(I32),
             )
         for a in range(1, K_PASSES):
-            load_w1(0, a)
             load_table(a)
+            load_w1(0, a)
         nc.sync.dma_start(pos1_sb[:], pos1)
         nc.sync.dma_start(pos2_sb[:], pos2)
         for j in range(1, len(PARTS)):
@@ -135,9 +135,14 @@ def tile_list_cloth_edge_strain_kernel(
         def entries(e0, e1):
             return slice(e0 // LANES, e1 // LANES)
 
+        def words(a, s0, s1):
+            if a == last_pass and s0 >= CUT:
+                return v_rest[:, s0 - CUT : s1 - CUT]
+            return v_codes[a][:, s0:s1]
+
         def gather_words(a, s0, s1):
             window = table[a][:].bitcast(U32)
-            nc.vector.tensor_copy(v_codes[a][:, s0:s1], window.indirect(offs_sb[:, entries(s0, s1)]))
+            nc.vector.tensor_copy(words(a, s0, s1), window.indirect(offs_sb[:, entries(s0, s1)]))
 
         def round_w1(j, a, copy):
             copy(
@@ -156,44 +161,30 @@ def tile_list_cloth_edge_strain_kernel(
                 out=w1_codes[j, a][:].bitcast(FP8X4), scales=w1_plane[j, a][:], in_=rounded[j, a][:]
             )
 
-        def quantize_joint(j):
-            both, codes, plane = joint[j]
-            nc.vector.quantize_mx(out=codes[:].bitcast(FP8X4), scales=plane[:], in_=both[:])
-
         def h_bank(c, half):
             return bank[2 * (c % H_SETS) + half]
 
-        def project(c, half, a):
+        def project(c, dst, s0, s1, a, stop):
             j = min(c // 2, DEALT)
             rows = slice((c - 2 * j) * P, (c - 2 * j + 1) * P)
-            cols = slice(half * BANK, (half + 1) * BANK)
             nc.tensor.matmul_mx(
-                out=h_bank(c, half)[:],
+                out=dst,
                 lhsT=w1_codes[j, a][:, rows].bitcast(FP8X4),
                 lhsT_scale=w1_plane[j, a][:, rows],
-                rhs=v_codes[a][:, cols].bitcast(FP8X4),
-                rhs_scale=v_plane[4 * a : P, cols],
-                start=(a == 0),
-                stop=(a == K_PASSES - 1),
-            )
-
-        def project_first(piece, a):
-            dst, s0, s1 = piece
-            nc.tensor.matmul_mx(
-                out=dst[:, 0 : s1 - s0],
-                lhsT=w1_codes[0, a][:, 0:P].bitcast(FP8X4),
-                lhsT_scale=w1_plane[0, a][:, 0:P],
-                rhs=v_codes[a][:, s0:s1].bitcast(FP8X4),
+                rhs=words(a, s0, s1).bitcast(FP8X4),
                 rhs_scale=v_plane[4 * a : P, s0:s1],
                 start=(a == 0),
-                stop=(a == K_PASSES - 1),
+                stop=stop,
             )
 
         def project_passes(tiles, passes):
             for c in tiles:
                 for half in range(2):
                     for a in passes:
-                        project(c, half, a)
+                        cut = (BANK, CUT, S) if half == 1 and a == last_pass else (half * BANK, (half + 1) * BANK)
+                        for s0, s1 in zip(cut, cut[1:]):
+                            dst = h_bank(c, half)[:, s0 - half * BANK : s1 - half * BANK]
+                            project(c, dst, s0, s1, a, a == last_pass and s1 == cut[-1])
 
         def drain(c):
             nc.scalar.copy(h[c][:, 0:BANK], h_bank(c, 0)[:])
@@ -289,23 +280,24 @@ def tile_list_cloth_edge_strain_kernel(
                 in_=result[b][:, n0:n1, :],
             )
 
-        last_pass = K_PASSES - 1
         gather_words(0, 0, S)
         nc.vector.tensor_copy(v_plane[:], tab_plane[:].bitcast(U8).indirect(offs_sb[:]))
         for a in range(K_PASSES):
             round_w1(0, a, nc.scalar.copy)
+        pieces = ((bank[0], 0, BANK), (bank[1], BANK, CUT), (bank[6], CUT, S))
         quantize_w1(0, 0)
         gather_words(1, 0, S)
-        quantize_joint(0)
-        pieces = ((bank[0], 0, BANK), (bank[1], BANK, CUT), (bank[6], CUT, S))
+        quantize_w1(0, 1)
         for a in range(last_pass):
-            for piece in pieces:
-                project_first(piece, a)
+            for dst, s0, s1 in pieces:
+                project(0, dst[:, 0 : s1 - s0], s0, s1, a, False)
             project_passes((1,), (a,))
         gather_words(last_pass, 0, CUT)
+        quantize_w1(0, last_pass)
+        v_rest = held([P, S - CUT], U32, "v_rest", reuse="raw0_2")
         gather_words(last_pass, CUT, S)
-        for piece in pieces:
-            project_first(piece, last_pass)
+        for dst, s0, s1 in pieces:
+            project(0, dst[:, 0 : s1 - s0], s0, s1, last_pass, True)
         project_passes((1,), (last_pass,))
 
         round_w1(1, 0, nc.scalar.copy)
@@ -319,7 +311,7 @@ def tile_list_cloth_edge_strain_kernel(
         h[1] = held([P, S], F32, "h1", reuse="raw1_2")
         drain(1)
         gather_ends(0, reuse="raw1_1")
-        quantize_joint(1)
+        nc.vector.quantize_mx(out=joint_codes[:].bitcast(FP8X4), scales=joint_plane[:], in_=joint_rounded[:])
         project_passes((2, 3), (1, 2))
         gather_ends(1)
 

@@ -68,7 +68,8 @@ def tile_list_cloth_edge_strain_kernel(
             for a in range(K_PASSES):
                 raw[j, a] = held([P, PACK, c1 - c0], F32, "raw%d_%d" % (j, a))
                 if a == 0 or j != JOINT:
-                    rounded[j, a] = held([P, PACK * (c1 - c0)], BF16, "rounded%d_%d" % (j, a))
+                    if (j, a) != (0, 1):
+                        rounded[j, a] = held([P, PACK * (c1 - c0)], BF16, "rounded%d_%d" % (j, a))
                     w1_codes[j, a] = held([P, c1 - c0], U32, "w1_codes%d_%d" % (j, a))
                     w1_plane[j, a] = held([P, c1 - c0], U8, "w1_plane%d_%d" % (j, a))
         width = PARTS[JOINT][1] - PARTS[JOINT][0]
@@ -148,6 +149,16 @@ def tile_list_cloth_edge_strain_kernel(
             copy(
                 rounded[j, a][:].rearrange("p (c n u i) -> p c u n i", n=RUN, u=2, i=2),
                 raw[j, a][:].rearrange("p (u i) (c n) -> p c u n i", n=RUN, i=2),
+            )
+
+        def round_on_gpsimd(j, a):
+            nc.gpsimd.tensor_scalar(
+                rounded[j, a][:].rearrange("p (c i) -> p c i", i=PACK),
+                raw[j, a][:].rearrange("p i c -> p c i"),
+                1.0,
+                0.0,
+                ALU.mult,
+                ALU.add,
             )
 
         def round_dealt(a, m0, m1, copy):
@@ -282,10 +293,12 @@ def tile_list_cloth_edge_strain_kernel(
 
         gather_words(0, 0, S)
         nc.vector.tensor_copy(v_plane[:], tab_plane[:].bitcast(U8).indirect(offs_sb[:]))
-        for a in range(K_PASSES):
-            round_w1(0, a, nc.scalar.copy)
+        round_on_gpsimd(0, 0)
+        round_w1(0, last_pass, nc.scalar.copy)
         pieces = ((bank[0], 0, BANK), (bank[1], BANK, CUT), (bank[6], CUT, S))
         quantize_w1(0, 0)
+        rounded[0, 1] = held([P, PACK * PARTS[0][1]], BF16, "rounded_second", reuse="rounded0_0")
+        round_on_gpsimd(0, 1)
         gather_words(1, 0, S)
         quantize_w1(0, 1)
         for a in range(last_pass):

@@ -37,9 +37,9 @@ DUOS = PASS // 2
 PARTS = ((0, 2 * P), (2 * P, PASS), (PASS, H))
 JOINT = 1
 DEALT = 2
+WIDE = 3
 BY_BLOCKS = 3
 LAST = BLOCKS - 1
-SCALAR_SHARE = 56
 
 
 def tile_list_cloth_edge_strain_kernel(
@@ -63,26 +63,31 @@ def tile_list_cloth_edge_strain_kernel(
         last_pass = K_PASSES - 1
         v_codes = [held([P, CUT if a == last_pass else S], U32, "v_codes%d" % a) for a in range(K_PASSES)]
         v_plane = held([P, S], U8, "v_plane")
+        wide = [held([P, 2 * S], F32, "wide%d" % c) for c in range(WIDE)]
+        lodged = {(0, 0): (0, 1), (0, 1): (1, 1), (1, 0): (0, 0), (1, 1): (1, 0)}
         raw, rounded, w1_codes, w1_plane = {}, {}, {}, {}
         for j, (c0, c1) in enumerate(PARTS):
             for a in range(K_PASSES):
-                raw[j, a] = held([P, PACK, c1 - c0], F32, "raw%d_%d" % (j, a))
+                if (j, a) in lodged:
+                    c, half = lodged[j, a]
+                    raw[j, a] = wide[c][:, half * S : (half + 1) * S].rearrange("p (i c) -> p i c", i=PACK)
+                else:
+                    raw[j, a] = held([P, PACK, c1 - c0], F32, "raw%d_%d" % (j, a))
                 if a == 0 or j != JOINT:
-                    if (j, a) != (0, 1):
+                    if j != DEALT:
                         rounded[j, a] = held([P, PACK * (c1 - c0)], BF16, "rounded%d_%d" % (j, a))
                     w1_codes[j, a] = held([P, c1 - c0], U32, "w1_codes%d_%d" % (j, a))
                     w1_plane[j, a] = held([P, c1 - c0], U8, "w1_plane%d_%d" % (j, a))
         width = PARTS[JOINT][1] - PARTS[JOINT][0]
-        joint_rounded = held([P, 2 * PACK * width], BF16, "joint_rounded")
         joint_codes = held([P, 2 * width], U32, "joint_codes")
         joint_plane = held([P, 2 * width], U8, "joint_plane")
         for a in (1, 2):
-            rounded[JOINT, a] = joint_rounded[:, (a - 1) * PACK * width : a * PACK * width]
             w1_codes[JOINT, a] = joint_codes[:, (a - 1) * width : a * width]
             w1_plane[JOINT, a] = joint_plane[:, (a - 1) * width : a * width]
-        h = {c: held([P, S], F32, "h%d" % c) for c in range(2, TILES)}
-        minus_one = held([P, E], F32, "minus_one")
-        ends = {}
+        h = {c: held([P, S], F32, "h%d" % c) if c >= WIDE else wide[c] for c in range(TILES)}
+        first_end = {c: wide[2][:, S + c * E : S + (c + 1) * E] for c in (0, 1)}
+        first_end[2] = held([P, E], F32, "first_end2")[:]
+        negated_end = {1: held([P, E], F32, "negated_end1")[:]}
         early_codes = held([P, E], U32, "early_codes")
         z_codes = {(0, b): early_codes[:, b * P : (b + 1) * P] for b in range(BLOCKS)}
         z_plane = [held([P, E], U8, "z_plane%d" % g) for g in range(R_PASSES)]
@@ -98,6 +103,7 @@ def tile_list_cloth_edge_strain_kernel(
         nc.vector.memset(one[:], 1.0)
         nc.scalar.activation(zero[:], one[:], ACT.Ln)
         nc.vector.memset(w2_plane[:], 0)
+        minus_one = held([P, E], F32, "minus_one")
         nc.vector.memset(minus_one[:], -1.0)
         make_identity(nc, identity[:])
 
@@ -151,20 +157,19 @@ def tile_list_cloth_edge_strain_kernel(
                 raw[j, a][:].rearrange("p (u i) (c n) -> p c u n i", n=RUN, i=2),
             )
 
-        def round_on_gpsimd(j, a):
-            nc.gpsimd.tensor_scalar(
-                rounded[j, a][:].rearrange("p (c i) -> p c i", i=PACK),
-                raw[j, a][:].rearrange("p i c -> p c i"),
-                1.0,
-                0.0,
-                ALU.mult,
-                ALU.add,
+        def round_on_gpsimd(dst, src):
+            nc.gpsimd.tensor_scalar(dst, src, 1.0, 0.0, ALU.mult, ALU.add)
+
+        def round_dealt_on_gpsimd(a, t0, t1):
+            round_on_gpsimd(
+                rounded[DEALT, a][:].rearrange("p (t m i) -> p m t i", t=PACK, i=PACK)[:, :, t0:t1],
+                raw[DEALT, a][:].rearrange("p i (m t) -> p m t i", t=PACK)[:, :, t0:t1],
             )
 
-        def round_dealt(a, m0, m1, copy):
+        def round_dealt(a, t0, t1, copy):
             copy(
-                rounded[DEALT, a][:].rearrange("p (t m u i) -> p m u t i", t=PACK, u=2, i=2)[:, m0:m1],
-                raw[DEALT, a][:].rearrange("p (u i) (m t) -> p m u t i", t=PACK, i=2)[:, m0:m1],
+                rounded[DEALT, a][:].rearrange("p (t m u i) -> p m u t i", t=PACK, u=2, i=2)[:, :, :, t0:t1],
+                raw[DEALT, a][:].rearrange("p (u i) (m t) -> p m u t i", t=PACK, i=2)[:, :, :, t0:t1],
             )
 
         def quantize_w1(j, a):
@@ -201,23 +206,22 @@ def tile_list_cloth_edge_strain_kernel(
             nc.scalar.copy(h[c][:, 0:BANK], h_bank(c, 0)[:])
             nc.scalar.copy(h[c][:, BANK:S], h_bank(c, 1)[:])
 
-        def gather_first_end(c, reuse=None):
-            ends[c] = held([P, 2 * E], F32, "ends%d" % c, reuse)
-            nc.vector.tensor_copy(ends[c][:, 0:E], h[c][:].indirect(pos1_sb[:]))
+        def gather_first_end(c):
+            nc.vector.tensor_copy(first_end[c], h[c][:].indirect(pos1_sb[:]))
 
         def gather_negated_end(c):
-            nc.vector.tensor_tensor(ends[c][:, E : 2 * E], h[c][:].indirect(pos2_sb[:]), minus_one[:], ALU.mult)
-
-        def gather_ends(c, reuse=None):
-            gather_first_end(c, reuse)
-            gather_negated_end(c)
+            window = h[c][:].indirect(pos2_sb[:])
+            if c < WIDE:
+                nc.vector.tensor_scalar(negated_end[c], window, -1.0, 0.0, ALU.mult, ALU.add)
+            else:
+                nc.vector.tensor_tensor(negated_end[c], window, minus_one[:], ALU.mult)
 
         def turn(c, dst):
             for b in range(BLOCKS):
                 for i in range(2):
                     nc.tensor.matmul(
                         dst[:, b * P : (b + 1) * P],
-                        lhsT=ends[c][:, i * E + b * P : i * E + (b + 1) * P],
+                        lhsT=(first_end, negated_end)[i][c][:, b * P : (b + 1) * P],
                         rhs=identity[:],
                         start=(i == 0),
                         stop=(i == 1),
@@ -293,12 +297,10 @@ def tile_list_cloth_edge_strain_kernel(
 
         gather_words(0, 0, S)
         nc.vector.tensor_copy(v_plane[:], tab_plane[:].bitcast(U8).indirect(offs_sb[:]))
-        round_on_gpsimd(0, 0)
-        round_w1(0, last_pass, nc.scalar.copy)
+        for a in range(K_PASSES):
+            round_w1(0, a, nc.scalar.copy)
         pieces = ((bank[0], 0, BANK), (bank[1], BANK, CUT), (bank[6], CUT, S))
         quantize_w1(0, 0)
-        rounded[0, 1] = held([P, PACK * PARTS[0][1]], BF16, "rounded_second", reuse="rounded0_0")
-        round_on_gpsimd(0, 1)
         gather_words(1, 0, S)
         quantize_w1(0, 1)
         for a in range(last_pass):
@@ -314,31 +316,45 @@ def tile_list_cloth_edge_strain_kernel(
         project_passes((1,), (last_pass,))
 
         round_w1(1, 0, nc.scalar.copy)
-        h[0] = held([P, S], F32, "h0", reuse="raw1_0")
-        round_w1(1, 1, nc.vector.tensor_copy)
+        quantize_w1(1, 0)
         for (src, s0, s1), copy in zip(pieces, (nc.scalar.copy, nc.scalar.copy, nc.vector.tensor_copy)):
             copy(h[0][:, s0:s1], src[:, 0 : s1 - s0])
-        quantize_w1(1, 0)
         project_passes((2, 3), (0,))
+        joint_rounded = held([P, 2 * PACK * width], BF16, "joint_rounded", reuse="rounded1_0")
+        for a in (1, 2):
+            rounded[JOINT, a] = joint_rounded[:, (a - 1) * PACK * width : a * PACK * width]
+        round_on_gpsimd(
+            rounded[JOINT, 1].rearrange("p (c i) -> p c i", i=PACK), raw[JOINT, 1][:].rearrange("p i c -> p c i")
+        )
         round_w1(1, 2, nc.scalar.copy)
-        h[1] = held([P, S], F32, "h1", reuse="raw1_2")
         drain(1)
-        gather_ends(0, reuse="raw1_1")
+        gather_first_end(0)
         nc.vector.quantize_mx(out=joint_codes[:].bitcast(FP8X4), scales=joint_plane[:], in_=joint_rounded[:])
+        negated_end[0] = held([P, E], F32, "negated_end0", reuse="raw1_2")[:]
+        gather_negated_end(0)
         project_passes((2, 3), (1, 2))
-        gather_ends(1)
+        gather_first_end(1)
+        gather_negated_end(1)
 
-        round_dealt(0, 0, P, nc.scalar.copy)
+        rounded[DEALT, 0] = held([P, PACK * PASS], BF16, "rounded2_0", reuse="rounded1_0")
+        round_dealt_on_gpsimd(0, 2, PACK)
+        round_dealt(0, 0, 2, nc.scalar.copy)
         drain(2)
-        round_dealt(1, 0, P, nc.scalar.copy)
-        round_dealt(2, 0, SCALAR_SHARE, nc.scalar.copy)
-        drain(3)
-        gather_first_end(2)
+        rounded[DEALT, 1] = held([P, PACK * PASS], BF16, "rounded2_1")
+        round_dealt_on_gpsimd(1, 2, PACK)
+        round_dealt(1, 0, 2, nc.scalar.copy)
         quantize_w1(DEALT, 0)
-        gather_negated_end(2)
-        round_dealt(2, SCALAR_SHARE, P, nc.vector.tensor_copy)
+        drain(3)
+        rounded[DEALT, 2] = held([P, PACK * PASS], BF16, "rounded2_2", reuse="rounded1_0")
+        round_dealt_on_gpsimd(2, 2, PACK)
+        round_dealt(2, 0, 2, nc.scalar.copy)
+        gather_first_end(2)
         quantize_w1(DEALT, 1)
+        negated_end[2] = held([P, E], F32, "negated_end2", reuse="raw2_1")[:]
+        gather_negated_end(2)
         quantize_w1(DEALT, 2)
+        ends3 = held([P, 2 * E], F32, "ends3", reuse="rounded1_0")
+        first_end[3], negated_end[3] = ends3[:, 0:E], ends3[:, E : 2 * E]
         turn(0, bank[6])
         turn(1, bank[7])
         project_passes((4, 5), (0,))
@@ -346,21 +362,22 @@ def tile_list_cloth_edge_strain_kernel(
             for a in (1, 2):
                 project_passes((c,), (a,))
         project_passes((6,), range(K_PASSES))
-        gather_ends(3)
+        gather_first_end(3)
+        gather_negated_end(3)
 
         z_rows = held([P, BLOCKS, DUOS], F32, "z_rows", reuse="raw2_2")
         square_early(0, bank[6])
         square_early(1, bank[7])
         drain(4)
-        turn(2, bank[6])
-        turn(3, bank[7])
+        turn(2, bank[7])
+        turn(3, bank[6])
         project_passes((7,), range(K_PASSES))
         drain(5)
         drain(6)
-        square_early(2, bank[6])
-        square_early(3, bank[7])
+        square_early(2, bank[7])
+        square_early(3, bank[6])
         drain(7)
-        d_late = held([P, PACK, E], F32, "d_late", reuse="ends2")
+        d_late = held([P, PACK, E], F32, "d_late", reuse="rounded1_0")
         second_of_4 = held([P, E], F32, "second_of_4")
         gather_second(second_of_4[:], PACK, 0, BLOCKS)
         gather_difference(second_of_4[:], PACK, 0, BLOCKS)

@@ -87,7 +87,7 @@ def tile_list_cloth_edge_strain_kernel(
         h = {c: held([P, S], F32, "h%d" % c) if c >= WIDE else wide[c] for c in range(TILES)}
         first_end = {c: wide[2][:, S + c * E : S + (c + 1) * E] for c in (0, 1)}
         first_end[2] = held([P, E], F32, "first_end2")[:]
-        negated_end = {1: held([P, E], F32, "negated_end1")[:]}
+        negated_end = {2: held([P, E], F32, "negated_end2")[:]}
         early_codes = held([P, E], U32, "early_codes")
         z_codes = {(0, b): early_codes[:, b * P : (b + 1) * P] for b in range(BLOCKS)}
         z_plane = [held([P, E], U8, "z_plane%d" % g) for g in range(R_PASSES)]
@@ -193,14 +193,14 @@ def tile_list_cloth_edge_strain_kernel(
                 stop=stop,
             )
 
-        def project_passes(tiles, passes):
+        def project_passes(tiles, passes, closing=last_pass):
             for c in tiles:
                 for half in range(2):
                     for a in passes:
                         cut = (BANK, CUT, S) if half == 1 and a == last_pass else (half * BANK, (half + 1) * BANK)
                         for s0, s1 in zip(cut, cut[1:]):
                             dst = h_bank(c, half)[:, s0 - half * BANK : s1 - half * BANK]
-                            project(c, dst, s0, s1, a, a == last_pass and s1 == cut[-1])
+                            project(c, dst, s0, s1, a, a == closing and s1 == cut[-1])
 
         def drain(c):
             nc.scalar.copy(h[c][:, 0:BANK], h_bank(c, 0)[:])
@@ -333,37 +333,35 @@ def tile_list_cloth_edge_strain_kernel(
         negated_end[0] = held([P, E], F32, "negated_end0", reuse="raw1_2")[:]
         gather_negated_end(0)
         project_passes((2, 3), (1, 2))
-        gather_first_end(1)
-        gather_negated_end(1)
-
         rounded[DEALT, 0] = held([P, PACK * PASS], BF16, "rounded2_0", reuse="rounded1_0")
         round_dealt_on_gpsimd(0, 2, PACK)
         round_dealt(0, 0, 2, nc.scalar.copy)
         drain(2)
-        rounded[DEALT, 1] = held([P, PACK * PASS], BF16, "rounded2_1")
-        round_dealt_on_gpsimd(1, 2, PACK)
-        round_dealt(1, 0, 2, nc.scalar.copy)
+        gather_first_end(1)
         quantize_w1(DEALT, 0)
+        negated_end[1] = held([P, E], F32, "negated_end1", reuse="raw2_0")[:]
+        gather_negated_end(1)
+        rounded[DEALT, 1] = held([P, PACK * PASS], BF16, "rounded2_1", reuse="rounded1_0")
+        rounded[DEALT, 2] = held([P, PACK * PASS], BF16, "rounded2_2")
+        for a in (1, 2):
+            round_dealt_on_gpsimd(a, 2, PACK)
+        round_dealt(1, 0, 2, nc.scalar.copy)
         drain(3)
-        rounded[DEALT, 2] = held([P, PACK * PASS], BF16, "rounded2_2", reuse="rounded1_0")
-        round_dealt_on_gpsimd(2, 2, PACK)
         round_dealt(2, 0, 2, nc.scalar.copy)
         gather_first_end(2)
-        quantize_w1(DEALT, 1)
-        negated_end[2] = held([P, E], F32, "negated_end2", reuse="raw2_1")[:]
         gather_negated_end(2)
+        quantize_w1(DEALT, 1)
         quantize_w1(DEALT, 2)
-        ends3 = held([P, 2 * E], F32, "ends3", reuse="rounded1_0")
+        ends3 = held([P, 2 * E], F32, "ends3", reuse="rounded2_2")
         first_end[3], negated_end[3] = ends3[:, 0:E], ends3[:, E : 2 * E]
-        turn(0, bank[6])
-        turn(1, bank[7])
-        project_passes((4, 5), (0,))
-        for c in (4, 5):
-            for a in (1, 2):
-                project_passes((c,), (a,))
-        project_passes((6,), range(K_PASSES))
         gather_first_end(3)
         gather_negated_end(3)
+        turn(0, bank[6])
+        turn(1, bank[7])
+        project_passes((4, 5, 6), (0,))
+        project_passes((4,), (1, 2))
+        for c in (5, 6):
+            project_passes((c,), (2, 1), closing=1)
 
         z_rows = held([P, BLOCKS, DUOS], F32, "z_rows", reuse="raw2_2")
         square_early(0, bank[6])
@@ -377,7 +375,7 @@ def tile_list_cloth_edge_strain_kernel(
         square_early(2, bank[7])
         square_early(3, bank[6])
         drain(7)
-        d_late = held([P, PACK, E], F32, "d_late", reuse="rounded1_0")
+        d_late = held([P, PACK, E], F32, "d_late", reuse="rounded2_2")
         second_of_4 = held([P, E], F32, "second_of_4")
         gather_second(second_of_4[:], PACK, 0, BLOCKS)
         gather_difference(second_of_4[:], PACK, 0, BLOCKS)

@@ -48,10 +48,14 @@ def tile_list_cloth_edge_strain_kernel(
     nc = tc.nc
     with ExitStack() as ctx:
         keep = ctx.enter_context(tc.tile_pool(name="keep", bufs=1))
+        shared = ctx.enter_context(tc.tile_pool(name="shared", bufs=1))
         psum = ctx.enter_context(tc.psum_pool(name="psum", bufs=1))
 
         def held(shape, dtype, name, reuse=None):
             return keep.tile(shape, dtype, name=name, tag=reuse or name, align_bytes=64)
+
+        def placed(shape, dtype, name, offset):
+            return shared.tile(shape, dtype, name=name, offset=offset, align_bytes=64)
 
         offs_sb = keep.tile([P, S // LANES], U16, name="offs_sb")
         pos1_sb = keep.tile([P, E // LANES], U16, name="pos1_sb")
@@ -71,13 +75,16 @@ def tile_list_cloth_edge_strain_kernel(
                 if (j, a) in lodged:
                     c, half = lodged[j, a]
                     raw[j, a] = wide[c][:, half * S : (half + 1) * S].rearrange("p (i c) -> p i c", i=PACK)
+                elif (j, a) == (DEALT, last_pass):
+                    raw[j, a] = placed([P, PACK, c1 - c0], F32, "raw2_2", 0)
                 else:
                     raw[j, a] = held([P, PACK, c1 - c0], F32, "raw%d_%d" % (j, a))
                 if a == 0 or j != JOINT:
                     if j != DEALT:
                         rounded[j, a] = held([P, PACK * (c1 - c0)], BF16, "rounded%d_%d" % (j, a))
                     w1_codes[j, a] = held([P, c1 - c0], U32, "w1_codes%d_%d" % (j, a))
-                    w1_plane[j, a] = held([P, c1 - c0], U8, "w1_plane%d_%d" % (j, a))
+                    if (j, a) != (DEALT, 1):
+                        w1_plane[j, a] = held([P, c1 - c0], U8, "w1_plane%d_%d" % (j, a))
         width = PARTS[JOINT][1] - PARTS[JOINT][0]
         joint_codes = held([P, 2 * width], U32, "joint_codes")
         joint_plane = held([P, 2 * width], U8, "joint_plane")
@@ -120,7 +127,7 @@ def tile_list_cloth_edge_strain_kernel(
         nc.sync.dma_start(offs_sb[:], offs)
         load_w1(0, 0)
         for q in range(QUADS):
-            nc.sync.dma_start(
+            (nc.sync, nc.scalar)[q % 2].dma_start(
                 out=tab_plane[32 * q : 32 * q + 4 * K_PASSES, :],
                 in_=tab_scales[:, 4 * q : 4 * q + 4, :].bitcast(I32),
             )
@@ -317,7 +324,7 @@ def tile_list_cloth_edge_strain_kernel(
 
         round_w1(1, 0, nc.scalar.copy)
         quantize_w1(1, 0)
-        for (src, s0, s1), copy in zip(pieces, (nc.scalar.copy, nc.scalar.copy, nc.vector.tensor_copy)):
+        for (src, s0, s1), copy in zip(pieces, (nc.scalar.copy, nc.vector.tensor_copy, nc.scalar.copy)):
             copy(h[0][:, s0:s1], src[:, 0 : s1 - s0])
         project_passes((2, 3), (0,))
         joint_rounded = held([P, 2 * PACK * width], BF16, "joint_rounded", reuse="rounded1_0")
@@ -350,9 +357,10 @@ def tile_list_cloth_edge_strain_kernel(
         round_dealt(2, 0, 2, nc.scalar.copy)
         gather_first_end(2)
         gather_negated_end(2)
+        w1_plane[DEALT, 1] = placed([P, PASS], U8, "w1_plane2_1", 0)
         quantize_w1(DEALT, 1)
         quantize_w1(DEALT, 2)
-        ends3 = held([P, 2 * E], F32, "ends3", reuse="rounded2_2")
+        ends3 = held([P, 2 * E], F32, "ends3", reuse="rounded1_0")
         first_end[3], negated_end[3] = ends3[:, 0:E], ends3[:, E : 2 * E]
         gather_first_end(3)
         gather_negated_end(3)
@@ -363,7 +371,7 @@ def tile_list_cloth_edge_strain_kernel(
         for c in (5, 6):
             project_passes((c,), (2, 1), closing=1)
 
-        z_rows = held([P, BLOCKS, DUOS], F32, "z_rows", reuse="raw2_2")
+        z_rows = placed([P, BLOCKS, DUOS], F32, "z_rows", 4096)
         square_early(0, bank[6])
         square_early(1, bank[7])
         drain(4)
@@ -375,7 +383,7 @@ def tile_list_cloth_edge_strain_kernel(
         square_early(2, bank[7])
         square_early(3, bank[6])
         drain(7)
-        d_late = held([P, PACK, E], F32, "d_late", reuse="rounded2_2")
+        d_late = held([P, PACK, E], F32, "d_late", reuse="rounded1_0")
         second_of_4 = held([P, E], F32, "second_of_4")
         gather_second(second_of_4[:], PACK, 0, BLOCKS)
         gather_difference(second_of_4[:], PACK, 0, BLOCKS)
@@ -390,7 +398,7 @@ def tile_list_cloth_edge_strain_kernel(
             for b0, b1 in cuts:
                 gather_second(second[:, b0 * P : b1 * P], c, b0, b1)
             if c == late_tiles[-1]:
-                z_01 = held([P, 2 * PASS], BF16, "z_01", reuse="raw2_2")
+                z_01 = placed([P, 2 * PASS], BF16, "z_01", 4096)
                 square_late(z_01, 0, 2, 0, PACK - 1)
             for b0, b1 in cuts:
                 gather_difference(second[:, b0 * P : b1 * P], c, b0, b1)
@@ -407,7 +415,7 @@ def tile_list_cloth_edge_strain_kernel(
         mix(1, 0)
         mix(1, 1, first=1)
         mix(0, 1, first=1)
-        last_seconds = held([P, BY_BLOCKS, P], F32, "last_seconds", reuse="raw2_2")
+        last_seconds = placed([P, BY_BLOCKS, P], F32, "last_seconds", 4096)
         for i, c in enumerate(late_tiles):
             gather_second(last_seconds[:, i, :], c, LAST, BLOCKS)
         quantize_late(z_2, 2, LAST)

@@ -127,7 +127,7 @@ def tile_list_cloth_edge_strain_kernel(
         nc.sync.dma_start(offs_sb[:], offs)
         load_w1(0, 0)
         for q in range(QUADS):
-            (nc.sync, nc.scalar)[q % 2].dma_start(
+            nc.sync.dma_start(
                 out=tab_plane[32 * q : 32 * q + 4 * K_PASSES, :],
                 in_=tab_scales[:, 4 * q : 4 * q + 4, :].bitcast(I32),
             )
@@ -429,7 +429,8 @@ def tile_list_cloth_edge_strain_kernel(
         log_and_store(0, 0, OUT_TILES)
         magnitude(2)
         log_and_store(1, 0, OUT_TILES)
-        log_and_store(2, 0, OUT_TILES)
+        log_and_store(2, 0, OUT_TILES // 2)
+        log_and_store(2, OUT_TILES // 2, OUT_TILES)
 
         z_3 = held([P, PASS], BF16, "z_3")
         d_3 = d_late[:, :, LAST * P : E].rearrange("p t (c n) -> p c t n", n=LINE)
@@ -441,7 +442,9 @@ def tile_list_cloth_edge_strain_kernel(
         negated = held([P, OUT_TILES, P], F32, "negated")
         for y, (n0, n1) in zip(y_3, halves):
             nc.vector.tensor_scalar(negated[:, n0:n1, :], y, -1.0, None, ALU.mult)
-        for y, (n0, n1) in zip(y_3, halves):
-            nc.vector.tensor_tensor(size[LAST][:, n0:n1, :], y, negated[:, n0:n1, :], ALU.max)
-        for n0, n1 in halves:
-            log_and_store(LAST, n0, n1)
+        nc.vector.tensor_tensor(size[LAST][:, 0:2, :], y_3[0], negated[:, 0:2, :], ALU.max)
+        for n in range(*halves[1]):
+            nc.vector.tensor_tensor(size[LAST][:, n, :], y_3[1][:, n - 2, :], negated[:, n, :], ALU.max)
+        log_and_store(LAST, *halves[0])
+        for n in range(*halves[1]):
+            log_and_store(LAST, n, n + 1)

@@ -97,6 +97,7 @@ def tile_list_cloth_edge_strain_kernel(
         negated_end = {2: held([P, E], F32, "negated_end2")[:]}
         early_codes = held([P, E], U32, "early_codes")
         z_codes = {(0, b): early_codes[:, b * P : (b + 1) * P] for b in range(BLOCKS)}
+        wide_codes = {0: early_codes}
         z_plane = [held([P, E], U8, "z_plane%d" % g) for g in range(R_PASSES)]
         size = [held([P, OUT_TILES, P], F32, "size%d" % b) for b in range(BLOCKS)]
         result = [held([P, OUT_TILES, P], F32, "result%d" % b) for b in range(BLOCKS)]
@@ -269,6 +270,7 @@ def tile_list_cloth_edge_strain_kernel(
 
         def quantize_late(z, b0, b1):
             codes = held([P, (b1 - b0) * P], U32, "late_codes%d" % b0)
+            wide_codes[b0] = codes
             for b in range(b0, b1):
                 z_codes[1, b] = codes[:, (b - b0) * P : (b - b0 + 1) * P]
             nc.vector.quantize_mx(out=codes[:].bitcast(FP8X4), scales=z_plane[1][:, b0 * P : b1 * P], in_=z[:])
@@ -290,6 +292,25 @@ def tile_list_cloth_edge_strain_kernel(
                     start=(g == first and n == n_first),
                     stop=(g != first and n == n_last),
                 )
+
+        def mix_wide(g, i, first=0):
+            for n in (2 * i, 2 * i + 1):
+                nc.tensor.matmul_mx(
+                    out=y_banks[i][:, n % 2 * 2 * P : (n % 2 + 1) * 2 * P],
+                    lhsT=w2_codes[:, g, :].bitcast(U8)[:, 2 * n * P : 2 * (n + 1) * P].bitcast(FP4X4),
+                    lhsT_scale=w2_plane[:, g, :].bitcast(U8)[:, n * P : (n + 1) * P],
+                    rhs=(early_codes[:, 0 : 2 * P], wide_codes[0][:])[g].bitcast(FP8X4),
+                    rhs_scale=z_plane[g][:, 0 : 2 * P],
+                    start=(g == first and n % 2 == 0),
+                    stop=(g != first and n % 2 == 1),
+                )
+
+        def log_and_store_wide(i):
+            nc.scalar.activation(result[i][:], size[i][:], ACT.Ln, bias=1.0)
+            nc.sync.dma_start(
+                out=out[2 * i * P : 2 * (i + 1) * P, 0 : 2 * P].rearrange("(n p) e -> p n e", p=P),
+                in_=result[i][:].rearrange("p n e -> p (n e)").rearrange("p (n e) -> p n e", n=2),
+            )
 
         def magnitude(b):
             y = y_banks[b][:].rearrange("p (n e) -> p n e", e=P)
@@ -408,13 +429,13 @@ def tile_list_cloth_edge_strain_kernel(
             scales=z_plane[0][:],
             in_=z_cols[:].rearrange("p e u -> p (e u)").bitcast(BF16),
         )
-        mix(0, 0)
+        mix_wide(0, 0)
         z_2 = held([P, PASS], BF16, "z_2", reuse="z_cols")
         square_late(z_2, 2, LAST, 0, PACK)
         quantize_late(z_01, 0, 2)
-        mix(1, 0)
-        mix(1, 1, first=1)
-        mix(0, 1, first=1)
+        mix_wide(1, 0)
+        mix_wide(1, 1, first=1)
+        mix_wide(0, 1, first=1)
         last_seconds = placed([P, BY_BLOCKS, P], F32, "last_seconds", 4096)
         for i, c in enumerate(late_tiles):
             gather_second(last_seconds[:, i, :], c, LAST, BLOCKS)
@@ -426,9 +447,9 @@ def tile_list_cloth_edge_strain_kernel(
         magnitude(0)
         magnitude(1)
         mix(0, LAST)
-        log_and_store(0, 0, OUT_TILES)
+        log_and_store_wide(0)
         magnitude(2)
-        log_and_store(1, 0, OUT_TILES)
+        log_and_store_wide(1)
         log_and_store(2, 0, OUT_TILES // 2)
         log_and_store(2, OUT_TILES // 2, OUT_TILES)
 

@@ -26,7 +26,7 @@ QUADS = 4
 BANK = 512
 CUT = 768
 BANKS = 8
-H_SETS = 3
+H_SET = (0, 1, 2, 0, 1, 2, 0, 3)
 LANES = 16
 RUN = 4
 LINE = 2
@@ -186,7 +186,7 @@ def tile_list_cloth_edge_strain_kernel(
             )
 
         def h_bank(c, half):
-            return bank[2 * (c % H_SETS) + half]
+            return bank[2 * H_SET[c] + half]
 
         def project(c, dst, s0, s1, a, stop):
             j = min(c // 2, DEALT)
@@ -263,7 +263,7 @@ def tile_list_cloth_edge_strain_kernel(
 
         def square_late(z, b0, b1, t0, t1):
             nc.scalar.activation(
-                z[:].rearrange("p (c n t) -> p c t n", n=LINE, t=PACK)[:, :, t0:t1],
+                z.rearrange("p (c n t) -> p c t n", n=LINE, t=PACK)[:, :, t0:t1],
                 d_late[:, t0:t1, b0 * P : b1 * P].rearrange("p t (c n) -> p c t n", n=LINE),
                 ACT.Square,
             )
@@ -396,34 +396,32 @@ def tile_list_cloth_edge_strain_kernel(
         square_early(0, bank[6])
         square_early(1, bank[7])
         drain(4)
-        turn(2, bank[7])
-        turn(3, bank[6])
         project_passes((7,), range(K_PASSES))
+        turn(2, bank[2])
+        turn(3, bank[3])
         drain(5)
         drain(6)
-        square_early(2, bank[7])
-        square_early(3, bank[6])
         drain(7)
-        d_late = held([P, PACK, E], F32, "d_late", reuse="rounded1_0")
-        second_of_4 = held([P, E], F32, "second_of_4")
-        gather_second(second_of_4[:], PACK, 0, BLOCKS)
-        gather_difference(second_of_4[:], PACK, 0, BLOCKS)
+        square_early(2, bank[2])
+        square_early(3, bank[3])
         z_cols = held([P, E, 2], F32, "z_cols")
         turn_back(0, 2, bank[4])
         turn_back(2, BLOCKS, bank[5])
 
+        d_late = held([P, PACK, E], F32, "d_late", reuse="w1_codes2_2")
         late_tiles = range(TILES - BY_BLOCKS, TILES)
-        for c in late_tiles:
-            second = held([P, LAST * P], F32, "second_of_%d" % c)
-            cuts = ((0, LAST),) if c == late_tiles[0] else ((0, 2), (2, LAST))
-            for b0, b1 in cuts:
-                gather_second(second[:, b0 * P : b1 * P], c, b0, b1)
-            if c == late_tiles[-1]:
-                z_01 = placed([P, 2 * PASS], BF16, "z_01", 4096)
-                square_late(z_01, 0, 2, 0, PACK - 1)
-            for b0, b1 in cuts:
-                gather_difference(second[:, b0 * P : b1 * P], c, b0, b1)
-        square_late(z_01, 0, 2, PACK - 1, PACK)
+        second = {c: held([P, E if c == PACK else LAST * P], F32, "second_of_%d" % c) for c in range(PACK, TILES)}
+        for c in range(PACK, TILES - 1):
+            gather_second(second[c][:], c, 0, BLOCKS if c == PACK else LAST)
+        for c in range(PACK, TILES - 1):
+            gather_difference(second[c][:], c, 0, BLOCKS if c == PACK else LAST)
+        for b0, b1 in ((0, 2), (2, LAST)):
+            gather_second(second[7][:, b0 * P : b1 * P], 7, b0, b1)
+        z_01 = placed([P, 2 * PASS], BF16, "z_01", 4096)
+        for b in range(LAST):
+            gather_difference(second[7][:, b * P : (b + 1) * P], 7, b, b + 1)
+            if b < 2:
+                square_late(z_01[:, b * PASS : (b + 1) * PASS], b, b + 1, 0, PACK)
         nc.vector.quantize_mx(
             out=early_codes[:].bitcast(FP8X4),
             scales=z_plane[0][:],
@@ -431,12 +429,12 @@ def tile_list_cloth_edge_strain_kernel(
         )
         mix_wide(0, 0)
         z_2 = held([P, PASS], BF16, "z_2", reuse="z_cols")
-        square_late(z_2, 2, LAST, 0, PACK)
+        square_late(z_2[:], 2, LAST, 0, PACK)
         quantize_late(z_01, 0, 2)
         mix_wide(1, 0)
         mix_wide(1, 1, first=1)
         mix_wide(0, 1, first=1)
-        last_seconds = placed([P, BY_BLOCKS, P], F32, "last_seconds", 4096)
+        last_seconds = d_late[:, :, P : 2 * P]
         for i, c in enumerate(late_tiles):
             gather_second(last_seconds[:, i, :], c, LAST, BLOCKS)
         quantize_late(z_2, 2, LAST)

@@ -40,6 +40,7 @@ DEALT = 2
 WIDE = 3
 BY_BLOCKS = 3
 LAST = BLOCKS - 1
+HALF = P // 2
 
 
 def tile_list_cloth_edge_strain_kernel(
@@ -440,8 +441,13 @@ def tile_list_cloth_edge_strain_kernel(
         quantize_late(z_2, 2, LAST)
         mix(1, 2, first=1)
         mix(0, 2, first=1)
-        for i, c in enumerate(late_tiles):
+        for i, c in enumerate(late_tiles[:-1]):
             gather_difference(last_seconds[:, i, :], c, LAST, BLOCKS)
+        for e0 in (0, HALF):
+            at = LAST * P + e0
+            window = h[TILES - 1][:].indirect(pos1_sb[:, entries(at, at + HALF)])
+            second_end = last_seconds[:, BY_BLOCKS - 1, e0 : e0 + HALF]
+            nc.vector.tensor_tensor(d_late[:, PACK - 1, at : at + HALF], window, second_end, ALU.subtract)
         magnitude(0)
         magnitude(1)
         mix(0, LAST)
@@ -452,9 +458,17 @@ def tile_list_cloth_edge_strain_kernel(
         log_and_store(2, OUT_TILES // 2, OUT_TILES)
 
         z_3 = held([P, PASS], BF16, "z_3")
-        d_3 = d_late[:, :, LAST * P : E].rearrange("p t (c n) -> p c t n", n=LINE)
-        nc.vector.tensor_tensor(z_3[:].rearrange("p (c n t) -> p c t n", n=LINE, t=PACK), d_3, d_3, ALU.mult)
-        quantize_late(z_3, LAST, BLOCKS)
+        z_codes[1, LAST] = held([P, P], U32, "late_codes3")[:]
+        for e0 in (0, HALF):
+            d_3 = d_late[:, :, LAST * P + e0 : LAST * P + e0 + HALF].rearrange("p t (c n) -> p c t n", n=LINE)
+            squares = z_3[:, PACK * e0 : PACK * (e0 + HALF)].rearrange("p (c n t) -> p c t n", n=LINE, t=PACK)
+            nc.vector.tensor_tensor(squares, d_3, d_3, ALU.mult)
+        for e0 in (0, HALF):
+            nc.vector.quantize_mx(
+                out=z_codes[1, LAST][:, e0 : e0 + HALF].bitcast(FP8X4),
+                scales=z_plane[1][:, LAST * P + e0 : LAST * P + e0 + HALF],
+                in_=z_3[:, PACK * e0 : PACK * (e0 + HALF)],
+            )
         mix(1, LAST)
         halves = ((0, OUT_TILES // 2), (OUT_TILES // 2, OUT_TILES))
         y_3 = [y_group(LAST, n0)[0][:].rearrange("p (n e) -> p n e", e=P)[:, n0:n1, :] for n0, n1 in halves]

from contextlib import ExitStack

import concourse.mybir as mybir
from concourse.masks import make_identity

K, T, S, E, H, N = 1536, 2048, 1024, 512, 1024, 512
FLOPS = 2 * K * H * S + 2 * H * N * E

F32 = mybir.dt.float32
BF16 = mybir.dt.bfloat16
I32 = mybir.dt.int32
U32 = mybir.dt.uint32
U16 = mybir.dt.uint16
U8 = mybir.dt.uint8
FP8X4 = mybir.dt.float8_e4m3fn_x4
FP4X4 = mybir.dt.float4_e2m1fn_x4
ACT = mybir.ActivationFunctionType
ALU = mybir.AluOpType

P = 128
PACK = 4
PASS = P * PACK
K_PASSES = K // PASS
R_PASSES = H // PASS
QUADS = 4
BANK = 512
CUT = 768
BANKS = 8
H_SET = (0, 1, 2, 0, 1, 2, 0, 3)
LANES = 16
RUN = 4
LINE = 2
TILES = H // P
BLOCKS = E // P
OUT_TILES = N // P
DUOS = PASS // 2
PARTS = ((0, 2 * P), (2 * P, PASS), (PASS, H))
JOINT = 1
DEALT = 2
WIDE = 3
BY_BLOCKS = 3
LAST = BLOCKS - 1
HALF = P // 2


def tile_list_cloth_edge_strain_kernel(
    tc, tab_words, tab_scales, offs, pos1, pos2, w1, w2_words, w2_scales, out
):
    nc = tc.nc
    with ExitStack() as ctx:
        keep = ctx.enter_context(tc.tile_pool(name="keep", bufs=1))
        shared = ctx.enter_context(tc.tile_pool(name="shared", bufs=1))
        psum = ctx.enter_context(tc.psum_pool(name="psum", bufs=1))

        def held(shape, dtype, name, reuse=None):
            return keep.tile(shape, dtype, name=name, tag=reuse or name, align_bytes=64)

        def placed(shape, dtype, name, offset):
            return shared.tile(shape, dtype, name=name, offset=offset, align_bytes=64)

        offs_sb = keep.tile([P, S // LANES], U16, name="offs_sb")
        pos1_sb = keep.tile([P, E // LANES], U16, name="pos1_sb")
        pos2_sb = keep.tile([P, E // LANES], U16, name="pos2_sb")
        tab_plane = held([P, T // 4], I32, "tab_plane")
        w2_plane = held([P, R_PASSES, N // 4], I32, "w2_plane")
        w2_codes = held([P, R_PASSES, N // 2], I32, "w2_codes")
        table = [held([P, T], I32, "table%d" % a) for a in range(K_PASSES)]
        last_pass = K_PASSES - 1
        v_codes = [held([P, CUT if a == last_pass else S], U32, "v_codes%d" % a) for a in range(K_PASSES)]
        v_plane = held([P, S], U8, "v_plane")
        wide = [held([P, 2 * S], F32, "wide%d" % c) for c in range(WIDE)]
        lodged = {(0, 0): (0, 1), (0, 1): (1, 1), (1, 0): (0, 0), (1, 1): (1, 0)}
        raw, rounded, w1_codes, w1_plane = {}, {}, {}, {}
        for j, (c0, c1) in enumerate(PARTS):
            for a in range(K_PASSES):
                if (j, a) in lodged:
                    c, half = lodged[j, a]
                    raw[j, a] = wide[c][:, half * S : (half + 1) * S].rearrange("p (i c) -> p i c", i=PACK)
                elif (j, a) == (DEALT, last_pass):
                    raw[j, a] = placed([P, PACK, c1 - c0], F32, "raw2_2", 0)
                else:
                    raw[j, a] = held([P, PACK, c1 - c0], F32, "raw%d_%d" % (j, a))
                if a == 0 or j != JOINT:
                    if j != DEALT:
                        rounded[j, a] = held([P, PACK * (c1 - c0)], BF16, "rounded%d_%d" % (j, a))
                    w1_codes[j, a] = held([P, c1 - c0], U32, "w1_codes%d_%d" % (j, a))
                    if (j, a) != (DEALT, 1):
                        w1_plane[j, a] = held([P, c1 - c0], U8, "w1_plane%d_%d" % (j, a))
        width = PARTS[JOINT][1] - PARTS[JOINT][0]
        joint_codes = held([P, 2 * width], U32, "joint_codes")
        joint_plane = held([P, 2 * width], U8, "joint_plane")
        for a in (1, 2):
            w1_codes[JOINT, a] = joint_codes[:, (a - 1) * width : a * width]
            w1_plane[JOINT, a] = joint_plane[:, (a - 1) * width : a * width]
        h = {c: held([P, S], F32, "h%d" % c) if c >= WIDE else wide[c] for c in range(TILES)}
        first_end = {c: wide[2][:, S + c * E : S + (c + 1) * E] for c in (0, 1)}
        first_end[2] = held([P, E], F32, "first_end2")[:]
        negated_end = {2: held([P, E], F32, "negated_end2")[:]}
        early_codes = held([P, E], U32, "early_codes")
        z_codes = {(0, b): early_codes[:, b * P : (b + 1) * P] for b in range(BLOCKS)}
        wide_codes = {0: early_codes}
        z_plane = [held([P, E], U8, "z_plane%d" % g) for g in range(R_PASSES)]
        size = [held([P, OUT_TILES, P], F32, "size%d" % b) for b in range(BLOCKS)]
        result = [held([P, OUT_TILES, P], F32, "result%d" % b) for b in range(BLOCKS)]
        identity = held([P, P], F32, "identity")
        bank = [psum.tile([P, BANK], F32, name="bank%d" % i) for i in range(BANKS)]
        y_banks = [bank[i] for i in (6, 7, 2, 6, 7)]

        nc.gpsimd.memset(tab_plane[:], 0)
        one = held([P, 1], F32, "one")
        zero = held([P, 1], F32, "zero")
        nc.vector.memset(one[:], 1.0)
        nc.scalar.activation(zero[:], one[:], ACT.Ln)
        nc.vector.memset(w2_plane[:], 0)
        minus_one = held([P, E], F32, "minus_one")
        nc.vector.memset(minus_one[:], -1.0)
        make_identity(nc, identity[:])

        def load_table(a):
            words = tab_words[a].rearrange("p t i -> p (t i)").bitcast(I32)
            nc.sync.dma_start(out=table[a][:], in_=words)

        def load_w1(j, a):
            c0, c1 = PARTS[j]
            rows = w1[a * PASS : (a + 1) * PASS, c0:c1]
            nc.sync.dma_start(out=raw[j, a][:], in_=rows.rearrange("(p i) c -> p i c", i=PACK))

        load_table(0)
        nc.sync.dma_start(offs_sb[:], offs)
        load_w1(0, 0)
        for q in range(QUADS):
            nc.sync.dma_start(
                out=tab_plane[32 * q : 32 * q + 4 * K_PASSES, :],
                in_=tab_scales[:, 4 * q : 4 * q + 4, :].bitcast(I32),
            )
        for a in range(1, K_PASSES):
            load_table(a)
            load_w1(0, a)
        nc.sync.dma_start(pos1_sb[:], pos1)
        nc.sync.dma_start(pos2_sb[:], pos2)
        for j in range(1, len(PARTS)):
            for a in range(K_PASSES):
                load_w1(j, a)
        nc.sync.dma_start(out=w2_codes[:], in_=w2_words.bitcast(I32).rearrange("a p c -> p a c"))
        for q in range(QUADS):
            nc.sync.dma_start(
                out=w2_plane[32 * q : 32 * q + 4, :, :],
                in_=w2_scales[:, 4 * q : 4 * q + 4, :].bitcast(I32).rearrange("a r c -> r a c"),
            )

        def entries(e0, e1):
            return slice(e0 // LANES, e1 // LANES)

        def words(a, s0, s1):
            if a == last_pass and s0 >= CUT:
                return v_rest[:, s0 - CUT : s1 - CUT]
            return v_codes[a][:, s0:s1]

        def gather_words(a, s0, s1):
            window = table[a][:].bitcast(U32)
            nc.vector.tensor_copy(words(a, s0, s1), window.indirect(offs_sb[:, entries(s0, s1)]))

        def round_w1(j, a, copy):
            copy(
                rounded[j, a][:].rearrange("p (c n u i) -> p c u n i", n=RUN, u=2, i=2),
                raw[j, a][:].rearrange("p (u i) (c n) -> p c u n i", n=RUN, i=2),
            )

        def round_on_gpsimd(dst, src):
            nc.gpsimd.tensor_scalar(dst, src, 1.0, 0.0, ALU.mult, ALU.add)

        def round_dealt_on_gpsimd(a, t0, t1):
            round_on_gpsimd(
                rounded[DEALT, a][:].rearrange("p (t m i) -> p m t i", t=PACK, i=PACK)[:, :, t0:t1],
                raw[DEALT, a][:].rearrange("p i (m t) -> p m t i", t=PACK)[:, :, t0:t1],
            )

        def round_dealt(a, t0, t1, copy):
            copy(
                rounded[DEALT, a][:].rearrange("p (t m u i) -> p m u t i", t=PACK, u=2, i=2)[:, :, :, t0:t1],
                raw[DEALT, a][:].rearrange("p (u i) (m t) -> p m u t i", t=PACK, i=2)[:, :, :, t0:t1],
            )

        def quantize_w1(j, a):
            nc.vector.quantize_mx(
                out=w1_codes[j, a][:].bitcast(FP8X4), scales=w1_plane[j, a][:], in_=rounded[j, a][:]
            )

        def h_bank(c, half):
            return bank[2 * H_SET[c] + half]

        def project(c, dst, s0, s1, a, stop):
            j = min(c // 2, DEALT)
            rows = slice((c - 2 * j) * P, (c - 2 * j + 1) * P)
            nc.tensor.matmul_mx(
                out=dst,
                lhsT=w1_codes[j, a][:, rows].bitcast(FP8X4),
                lhsT_scale=w1_plane[j, a][:, rows],
                rhs=words(a, s0, s1).bitcast(FP8X4),
                rhs_scale=v_plane[4 * a : P, s0:s1],
                start=(a == 0),
                stop=stop,
            )

        def project_passes(tiles, passes, closing=last_pass):
            for c in tiles:
                for half in range(2):
                    for a in passes:
                        cut = (BANK, CUT, S) if half == 1 and a == last_pass else (half * BANK, (half + 1) * BANK)
                        for s0, s1 in zip(cut, cut[1:]):
                            dst = h_bank(c, half)[:, s0 - half * BANK : s1 - half * BANK]
                            project(c, dst, s0, s1, a, a == closing and s1 == cut[-1])

        def drain(c):
            nc.scalar.copy(h[c][:, 0:BANK], h_bank(c, 0)[:])
            nc.scalar.copy(h[c][:, BANK:S], h_bank(c, 1)[:])

        def gather_first_end(c):
            nc.vector.tensor_copy(first_end[c], h[c][:].indirect(pos1_sb[:]))

        def gather_negated_end(c):
            window = h[c][:].indirect(pos2_sb[:])
            if c < WIDE:
                nc.vector.tensor_scalar(negated_end[c], window, -1.0, 0.0, ALU.mult, ALU.add)
            else:
                nc.vector.tensor_tensor(negated_end[c], window, minus_one[:], ALU.mult)

        def turn(c, dst):
            for b in range(BLOCKS):
                for i in range(2):
                    nc.tensor.matmul(
                        dst[:, b * P : (b + 1) * P],
                        lhsT=(first_end, negated_end)[i][c][:, b * P : (b + 1) * P],
                        rhs=identity[:],
                        start=(i == 0),
                        stop=(i == 1),
                        is_transpose=True,
                    )

        def square_early(c, src):
            flat = z_rows[:].rearrange("p b w -> p (b w)").bitcast(BF16)
            nc.scalar.activation(
                flat.rearrange("p (b u c q j) -> p c u b q j", b=BLOCKS, u=2, c=PACK, j=2)[:, c],
                src[:].rearrange("p (b q u j) -> p u b q j", b=BLOCKS, u=2, j=2),
                ACT.Square,
            )

        def turn_back(b0, b1, dst):
            for b in range(b0, b1):
                for u in range(2):
                    at = (2 * (b - b0) + u) * P
                    nc.tensor.transpose(dst[:, at : at + P], z_rows[:, b, u * P : (u + 1) * P], identity[:])
            nc.scalar.copy(
                z_cols[:, b0 * P : b1 * P, :].rearrange("p (b e) u -> p b e u", e=P),
                dst[:, 0 : 2 * (b1 - b0) * P].rearrange("p (b u e) -> p b e u", u=2, e=P),
            )

        def gather_second(dst, c, b0, b1):
            nc.vector.tensor_copy(dst, h[c][:].indirect(pos2_sb[:, entries(b0 * P, b1 * P)]))

        def gather_difference(second, c, b0, b1):
            window = h[c][:].indirect(pos1_sb[:, entries(b0 * P, b1 * P)])
            nc.vector.tensor_tensor(d_late[:, c - PACK, b0 * P : b1 * P], window, second, ALU.subtract)

        def square_late(z, b0, b1, t0, t1):
            nc.scalar.activation(
                z.rearrange("p (c n t) -> p c t n", n=LINE, t=PACK)[:, :, t0:t1],
                d_late[:, t0:t1, b0 * P : b1 * P].rearrange("p t (c n) -> p c t n", n=LINE),
                ACT.Square,
            )

        def quantize_late(z, b0, b1):
            codes = held([P, (b1 - b0) * P], U32, "late_codes%d" % b0)
            wide_codes[b0] = codes
            for b in range(b0, b1):
                z_codes[1, b] = codes[:, (b - b0) * P : (b - b0 + 1) * P]
            nc.vector.quantize_mx(out=codes[:].bitcast(FP8X4), scales=z_plane[1][:, b0 * P : b1 * P], in_=z[:])

        def y_group(b, n):
            if b < LAST:
                return y_banks[b], 0, OUT_TILES - 1
            return y_banks[b + n // 2], n - n % 2, n - n % 2 + 1

        def mix(g, b, first=0):
            for n in range(OUT_TILES):
                dst, n_first, n_last = y_group(b, n)
                nc.tensor.matmul_mx(
                    out=dst[:, n * P : (n + 1) * P],
                    lhsT=w2_codes[:, g, :].bitcast(U8)[:, 2 * n * P : 2 * (n + 1) * P].bitcast(FP4X4),
                    lhsT_scale=w2_plane[:, g, :].bitcast(U8)[:, n * P : (n + 1) * P],
                    rhs=z_codes[g, b].bitcast(FP8X4),
                    rhs_scale=z_plane[g][:, b * P : (b + 1) * P],
                    start=(g == first and n == n_first),
                    stop=(g != first and n == n_last),
                )

        def mix_wide(g, i, first=0):
            for n in (2 * i, 2 * i + 1):
                nc.tensor.matmul_mx(
                    out=y_banks[i][:, n % 2 * 2 * P : (n % 2 + 1) * 2 * P],
                    lhsT=w2_codes[:, g, :].bitcast(U8)[:, 2 * n * P : 2 * (n + 1) * P].bitcast(FP4X4),
                    lhsT_scale=w2_plane[:, g, :].bitcast(U8)[:, n * P : (n + 1) * P],
                    rhs=(early_codes[:, 0 : 2 * P], wide_codes[0][:])[g].bitcast(FP8X4),
                    rhs_scale=z_plane[g][:, 0 : 2 * P],
                    start=(g == first and n % 2 == 0),
                    stop=(g != first and n % 2 == 1),
                )

        def log_and_store_wide(i):
            nc.scalar.activation(result[i][:], size[i][:], ACT.Ln, bias=1.0)
            nc.sync.dma_start(
                out=out[2 * i * P : 2 * (i + 1) * P, 0 : 2 * P].rearrange("(n p) e -> p n e", p=P),
                in_=result[i][:].rearrange("p n e -> p (n e)").rearrange("p (n e) -> p n e", n=2),
            )

        def magnitude(b):
            y = y_banks[b][:].rearrange("p (n e) -> p n e", e=P)
            nc.scalar.activation(size[b][:], y, ACT.Abs, bias=zero[:])

        def log_and_store(b, n0, n1):
            nc.scalar.activation(result[b][:, n0:n1, :], size[b][:, n0:n1, :], ACT.Ln, bias=1.0)
            nc.sync.dma_start(
                out=out[n0 * P : n1 * P, b * P : (b + 1) * P].rearrange("(n p) e -> p n e", p=P),
                in_=result[b][:, n0:n1, :],
            )

        gather_words(0, 0, S)
        nc.vector.tensor_copy(v_plane[:], tab_plane[:].bitcast(U8).indirect(offs_sb[:]))
        for a in range(K_PASSES):
            round_w1(0, a, nc.scalar.copy)
        pieces = ((bank[0], 0, BANK), (bank[1], BANK, CUT), (bank[6], CUT, S))
        quantize_w1(0, 0)
        gather_words(1, 0, S)
        quantize_w1(0, 1)
        for a in range(last_pass):
            for dst, s0, s1 in pieces:
                project(0, dst[:, 0 : s1 - s0], s0, s1, a, False)
            project_passes((1,), (a,))
        gather_words(last_pass, 0, CUT)
        quantize_w1(0, last_pass)
        v_rest = held([P, S - CUT], U32, "v_rest", reuse="raw0_2")
        gather_words(last_pass, CUT, S)
        for dst, s0, s1 in pieces:
            project(0, dst[:, 0 : s1 - s0], s0, s1, last_pass, True)
        project_passes((1,), (last_pass,))

        round_w1(1, 0, nc.scalar.copy)
        quantize_w1(1, 0)
        for (src, s0, s1), copy in zip(pieces, (nc.scalar.copy, nc.vector.tensor_copy, nc.scalar.copy)):
            copy(h[0][:, s0:s1], src[:, 0 : s1 - s0])
        project_passes((2, 3), (0,))
        joint_rounded = held([P, 2 * PACK * width], BF16, "joint_rounded", reuse="rounded1_0")
        for a in (1, 2):
            rounded[JOINT, a] = joint_rounded[:, (a - 1) * PACK * width : a * PACK * width]
        round_on_gpsimd(
            rounded[JOINT, 1].rearrange("p (c i) -> p c i", i=PACK), raw[JOINT, 1][:].rearrange("p i c -> p c i")
        )
        round_w1(1, 2, nc.scalar.copy)
        drain(1)
        gather_first_end(0)
        nc.vector.quantize_mx(out=joint_codes[:].bitcast(FP8X4), scales=joint_plane[:], in_=joint_rounded[:])
        negated_end[0] = held([P, E], F32, "negated_end0", reuse="raw1_2")[:]
        gather_negated_end(0)
        project_passes((2, 3), (1, 2))
        rounded[DEALT, 0] = held([P, PACK * PASS], BF16, "rounded2_0", reuse="rounded1_0")
        round_dealt_on_gpsimd(0, 2, PACK)
        round_dealt(0, 0, 2, nc.scalar.copy)
        drain(2)
        gather_first_end(1)
        quantize_w1(DEALT, 0)
        negated_end[1] = held([P, E], F32, "negated_end1", reuse="raw2_0")[:]
        gather_negated_end(1)
        rounded[DEALT, 1] = held([P, PACK * PASS], BF16, "rounded2_1", reuse="rounded1_0")
        rounded[DEALT, 2] = held([P, PACK * PASS], BF16, "rounded2_2")
        for a in (1, 2):
            round_dealt_on_gpsimd(a, 2, PACK)
        round_dealt(1, 0, 2, nc.scalar.copy)
        drain(3)
        round_dealt(2, 0, 2, nc.scalar.copy)
        gather_first_end(2)
        gather_negated_end(2)
        w1_plane[DEALT, 1] = placed([P, PASS], U8, "w1_plane2_1", 0)
        quantize_w1(DEALT, 1)
        quantize_w1(DEALT, 2)
        ends3 = held([P, 2 * E], F32, "ends3", reuse="rounded1_0")
        first_end[3], negated_end[3] = ends3[:, 0:E], ends3[:, E : 2 * E]
        gather_first_end(3)
        gather_negated_end(3)
        turn(0, bank[6])
        turn(1, bank[7])
        project_passes((4, 5, 6), (0,))
        project_passes((4,), (1, 2))
        for c in (5, 6):
            project_passes((c,), (2, 1), closing=1)

        z_rows = placed([P, BLOCKS, DUOS], F32, "z_rows", 4096)
        square_early(0, bank[6])
        square_early(1, bank[7])
        drain(4)
        project_passes((7,), range(K_PASSES))
        turn(2, bank[2])
        turn(3, bank[3])
        drain(5)
        drain(6)
        drain(7)
        square_early(2, bank[2])
        square_early(3, bank[3])
        z_cols = held([P, E, 2], F32, "z_cols")
        turn_back(0, 2, bank[4])
        turn_back(2, BLOCKS, bank[5])

        d_late = held([P, PACK, E], F32, "d_late", reuse="w1_codes2_2")
        late_tiles = range(TILES - BY_BLOCKS, TILES)
        second = {c: held([P, E if c == PACK else LAST * P], F32, "second_of_%d" % c) for c in range(PACK, TILES)}
        for c in range(PACK, TILES - 1):
            gather_second(second[c][:], c, 0, BLOCKS if c == PACK else LAST)
        for c in range(PACK, TILES - 1):
            gather_difference(second[c][:], c, 0, BLOCKS if c == PACK else LAST)
        for b0, b1 in ((0, 2), (2, LAST)):
            gather_second(second[7][:, b0 * P : b1 * P], 7, b0, b1)
        z_01 = placed([P, 2 * PASS], BF16, "z_01", 4096)
        for b in range(LAST):
            gather_difference(second[7][:, b * P : (b + 1) * P], 7, b, b + 1)
            if b < 2:
                square_late(z_01[:, b * PASS : (b + 1) * PASS], b, b + 1, 0, PACK)
        nc.vector.quantize_mx(
            out=early_codes[:].bitcast(FP8X4),
            scales=z_plane[0][:],
            in_=z_cols[:].rearrange("p e u -> p (e u)").bitcast(BF16),
        )
        mix_wide(0, 0)
        z_2 = held([P, PASS], BF16, "z_2", reuse="z_cols")
        square_late(z_2[:], 2, LAST, 0, PACK)
        quantize_late(z_01, 0, 2)
        mix_wide(1, 0)
        mix_wide(1, 1, first=1)
        mix_wide(0, 1, first=1)
        last_seconds = d_late[:, :, P : 2 * P]
        for i, c in enumerate(late_tiles):
            gather_second(last_seconds[:, i, :], c, LAST, BLOCKS)
        quantize_late(z_2, 2, LAST)
        mix(1, 2, first=1)
        mix(0, 2, first=1)
        for i, c in enumerate(late_tiles[:-1]):
            gather_difference(last_seconds[:, i, :], c, LAST, BLOCKS)
        for e0 in (0, HALF):
            at = LAST * P + e0
            window = h[TILES - 1][:].indirect(pos1_sb[:, entries(at, at + HALF)])
            second_end = last_seconds[:, BY_BLOCKS - 1, e0 : e0 + HALF]
            nc.vector.tensor_tensor(d_late[:, PACK - 1, at : at + HALF], window, second_end, ALU.subtract)
        magnitude(0)
        magnitude(1)
        mix(0, LAST)
        log_and_store_wide(0)
        magnitude(2)
        log_and_store_wide(1)
        log_and_store(2, 0, OUT_TILES // 2)
        log_and_store(2, OUT_TILES // 2, OUT_TILES)

        z_3 = held([P, PASS], BF16, "z_3")
        z_codes[1, LAST] = held([P, P], U32, "late_codes3")[:]
        for e0 in (0, HALF):
            d_3 = d_late[:, :, LAST * P + e0 : LAST * P + e0 + HALF].rearrange("p t (c n) -> p c t n", n=LINE)
            squares = z_3[:, PACK * e0 : PACK * (e0 + HALF)].rearrange("p (c n t) -> p c t n", n=LINE, t=PACK)
            nc.vector.tensor_tensor(squares, d_3, d_3, ALU.mult)
        for e0 in (0, HALF):
            nc.vector.quantize_mx(
                out=z_codes[1, LAST][:, e0 : e0 + HALF].bitcast(FP8X4),
                scales=z_plane[1][:, LAST * P + e0 : LAST * P + e0 + HALF],
                in_=z_3[:, PACK * e0 : PACK * (e0 + HALF)],
            )
        mix(1, LAST)
        halves = ((0, OUT_TILES // 2), (OUT_TILES // 2, OUT_TILES))
        y_3 = [y_group(LAST, n0)[0][:].rearrange("p (n e) -> p n e", e=P)[:, n0:n1, :] for n0, n1 in halves]
        negated = held([P, OUT_TILES, P], F32, "negated")
        for y, (n0, n1) in zip(y_3, halves):
            nc.vector.tensor_scalar(negated[:, n0:n1, :], y, -1.0, None, ALU.mult)
        nc.vector.tensor_tensor(size[LAST][:, 0:2, :], y_3[0], negated[:, 0:2, :], ALU.max)
        for n in range(*halves[1]):
            nc.vector.tensor_tensor(size[LAST][:, n, :], y_3[1][:, n - 2, :], negated[:, n, :], ALU.max)
        log_and_store(LAST, *halves[0])
        for n in range(*halves[1]):
            log_and_store(LAST, n, n + 1)
